import numpy as np, ml_dtypes
CORES = [2,3,42,43,82,83,122,123]
N = 8
import mx_ref
BF = ml_dtypes.bfloat16
def cols(t, e):
    v = np.concatenate([t.reshape(128, -1, 4), np.zeros((128, 1, 4), BF)], axis=1)
    return np.ascontiguousarray(v[:, e]).reshape(128, -1)
def cut(t, i, w=512):
    return t[:, w * i:w * i + w]
def pick(q, e):
    c = np.concatenate([q[0].reshape(128, -1, 4), np.zeros((128, 1, 4), np.uint8)], axis=1); s = np.concatenate([q[1], np.ones((16, 1), np.uint8)], axis=1)
    return (np.ascontiguousarray(c[:, e].reshape(128, -1)), np.ascontiguousarray(s[:, e]))
def join(*qs):
    return (np.concatenate([q[0] for q in qs], axis=1), np.concatenate([q[1] for q in qs], axis=1))
def put(q, e, v):
    c, s = q[0].reshape(128, -1, 4).copy(), q[1].copy(); c[:, e] = v[0].reshape(128, -1, 4); s[:, e] = v[1]
    return (c.reshape(128, -1), s)
def pk(c, s):
    return (np.ascontiguousarray(c), mx_ref.live(s))
def emit(q):
    return q[0], q[1]
def decode(q):
    o = []
    for b in range(4):
        e = np.zeros((128, 128, 4), np.float32); e[np.arange(128), np.arange(128), b] = 1
        o.append(mx_ref.matmul(mx_ref.quantize(e.reshape(128, 512).astype(BF)), q))
    return np.stack(o, axis=2).reshape(128, -1)
def f(rng, *shape):
    return mx_ref.flush((rng.standard_normal(shape, dtype=np.float32) * np.exp2(rng.integers(-2, 3, shape[:-1] + (1,)))).astype(BF))
def wide(rng, *shape, cols=0):
    v = rng.standard_normal(shape, dtype=np.float32) * np.exp2(rng.integers(-12, 13, shape)).astype(np.float32)
    if cols: v *= np.repeat(np.exp2(rng.integers(-cols, cols + 1, shape[:-2] + (1, shape[-1] // 4))) * (rng.random(shape[:-2] + (1, shape[-1] // 4)) > 0.0625), 4, axis=-1).astype(np.float32)
    return mx_ref.flush(v.astype(BF))
P, K, R, O = 256, 32, 2, 1
def big(v):
    v = v.astype(np.float32)
    v[np.abs(v) < np.float32(2.0 ** -16)] = 0
    return v.astype(BF)
def times(t, k):
    return mx_ref.flush((t.astype(np.float32) * np.float32(k)).astype(BF))
def signs(d, v, s):
    g = np.where(d["u"][0, :, :4].astype(np.float32) < 0, -1, 1)
    a = np.abs(v.astype(np.float32)).reshape(N, 128, -1, 4) * g[None, :, None, :] * s[:, None, :, None]
    return big(a.reshape(N, 128, -1))
def counted(rng, d):
    n = P // 2 + rng.permutation(K)[:N]
    return signs(d, d["tb"], np.stack([np.where(rng.permutation(P) < n[r], 1, -1) for r in range(N)]))
def setup_inputs(rng):
    v = np.zeros((128, 512), np.float32)
    v[:, :4] = f(rng, 128, 4).astype(np.float32)
    return {"tb": big(f(rng, N, 128, 4 * P)), "nz": big(f(rng, N, 128, 4 * R * K)), "u": np.stack([v.astype(BF)] * N), "w": f(rng, N, 128, 512 * O)}
def setup_inputs_down(rng):
    d = setup_inputs(rng)
    d["tb"] = counted(rng, d)
    d["nz"] = signs(d, 64 * (1 + rng.random((N, 128, 4 * R * K))), np.full((N, R * K), -1))
    return d
def setup_inputs_spread(rng):
    d = setup_inputs(rng)
    t, r = big(wide(rng, N, 128, 4 * P, cols=6)), int(rng.integers(0, N))
    x = (1 + rng.random((N, 128, 4 * P))) * np.exp2(rng.integers(12, 18, (N, 128, 4 * P)) + np.repeat(rng.integers(0, 4, (N, 1, P)), 4, axis=2))
    t[r] = signs(d, x, np.ones((N, P), np.int64))[r]
    return {**d, "tb": t, "nz": big(wide(rng, N, 128, 4 * R * K, cols=6)), "u": times(d["u"], 2.0 ** 24)}
def setup_inputs_swap(rng):
    d = setup_inputs(rng)
    d["tb"] = counted(rng, d)
    d["nz"] = signs(d, 64 * (1 + rng.random((N, 128, 4 * R * K))), np.full((N, R * K), 1))
    return d
def setup_inputs_ties(rng):
    d = setup_inputs(rng)
    a = rng.permutation(N) <= N // 2
    d["tb"] = np.stack([cols(d["tb"][int(a[r])], rng.permutation(P) % (P // (K + 1))) for r in range(N)])
    d["nz"] = np.stack([d["nz"][0]] * N)
    return d
def setup_inputs_zero(rng):
    d = setup_inputs(rng)
    d["u"] = times(np.abs(d["u"].astype(np.float32)), 2.0 ** -26)
    d["tb"], d["nz"] = big(times(d["tb"], 2.0 ** -10)), big(times(d["nz"], 2.0 ** -10))
    s, a = np.zeros((N, P), np.int64), rng.permutation(N)
    for i in range(N - 1):
        m, n, e = P // 2 - 4 * i, K // 2 - i, rng.permutation(P)
        s[a[i], e[:m]] = 1
        s[a[i], e[m:m + n]] = -1
    d["tb"] = signs(d, d["tb"], s)
    for r in range(N):
        d["tb"][r].reshape(128, P, 4)[:, np.flatnonzero(s[r] == 0)[1::2]] = BF(-0.0)
    d["nz"] = big(d["nz"].astype(np.float32) * np.repeat(rng.random((N, 1, R * K)) > 0.25, 4, axis=2))
    return d
def check_inputs(d):
    b = []
    for k, low, high in (("tb", -16, 26), ("nz", -16, 26), ("u", -30, 30), ("w", -30, 30)):
        v = np.abs(d[k].astype(np.float32))
        if not (np.isfinite(v).all() and ((v == 0) | (v >= 2.0 ** low) & (v <= 2.0 ** high)).all()): b.append("a value of " + k)
    v = d["u"].astype(np.float32)
    if (v[:, :, 4:] != 0).any(): b.append("u has numbers behind its column 0")
    if (v != v[:1]).any(): b.append("u isn't the same on all ranks")
    return b
def reference(tb, nz, u, w):
    T = [mx_ref.quantize(tb[r]) for r in range(N)]
    qu = [mx_ref.quantize(u[r]) for r in range(N)]
    od = np.zeros((N, R, N), np.float32)
    for t in range(R):
        s = [mx_ref.matmul(qu[r], T[r])[0] + np.float32(0) for r in range(N)]
        fitness = np.array([np.count_nonzero(s[r] > 0) for r in range(N)])
        place = np.argsort(-fitness, kind="stable")
        od[:, t] = place
        new = T[:]
        for i in range(N // 2):
            a, b = place[i], place[N - 1 - i]
            j = np.argsort(s[a], kind="stable")[:K]
            noise = mx_ref.quantize(np.ascontiguousarray(nz[b][:, 4 * t * K:4 * (t + 1) * K]))
            v = np.float32(0.5) * decode(pick(T[a], j)) + np.float32(0.5) * decode(noise)
            new[b] = put(T[a], j, mx_ref.quantize(np.ascontiguousarray(v.astype(BF))))
        T = new
    oc, osc, y = np.zeros((N, 128, 4 * P), np.uint8), np.zeros((N, 16, P), np.uint8), np.zeros((N, 128, O * P), np.float32)
    for r in range(N):
        oc[r], osc[r] = emit(T[r])
        for o in range(O):
            y[r, :, o * P:(o + 1) * P] = mx_ref.matmul(mx_ref.quantize(np.ascontiguousarray(cut(w[r], o))), T[r])
    return {"oc": oc, "osc": osc, "od": od, "y": y}

@@ -1,0 +1,595 @@
+from concourse.bass import DstId, RemoteDMATransfer
+from concourse.mybir import dt, AluOpType, AxisListType, ActivationFunctionType
+
+A = AluOpType
+F = ActivationFunctionType
+CODE, PLANE, F32, BF, I32, U16 = "float8_e4m3fn_x4", "uint8", "float32", "bfloat16", "int32", "uint16"
+SCRATCH, PART = {}, {}
+
+
+def _bufs():
+    def b(dtype, **kw):
+        for k in kw:
+            SCRATCH[k] = ("sbuf", [128, kw[k]], dtype)
+
+    def parts(name, dtype, **kw):
+        n = 0
+        for k in kw:
+            PART[k] = (name, n)
+            n += kw[k]
+        SCRATCH[name] = ("sbuf", [128, n], dtype)
+
+    def q(**kw):
+        for k in kw:
+            SCRATCH[k] = ("sbuf", [128, kw[k]], CODE)
+            SCRATCH[k + "s"] = ("sbuf", [128, kw[k]], PLANE)
+    b(BF, tbx=1024, nzx=768, wx=512, ux=512, u4=8, eb=2048, ct=1536, oh=512, vt=512, vt2=512, hb=128, idn=128,
+      cmp=768, gt=256, c1=256)
+    parts("bconst", BF, m16=256, r16=256, r8=64, r32=256, io64=64, i32r=128)
+    parts("fconst", F32, zf=128, dg=8, f0=128)
+    parts("fown", F32, ft=8, sm=256, pos=8, jm=64, js=64, junk=384)
+    parts("flist", F32, qf=8, c16=16, wr=8, w256=8,
+          tie=64, ri=64, i7=64, j8=64, wc=8, x32=8, colf=8, ones=64, m64=64, p256=64,
+          k1=64, cm=64, sc=64, ms=8, st=8, go=8, a0=64, b0=64, hit=64, hf=64, hfs=64, hh=64, hhs=64, tks=8, thr8=8,
+          thr=256, tmp=8, base1=8, wh8=8, wh=64, cola=8, o0=8, w0=8, sw=512, jr=512, oda=64, odb=64, odc=64,
+          s1=256, fit1=8, k1b=64, cmb=64, scb=64, ab=64, bb=64, miss=64, bs=64, o1=8, st0=8, t32=8, csj=128, dgo=128,
+          ds=128, lt=128, eq=128, jl=128, eqj=128, cnt=128, tp=64, cr=64, lm=128, lmo=128, sel=64, dif=64, mul=64,
+          off=64, jwm=64, jws=64, frow=256, fm=256, fs=256)
+    b(F32, nb=8, jt=1024, jt2=512, od0=8, od1=8, yo=256)
+    parts("iconst", I32, pi=8, rm=256, dm=256, qi=8, m16i=256, r16i=256, r8i=64, r32i=256, i32i=128, ji=64, c2i=16)
+    parts("iarr", I32, vi=8, fiti=8, nbi=8)
+    b(U16, vl=64)
+    parts("lists", U16, jl4=4, lrs=4, lq7=4, grs=4, gr=4, gis=4, l256=16, ofa=2, ofx=2, of=16, ofc=4, ofj=4, l1=2,
+          jw=4, fl=16)
+    q(uq=128, tq=256, nq=192, wq=128, eh=512, cq=384, oq=128, sp=64, land=256, cd=128, xw=192, xs=32, cw=512,
+      sl=256, sb=256, cc=64, cd2=128, fw=448, oq2=256, hq=256)
+    SCRATCH["dv"] = ("psum", [128, 2048], F32)
+    SCRATCH["pp"] = ("psum", [128, 2048], F32)
+
+
+_bufs()
+SEMAPHORES = ["cv", "cs", "ct_", "cg", "lo", "a_v", "a_c", "a_s", "b_c", "b_s", "c_c", "c_s", "s_c", "s_s", "h_c",
+              "h_s"] + ["d%d" % i for i in range(40)]
+
+
+def find_helpers(T, topo):
+    out = []
+    for c in T.cores:
+        for k in topo.cores_of(c):
+            if k in T.cores or k in out or topo.die(k) == topo.die(c):
+                continue
+            if all(topo.may_write(k, x) for x in T.cores):
+                out.append(k)
+                break
+    return out
+
+
+def bits(engines):
+    return sum(1 << e for e in engines)
+
+
+def ways(core, T, topo, me):
+    far = [r for r in range(len(T.cores)) if r != me and topo.chip(T.cores[r]) != topo.chip(core)]
+    near = [r for r in range(len(T.cores)) if r != me and topo.chip(T.cores[r]) == topo.chip(core)]
+    out = topo.engines(core, T.cores[far[0]])
+    inn = [e for e in topo.engines(core, T.cores[near[0]]) if e not in out]
+    return far, near, out, inn
+
+
+def dest(T, topo, r):
+    rid, pid, _ = topo.addr(T.cores[r])
+    return DstId(rid=rid, pnc=pid)
+
+
+def scatter_call(g, core, T, topo, me, src, dst, sem):
+    far, near, out, inn = ways(core, T, topo, me)
+    tr = [RemoteDMATransfer(dst_ids=[dest(T, topo, r)], dma_engine_mask=1 << out[i], remote_sem=sem,
+                            src=src(r), dst=dst) for i, r in enumerate(far)]
+    tr += [RemoteDMATransfer(dst_ids=[dest(T, topo, r)], dma_engine_mask=bits(inn), remote_sem=sem,
+                             src=src(r), dst=dst) for r in near]
+    g.remote_dma_fused(tr, local_sem=T.sem.lo)
+    return len(far) + len(inn) * len(near)
+
+
+def gather_call(g, core, T, topo, me, src, dst, sem):
+    far, near, out, inn = ways(core, T, topo, me)
+    g.remote_dma_fused([
+        RemoteDMATransfer(dst_ids=[dest(T, topo, r) for r in far], dma_engine_mask=bits(out), remote_sem=sem,
+                          srcs=[src], dsts=[dst] * len(far)),
+        RemoteDMATransfer(dst_ids=[dest(T, topo, r) for r in near], dma_engine_mask=bits(inn), remote_sem=sem,
+                          srcs=[src], dsts=[dst] * len(near))], local_sem=T.sem.lo)
+    return len(out) + len(inn)
+
+
+def hand_on(g, core, T, topo, r):
+    S = 32
+    c0 = S * (len(T.cores) - 1 - r)
+    g.wait_ge(T.sem.h_c, 16)
+    n = scatter_call(g, core, T, topo, r, lambda s: T.hq[:, S * s:S * s + S].bitcast(dt.uint8),
+                     T.sl[:, c0:c0 + S].bitcast(dt.uint8), T.sem.s_c)
+    g.wait_ge(T.sem.h_s, 16)
+    n += scatter_call(g, core, T, topo, r, lambda s: T.hqs[:, S * s:S * s + S], T.sls[:, c0:c0 + S], T.sem.s_s)
+    g.wait_ge(T.sem.lo, n)
+
+
+def builder(g, T):
+    queue = {"v": g.vector, "s": g.scalar, "t": g.tensor, "g": g, "y": g.sync}
+    sem = {"v": "cv", "s": "cs", "t": "ct_", "g": "cg"}
+    count = {"v": 0, "s": 0, "t": 0, "g": 0}
+    seen, log, dmas = {}, {}, [0]
+
+    def ap(n, a, b, st=1, p=None, bc=None, off=None):
+        n, k = PART.get(n, (n, 0))
+        a, b, t = a + k, b + k, T[n]
+        rows = slice(None) if p is None else slice(p[0], p[1])
+        v = t[rows, a:b] if st == 1 else t[rows, a:b:st]
+        if bc is not None:
+            v = v.bitcast(bc)
+        if off is not None:
+            v = v.indirect(off["v"])
+        return {"v": v, "n": n, "a": a, "b": b, "st": st, "off": off}
+
+    def apart(x, y):
+        if x["n"] in ("dv", "pp"):
+            return x["a"] // 512 != y["a"] // 512
+        if x["a"] >= y["b"] or y["a"] >= x["b"]:
+            return True
+        return x["st"] == y["st"] and x["st"] > 1 and (x["a"] - y["a"]) % x["st"] != 0
+
+    def wait(q, tok):
+        if seen.get((q, tok[0]), 0) < tok[1]:
+            queue[q].wait_ge(T.sem[tok[0]], tok[1])
+            seen[(q, tok[0])] = tok[1]
+
+    def need(q, outs, ins):
+        toks = {}
+        for w, xs in ((True, outs), (False, ins)):
+            for x in xs:
+                for (y, yw, yq, tok) in log.get(x["n"], []):
+                    if apart(x, y):
+                        continue
+                    psum = x["n"] in ("dv", "pp")
+                    if yw or (w and yq != q) or (psum and yq != q):
+                        if yq == q == "t" and yw and w:
+                            continue
+                        toks[tok[0]] = max(toks.get(tok[0], 0), tok[1])
+        for k in toks:
+            wait(q, (k, toks[k]))
+
+    def note(q, outs, ins, tok):
+        for w, xs in ((True, outs), (False, ins)):
+            for x in xs:
+                log.setdefault(x["n"], []).append((x, w, q, tok))
+
+    def full(xs):
+        return [x for x in xs if x] + [x["off"] for x in xs if x and x["off"]]
+
+    def run(q, fn, outs, ins):
+        ins = full(ins) + [x["off"] for x in outs if x["off"]]
+        need(q, outs, ins)
+        count[q] += 1
+        fn(queue[q]).then_inc(T.sem[sem[q]], 1)
+        note(q, outs, ins, (sem[q], count[q]))
+
+    def dma(q, out, in_, outs, ins):
+        need(q, outs, ins)
+        s = "d%d" % dmas[0]
+        dmas[0] += 1
+        queue[q].dma_start(out, in_).then_inc(T.sem[s], 16)
+        note("dma", outs, ins, (s, 16))
+
+    def arrive(n, a, b, tok):
+        x = {"n": n, "a": a, "b": b, "st": 1, "off": None}
+        log.setdefault(n, []).append((x, True, "far", tok))
+
+    def ready(q, ins):
+        need(q, [], full(ins))
+
+    def finish():
+        for q in count:
+            wait("y", (sem[q], count[q]))
+        for k in range(dmas[0]):
+            wait("y", ("d%d" % k, 16))
+    return ap, run, dma, arrive, ready, finish
+
+
+def rank_program(g, core, T, topo):
+    me = T.rank_of(core)
+    helpers = find_helpers(T, topo)
+    if me is None:
+        if core in helpers:
+            hand_on(g, core, T, topo, helpers.index(core))
+        return
+    ap, run, dma, arrive, ready, finish = builder(g, T)
+    u8, u32 = dt.uint8, dt.uint32
+    slot = 7 - me
+    sent = [0]
+
+    def sca(x):
+        return x["v"] if isinstance(x, dict) else x
+
+    def dic(*xs):
+        return [x for x in xs if isinstance(x, dict)]
+
+    def ts(out, in0, s1, op0, s2=None, op1=None):
+        if op1 is None:
+            run("v", lambda q: q.tensor_scalar(out["v"], in0["v"], sca(s1), None, op0), [out], dic(in0, s1))
+        else:
+            run("v", lambda q: q.tensor_scalar(out["v"], in0["v"], sca(s1), sca(s2), op0, op1), [out],
+                dic(in0, s1, s2))
+
+    def tt(out, in0, in1, op):
+        run("v", lambda q: q.tensor_tensor(out["v"], in0["v"], in1["v"], op), [out], [in0, in1])
+
+    def scan(out, d0, d1, op0=A.mult, op1=A.add):
+        run("v", lambda q: q.tensor_tensor_scan(out["v"], d0["v"], d1["v"], 0.0, op0, op1), [out], [d0, d1])
+
+    def cp(out, in_):
+        run("v", lambda q: q.tensor_copy(out["v"], in_["v"]), [out], [in_])
+
+    def fill(out, c):
+        run("v", lambda q: q.memset(out["v"], c), [out], [])
+
+    def red(out, in_):
+        run("v", lambda q: q.tensor_reduce(out["v"], in_["v"], AxisListType.X, A.add), [out], [in_])
+
+    def act(out, in_, func=F.Copy, bias=None, accum=None):
+        if bias is not None:
+            run("s", lambda q: q.activation(out["v"], in_["v"], F.Identity, bias=bias["v"]), [out], [in_, bias])
+        elif accum is not None:
+            run("s", lambda q: q.activation(out["v"], in_["v"], func, accum_out=accum["v"]), [out, accum], [in_])
+        else:
+            run("s", lambda q: q.activation(out["v"], in_["v"], func), [out], [in_])
+
+    def quant(n, a, b, tile, x0=0):
+        o, p, x = ap(n, a, b), ap(n + "s", a, b), ap(tile, x0, x0 + 4 * (b - a))
+        run("v", lambda q: q.quantize_mx(o["v"], p["v"], x["v"]), [o, p], [x])
+
+    def mm(out, l, la, r, ra, rb, start=True, stop=True):
+        xs = [ap(l, la, la + 128), ap(l + "s", la, la + 128), ap(r, ra, rb), ap(r + "s", ra, rb)]
+        run("t", lambda q: q.matmul_mx(out["v"], xs[0]["v"], xs[1]["v"], xs[2]["v"], xs[3]["v"], start, stop),
+            [out], xs)
+
+    def pick(dn, c, d, sn, a, b, on, e, f):
+        off = ap(on, e, f)
+        cp(ap(dn, c, d, bc=u32), ap(sn, a, b, bc=u32, off=off))
+        act(ap(dn + "s", c, d), ap(sn + "s", a, b, off=off))
+
+    def move(dn, c, sn, a, n):
+        o, i = ap(dn, c, c + n, bc=u8), ap(sn, a, a + n, bc=u8)
+        dma("y", o["v"], i["v"], [o], [i])
+        o, i = ap(dn + "s", c, c + n), ap(sn + "s", a, a + n)
+        dma("y", o["v"], i["v"], [o], [i])
+
+    def load(q, n, a, b, src):
+        o = ap(n, a, b)
+        dma(q, o["v"], src, [o], [])
+
+    def to_all(src, dst, sem):
+        ready("g", [src])
+        sent[0] += gather_call(g, core, T, topo, me, src["v"], dst["v"], T.sem[sem])
+
+    def c(n, k=0):
+        return ap(n, k, k + 1)
+
+    load("s", "u4", 0, 4, T.u[:, 0:4])
+    load("y", "tbx", 0, 1024, T.tb[:, 0:1024])
+    load("y", "nzx", 0, 256, T.nz[:, 0:256])
+    load("y", "wx", 0, 512, T.w[:, 0:512])
+
+    def iota(n, k, pat, base, cm):
+        o = ap(n, 0, k)
+        run("g", lambda q: q.iota(o["v"], pat, base, cm), [o], [])
+
+    def asel(n, i, op, fl):
+        o, x = ap(n, 0, 128), ap(i, 0, 128)
+        run("g", lambda q: q.affine_select(o["v"], x["v"], [[-1, 128]], op, fl, 0, 1), [o], [x])
+
+    iota("pi", 1, [[0, 1]], 0, 1)
+    fill(ap("zf", 0, 128), 0.0)
+    fill(ap("hb", 0, 128), 0.5)
+    asel("f0", "zf", A.is_gt, 1e29)
+    asel("idn", "hb", A.is_equal, 0.0)
+    iota("rm", 256, [[1, 256]], 0, 0)
+    iota("dm", 256, [[1, 256]], 128, -1)
+    for t in range(4):
+        act(ap("ux", t, 512, 4), ap("zf", 0, 128), bias=c("u4", t))
+    ts(c("qi", 0), c("pi"), 15, A.bitwise_and)
+    ts(c("qi", 1), c("pi"), 4, A.logical_shift_right)
+    ts(c("dg", 0), c("qi", 1), 16.0, A.mult)
+    ts(c("dg", 1), c("qi", 1), 16.0, A.mult, 128.0, A.add)
+    cp(c("dg", 2), c("qi", 0))
+    cp(c("dg", 3), c("qi", 1))
+    ts(c("dg", 4), c("qi", 1), 8.0, A.add)
+    fill(ap("oh", 0, 512), 0.0)
+    fill(ap("ct", 0, 1024), 0.0)
+    quant("uq", 0, 128, "ux")
+    for k, t, col in ((0, 0, 0), (0, 1, 1), (1, 0, 2), (1, 1, 2), (2, 0, 3), (2, 1, 4), (2, 2, 2), (2, 3, 2)):
+        act(ap("ct", 512 * k + t, 512 * k + 512, 4), ap("zf", 0, 128), bias=c("dg", col))
+    cp(ap("io64", 0, 64), ap("rm", 0, 64))
+    ts(ap("m16i", 0, 64), ap("dm", 0, 64), 15, A.bitwise_and)
+    ts(ap("m16", 0, 64), ap("m16i", 0, 64), 0.0, A.is_equal)
+    ts(ap("r16i", 0, 64), ap("rm", 0, 64), 15, A.bitwise_and)
+    ts(ap("r16", 0, 64), ap("r16i", 0, 64), 0.0, A.not_equal)
+
+    quant("tq", 0, 256, "tbx")
+    P0, P1, P2, P3 = 0, 512, 1024, 1536
+    mm(ap("pp", P0, P0 + 256), "uq", 0, "tq", 0, 256)
+    mm(ap("pp", P1, P1 + 128), "tq", 0, "uq", 0, 128)
+    mm(ap("pp", P2, P2 + 128), "tq", 128, "uq", 0, 128)
+    h = helpers[me]
+    rid, pid, _ = topo.addr(h)
+
+    def to_helper(n, o, sem):
+        ready("g", [n])
+        g.remote_dma(o["v"], n["v"], T.sem[sem], T.sem.lo, pid, rid, topo.mask(core, h))
+        sent[0] += len(topo.engines(core, h))
+    to_helper(ap("tq", 0, 256, bc=u8), ap("hq", 0, 256, bc=u8), "h_c")
+    quant("cq", 0, 384, "ct")
+    s0, s1 = c("pp", P1), c("pp", P2)
+    ts(ap("cmp", 0, 256), ap("pp", P0, P0 + 256), s0, A.is_lt)
+    ts(ap("sm", 0, 128), ap("f0", 0, 128), s0, A.add)
+    tt(ap("cmp", 256, 384), ap("pp", P0, P0 + 128), ap("sm", 0, 128), A.is_equal)
+    act(ap("junk", 0, 384), ap("cmp", 0, 384), accum=c("pos", 0))
+    ts(ap("cmp", 384, 512), ap("pp", P0, P0 + 128), s1, A.is_le)
+    ts(ap("cmp", 512, 640), ap("pp", P0 + 128, P0 + 256), s1, A.is_lt)
+    ts(ap("sm", 128, 256), ap("f0", 0, 128), s1, A.add)
+    tt(ap("cmp", 640, 768), ap("pp", P0 + 128, P0 + 256), ap("sm", 128, 256), A.is_equal)
+    red(c("pos", 4), ap("cmp", 384, 768))
+    for hh, k in ((0, 0), (1, 4)):
+        ts(ap("oh", hh, 256, 4), ap("io64", 0, 64), c("pos", k), A.is_equal)
+        ts(ap("oh", 258 + hh, 512, 4), ap("io64", 0, 64), c("pos", k), A.is_equal)
+    quant("oq", 0, 128, "oh")
+    mm(ap("pp", P3, P3 + 128), "cq", 0, "oq", 0, 128, True, False)
+    mm(ap("pp", P3, P3 + 128), "cq", 128, "oq", 0, 128, False, True)
+    mm(ap("pp", P1, P1 + 128), "oq", 0, "cq", 256, 384)
+    ts(ap("gt", 0, 256), ap("pp", P0, P0 + 256), 0.0, A.is_gt)
+    red(c("ft", 0), ap("gt", 0, 256))
+    ts(c("ft", 4), c("ft", 0), 16.0, A.mult)
+
+    def wrapped(lst, mm_, ss_, row, w):
+        tt(ap(mm_, 0, w), row, ap("m16", 0, w), A.mult)
+        scan(ap(ss_, 0, w), ap("r16", 0, w), ap(mm_, 0, w))
+        cp(ap(lst, 0, w // 16), ap(ss_, 15, w, 16))
+    wrapped("jl4", "jm", "js", ap("pp", P3, P3 + 64), 64)
+    v = c("vl", 8 * slot)
+    ts(v, c("pp", P1), c("ft", 4), A.add)
+    pick("sp", 0, 64, "tq", 0, 256, "jl4", 0, 4)
+
+    to_all(v, v, "a_v")
+    to_all(ap("sp", 0, 32, bc=u8), ap("land", 32 * slot, 32 * slot + 32, bc=u8), "a_c")
+    to_all(ap("sps", 0, 32), ap("lands", 32 * slot, 32 * slot + 32), "a_s")
+    to_helper(ap("tqs", 0, 256), ap("hqs", 0, 256), "h_s")
+    move("land", 32 * slot, "sp", 0, 32)
+    move("xw", 128, "sp", 0, 64)
+    move("cd", 0, "tq", 0, 128)
+    move("cd2", 0, "tq", 0, 128)
+    move("sl", 32 * slot, "tq", 32 * me, 32)
+
+    fill(ap("eb", 0, 2048), 0.0)
+    for b in range(4):
+        act(ap("eb", 512 * b + b, 512 * b + 512, 4), ap("idn", 0, 128))
+    quant("eh", 0, 512, "eb")
+    fill(ap("nzx", 256, 768), 0.0)
+    quant("nq", 0, 192, "nzx")
+
+    def noise(t):
+        for b in range(4):
+            mm(ap("dv", 512 * b, 512 * b + 128), "eh", 128 * b, "nq", 32 * t, 32 * t + 128, True, False)
+    noise(0)
+    fill(ap("vt", 128, 512), 0.0)
+    fill(ap("vt2", 128, 512), 0.0)
+    cp(c("qf", 0), c("qi", 0))
+    ts(c("qi", 2), c("pi"), 7, A.bitwise_and)
+    ts(c("qi", 3), c("qi", 0), 3, A.logical_shift_right)
+    cp(ap("c16", 0, 16), ap("rm", 0, 16))
+    ts(c("qf", 1), c("qi", 3), -1.0, A.mult, 7.0, A.add)
+    ts(c("qf", 2), c("qi", 3), -8.0, A.mult, 63.0, A.add)
+    ts(c("qf", 3), c("qi", 3), 8.0, A.mult, 7.0, A.add)
+    ts(c("qf", 4), c("qi", 2), -8.0, A.mult, 63.0, A.add)
+    cp(c("qf", 5), c("qi", 2))
+    c4 = ap("c16", 0, 4)
+    ts(ap("lrs", 0, 4), c4, -2.0, A.mult, c("qf", 1), A.add)
+    ts(ap("grs", 0, 4), c4, -16.0, A.mult, c("qf", 2), A.add)
+    ts(ap("gr", 0, 4), c4, 16.0, A.mult, c("qf", 3), A.add)
+    ts(ap("gis", 0, 4), c4, 0.0, A.mult, c("qf", 4), A.add)
+    ts(ap("lq7", 0, 4), c4, 0.0, A.mult, c("qf", 5), A.add)
+    ts(ap("wr", 0, 4), c4, 16.0, A.mult, c("qf", 0), A.add)
+    ts(ap("w256", 0, 4), ap("wr", 0, 4), 256.0, A.mult)
+    ts(ap("ji", 0, 64), ap("rm", 0, 64), 7, A.bitwise_and)
+    cp(ap("ri", 0, 64), ap("ji", 0, 64))
+    ts(ap("r8", 0, 64), ap("ji", 0, 64), 0.0, A.not_equal)
+    ts(ap("i7", 0, 64), ap("ri", 0, 64), -1.0, A.mult, 7.0, A.add)
+    ts(ap("r8i", 0, 64), ap("rm", 0, 64), 3, A.logical_shift_right)
+    cp(ap("j8", 0, 64), ap("r8i", 0, 64))
+    tt(ap("tie", 0, 64), ap("ri", 0, 64), ap("j8", 0, 64), A.add)
+    ts(ap("tie", 0, 64), ap("tie", 0, 64), 7.5, A.is_gt, -0.5, A.mult)
+    fill(ap("wc", 0, 8), 32.0)
+
+    n8 = 56
+    arrive("vl", 0, 8 * slot, ("a_v", n8))
+    arrive("vl", 8 * slot + 8, 64, ("a_v", n8))
+    for k in ((0, 32 * slot), (32 * slot + 32, 256)):
+        arrive("land", k[0], k[1], ("a_c", n8))
+        arrive("lands", k[0], k[1], ("a_s", n8))
+    cp(ap("vi", 0, 8), ap("vl", 0, 64, 8))
+    ts(ap("fiti", 0, 8), ap("vi", 0, 8), 4, A.logical_shift_right)
+
+    def places(fit, k1, cm, sc):
+        tt(ap(k1, 0, 64), ap(fit, 0, 8, off=ap("lrs", 0, 4)), ap("tie", 0, 64), A.add)
+        tt(ap(cm, 0, 64), ap(fit, 0, 8, off=ap("lq7", 0, 4)), ap(k1, 0, 64), A.is_gt)
+        scan(ap(sc, 0, 64), ap("r8", 0, 64), ap(cm, 0, 64))
+    places("fiti", "k1", "cm", "sc")
+    mine = c("sc", 8 * me + 7)
+    ts(ap("ms", 0, 8), ap("sc", 7, 64, 8), mine, A.add, 7.0, A.not_equal)
+    scan(ap("st", 0, 8), ap("wc", 0, 8), ap("ms", 0, 8), A.add, A.mult)
+    ts(ap("ofa", 0, 2), ap("wr", 0, 2), c("st", 7), A.add)
+    pick("cd", 0, 32, "land", 0, 256, "ofa", 0, 2)
+
+    def make(cd, vt, out, a):
+        for b in range(4):
+            mm(ap("dv", 512 * b, 512 * b + 128), "eh", 128 * b, cd, 0, 128, False, True)
+        for b in (0, 2, 1, 3):
+            o, i = ap(vt, b, 128, 4), ap("dv", 512 * b, 512 * b + 32)
+            if b < 2:
+                act(o, i)
+            else:
+                cp(o, i)
+        quant(out, a, a + 128, vt)
+    ts(c("go", 0), mine, 3.5, A.is_lt, 160.0, A.mult)
+    ts(ap("ofx", 0, 2), ap("wr", 0, 2), c("go", 0), A.add)
+    make("cd", "vt", "xw", 0)
+    pick("xs", 0, 32, "xw", 0, 192, "ofx", 0, 2)
+
+    to_all(ap("xs", 0, 32, bc=u8), ap("cw", 32 * slot, 32 * slot + 32, bc=u8), "b_c")
+    to_all(ap("xss", 0, 32), ap("cws", 32 * slot, 32 * slot + 32), "b_s")
+    move("cw", 32 * slot, "xs", 0, 32)
+
+    ts(ap("nbi", 0, 8), ap("vi", 0, 8), 15, A.bitwise_and)
+    cp(c("colf", 0), c("qi", 1))
+    ts(c("colf", 1), c("colf", 0), 3.5, A.is_lt, 15.0, A.mult)
+    ts(c("colf", 2), c("colf", 1), 1.0, A.add)
+    ts(ap("nb", 0, 8), ap("nbi", 0, 8), c("colf", 2), A.mult)
+    o, i = ap("jt", 0, 1024, p=(0, 1)), ap("nb", 0, 8)
+    dma("y", o["v"], i["v"], [o], [i])
+    move("cw", 256, "land", 0, 256)
+    gi, grs = ap("gis", 0, 4), ap("grs", 0, 4)
+    ts(ap("a0", 0, 64), ap("sc", 0, 64, off=grs), -1.0, A.mult, 7.0, A.add)
+    tt(ap("b0", 0, 64), ap("sc", 0, 64, off=grs), ap("a0", 0, 64), A.min)
+    tt(ap("hit", 0, 64), ap("sc", 0, 64, off=gi), ap("b0", 0, 64), A.is_equal)
+    tt(ap("hf", 0, 64), ap("fiti", 0, 8, off=ap("lq7", 0, 4)), ap("hit", 0, 64), A.mult)
+    scan(ap("hfs", 0, 64), ap("r8", 0, 64), ap("hf", 0, 64))
+    tt(ap("hh", 0, 64), ap("hit", 0, 64), ap("ri", 0, 64), A.mult)
+    scan(ap("hhs", 0, 64), ap("r8", 0, 64), ap("hh", 0, 64))
+    ts(ap("tks", 0, 8), ap("a0", 0, 64, 8), 3.5, A.is_lt)
+    ts(ap("thr8", 0, 8), ap("tks", 0, 8), -1e29, A.mult, 1e29, A.add)
+    ts(ap("c2i", 0, 16), ap("rm", 0, 16), 1, A.logical_shift_right)
+    cp(ap("l256", 0, 16), ap("c2i", 0, 16))
+    cp(ap("thr", 0, 256), ap("thr8", 0, 8, off=ap("l256", 0, 16)))
+    ts(ap("r32i", 0, 256), ap("rm", 0, 256), 31, A.bitwise_and)
+    ts(ap("r32", 0, 256), ap("r32i", 0, 256), 0.0, A.not_equal)
+    fh = ap("hfs", 7, 64, 8)
+    ts(ap("tmp", 0, 8), fh, 224.0, A.min)
+    tt(ap("tmp", 0, 8), ap("tmp", 0, 8), fh, A.subtract)
+    tt(ap("tmp", 0, 8), ap("tmp", 0, 8), ap("tks", 0, 8), A.mult)
+    tt(ap("base1", 0, 8), ap("tmp", 0, 8), fh, A.add)
+    fill(c("wh8", 0), 0.0)
+    tt(ap("wh8", 1, 8), ap("hhs", 7, 56, 8), ap("hhs", 15, 64, 8), A.subtract)
+    ts(ap("wh", 0, 64), ap("wh8", 0, 8, off=ap("lq7", 0, 4)), 32.0, A.mult)
+    ts(c("cola", 2), c("hhs", 63), 32.0, A.mult)
+    tt(c("cola", 0), c("cola", 2), c("qf", 0), A.add)
+    ts(c("cola", 1), c("cola", 0), 16.0, A.add)
+    fill(ap("ones", 0, 64), 1.0)
+    ts(ap("m64", 0, 64), ap("rm", 0, 64), -1.0, A.mult, 64.0, A.add)
+    ts(ap("p256", 0, 64), ap("rm", 0, 64), 256.0, A.add)
+    ts(ap("x32", 0, 8), ap("c16", 0, 8), 32.0, A.mult, 256.0, A.add)
+    ts(ap("o0", 0, 8), ap("tks", 0, 8), -256.0, A.mult)
+    tt(ap("o0", 0, 8), ap("o0", 0, 8), ap("x32", 0, 8), A.add)
+    fill(c("w0", 0), 0.0)
+    tt(ap("w0", 1, 8), ap("o0", 0, 7), ap("o0", 1, 8), A.subtract)
+    mm(ap("pp", P1, P1 + 256), "uq", 0, "land", 0, 256)
+    act(ap("sw", 256, 512), ap("pp", P1, P1 + 256))
+    j1, j2, j3 = ap("jt", 0, 512, p=(0, 1)), ap("jt", 512, 1024, p=(0, 1)), ap("jt2", 0, 512, p=(0, 1))
+    tt(j3, j1, j2, A.add)
+    jr = ap("jr", 0, 512)
+    run("g", lambda q: q.partition_broadcast(jr["v"], j3["v"], 128), [jr], [j3])
+
+    def order_out(sc, row, t):
+        tt(ap("oda", 0, 64), ap(sc, 0, 64, off=gi), ap("j8", 0, 64), A.is_equal)
+        tt(ap("odb", 0, 64), ap("oda", 0, 64), ap("i7", 0, 64), A.mult)
+        scan(ap("odc", 0, 64), ap("r8", 0, 64), ap("odb", 0, 64))
+        cp(ap(row, 0, 8), ap("odc", 7, 64, 8))
+        x = ap(row, 0, 8, p=(0, 1))
+        dma("y", T.od[t:t + 1, 0:8], x["v"], [], [x])
+    order_out("sc", "od0", 0)
+    ts(ap("m16i", 64, 256), ap("dm", 64, 256), 15, A.bitwise_and)
+    ts(ap("m16", 64, 256), ap("m16i", 64, 256), 0.0, A.is_equal)
+    ts(ap("r16i", 64, 256), ap("rm", 64, 256), 15, A.bitwise_and)
+    ts(ap("r16", 64, 256), ap("r16i", 64, 256), 0.0, A.not_equal)
+    ts(ap("i32i", 0, 128), ap("dm", 0, 128), 31, A.bitwise_and)
+    ts(ap("i32r", 0, 128), ap("i32i", 0, 128), 0.0, A.is_equal)
+    cp(ap("frow", 0, 256), ap("rm", 0, 256))
+    quant("wq", 0, 128, "wx")
+
+    for k in ((0, 32 * slot), (32 * slot + 32, 256)):
+        arrive("cw", k[0], k[1], ("b_c", n8))
+        arrive("cws", k[0], k[1], ("b_s", n8))
+        arrive("sl", k[0], k[1], ("s_c", 14))
+        arrive("sls", k[0], k[1], ("s_s", 14))
+    mm(ap("pp", P0, P0 + 256), "uq", 0, "cw", 0, 256)
+    noise(1)
+    tt(ap("c1", 0, 256), ap("pp", P0, P0 + 256), ap("thr", 0, 256), A.is_gt)
+    scan(ap("s1", 0, 256), ap("r32", 0, 256), ap("c1", 0, 256))
+    tt(ap("fit1", 0, 8), ap("s1", 31, 256, 32), ap("base1", 0, 8), A.add)
+    places("fit1", "k1b", "cmb", "scb")
+    gr = ap("gr", 0, 4)
+    ts(ap("ab", 0, 64), ap("scb", 0, 64, off=gr), -1.0, A.mult, 7.0, A.add)
+    tt(ap("bb", 0, 64), ap("scb", 0, 64, off=gr), ap("ab", 0, 64), A.min)
+    tt(ap("miss", 0, 64), ap("scb", 0, 64, off=gi), ap("bb", 0, 64), A.not_equal)
+    scan(ap("bs", 0, 64), ap("wh", 0, 64), ap("miss", 0, 64), A.add, A.mult)
+    ts(ap("of", 0, 16, 2), ap("bs", 7, 64, 8), c("cola", 0), A.add)
+    ts(ap("of", 1, 16, 2), ap("bs", 7, 64, 8), c("cola", 1), A.add)
+    pick("sb", 0, 256, "sl", 0, 256, "of", 0, 16)
+
+    for n, b, sem in (("sb", u8, "c_c"), ("sbs", None, "c_s")):
+        ready("g", [ap(n, 0, 256)])
+        sent[0] += scatter_call(g, core, T, topo, me,
+                                lambda r: ap(n, 32 * r, 32 * r + 32, bc=b)["v"],
+                                ap("fw" + n[2:], 32 * me, 32 * me + 32, bc=b)["v"], T.sem[sem])
+    move("fw", 32 * me, "sb", 32 * me, 32)
+
+    act(ap("sw", 0, 256), ap("pp", P0, P0 + 256))
+    tt(c("o1", 0), c("bs", 8 * me + 7), c("cola", 2), A.add)
+    scan(ap("st0", 0, 8), ap("w0", 0, 8), ap("miss", 8 * me, 8 * me + 8), A.add, A.mult)
+    ts(ap("ofc", 0, 2), ap("wr", 0, 2), c("st0", 7), A.add, c("o0", 7), A.add)
+    ts(ap("ofc", 2, 4), ap("wr", 0, 2), c("o1", 0), A.add)
+    ts(ap("ofj", 0, 4), ap("w256", 0, 4), c("o1", 0), A.add, 1.0 / 32, A.mult)
+    cp(ap("csj", 0, 64), ap("sw", 0, 512, off=ap("ofc", 0, 4)))
+    cp(ap("csj", 64, 128), ap("jr", 0, 512, off=ap("ofj", 0, 4)))
+    tt(ap("dgo", 0, 128), ap("csj", 0, 128), ap("i32r", 0, 128), A.mult)
+    scan(ap("ds", 0, 128), ap("r32", 0, 128), ap("dgo", 0, 128))
+    pick("cc", 0, 64, "cw", 0, 512, "ofc", 0, 4)
+    cs, cj, cr, tp = ap("csj", 0, 64), ap("csj", 64, 128), ap("cr", 0, 64), ap("tp", 0, 64)
+    for e in (0, 1):
+        w = (64 * e, 64 * e + 64)
+        ts(ap("lt", *w), cs, c("ds", 32 * e + 31), A.is_lt)
+        ts(ap("eq", *w), cs, c("ds", 32 * e + 31), A.is_equal)
+        ts(ap("jl", *w), cj, c("ds", 64 + 32 * e + 31), A.is_lt)
+        tt(ap("eqj", *w), ap("eq", *w), ap("jl", *w), A.mult)
+        scan(ap("cnt", *w), ap("lt", *w), ap("eqj", *w), A.add, A.add)
+        ts(ap("tp", 32 * e, 32 * e + 32), ap("zf", 0, 32), c("cnt", 64 * e + 63), A.add)
+    run("v", lambda q: q.transpose(cr["v"], tp["v"]), [cr], [tp])
+    for e in (0, 1):
+        w = (64 * e, 64 * e + 64)
+        ts(ap("lm", *w), cr, c("wr", e), A.not_equal)
+        scan(ap("lmo", *w), ap("ones", 0, 64), ap("lm", *w), A.add, A.mult)
+        ts(c("l1", e), c("lmo", 64 * e + 63), -1.0, A.mult, 63.0, A.add)
+    pick("cd2", 0, 32, "cc", 0, 64, "l1", 0, 2)
+    make("cd2", "vt2", "fw", 320)
+
+    ts(c("t32", 0), c("scb", 8 * me + 7), 3.5, A.is_gt, 32.0, A.mult)
+    ts(ap("sel", 0, 64), cr, c("t32", 0), A.is_lt)
+    tt(ap("dif", 0, 64), cr, ap("m64", 0, 64), A.add)
+    tt(ap("mul", 0, 64), ap("dif", 0, 64), ap("sel", 0, 64), A.mult)
+    tt(ap("off", 0, 64), ap("mul", 0, 64), ap("p256", 0, 64), A.add)
+    wrapped("jw", "jwm", "jws", cj, 64)
+    cp(ap("frow", 0, 256, off=ap("jw", 0, 4)), ap("off", 0, 64))
+    wrapped("fl", "fm", "fs", ap("frow", 0, 256), 256)
+    pick("fw", 256, 320, "cw", 0, 512, "ofc", 0, 4)
+
+    for k in ((0, 32 * me), (32 * me + 32, 256)):
+        arrive("fw", k[0], k[1], ("c_c", 14))
+        arrive("fws", k[0], k[1], ("c_s", 14))
+    pick("oq2", 0, 256, "fw", 0, 448, "fl", 0, 16)
+    x = ap("oq2", 0, 256, bc=u8)
+    dma("y", T.oc[:, 0:1024], x["v"], [], [x])
+    for k in range(4):
+        x = ap("oq2s", 0, 256, p=(32 * k, 32 * k + 4))
+        dma("s" if k % 2 else "y", T.osc[4 * k:4 * k + 4, 0:256], x["v"], [], [x])
+    mm(ap("pp", P2, P2 + 256), "wq", 0, "oq2", 0, 256)
+    cp(ap("yo", 0, 256), ap("pp", P2, P2 + 256))
+    x = ap("yo", 0, 256)
+    dma("y", T.y[:, 0:256], x["v"], [], [x])
+    order_out("scb", "od1", 1)
+    finish()
+    g.wait_ge(T.sem.lo, sent[0])

@@ -26,21 +26,21 @@ def _bufs():
     b(BF, tbx=1024, nzx=768, wx=512, ux=512, u4=8, eb=2048, ct=1536, oh=512, vt=512, vt2=512, hb=128, idn=128,
       cmp=768, gt=256, c1=256)
     parts("bconst", BF, m16=256, r16=256, r8=64, r32=256, io64=64, i32r=128)
-    parts("fconst", F32, zf=128, dg=8, f0=128)
-    parts("fown", F32, ft=8, sm=256, pos=8, jm=64, js=64, junk=384)
-    parts("flist", F32, qf=8, c16=16, wr=8, w256=8,
-          tie=64, ri=64, i7=64, j8=64, wc=8, x32=8, colf=8, ones=64, m64=64, p256=64,
+    parts("fconst", F32, zf=128, sx=128, f0=128, hif=8, wr=8, c16r=8, c2=8, md16=256)
+    parts("fown", F32, ft=8, sm=256, pos=8, jm=64, js=64, junk=896)
+    parts("flist", F32, xx=8, w256=8, tsum=64, tie5=64, tie=64, ri=64, i7=64, j8=64, md32=256, ef=8, wc=8, x32=8,
+          colf=8, ones=64, m64=64, p256=64, tmp2=8, o0a=8, dd=64, nd=64,
           k1=64, cm=64, sc=64, ms=8, st=8, go=8, a0=64, b0=64, hit=64, hf=64, hfs=64, hh=64, hhs=64, tks=8, thr8=8,
-          thr=256, tmp=8, base1=8, wh8=8, wh=64, cola=8, o0=8, w0=8, sw=512, jr=512, oda=64, odb=64, odc=64,
-          s1=256, fit1=8, k1b=64, cmb=64, scb=64, ab=64, bb=64, miss=64, bs=64, o1=8, st0=8, t32=8, csj=128, dgo=128,
+          thr=256, tmp=8, base1=8, wh8=8, w0=8, wh=64, cola=8, o0=8, sw=512, jr=512, oda=64, odb=64, odc=64,
+          s1=256, k1b=64, cmb=64, scb=64, ab=64, bb=64, miss=64, bs=64, o1=8, st0=8, t32=8, csj=128, dgo=128,
           ds=128, lt=128, eq=128, jl=128, eqj=128, cnt=128, tp=64, cr=64, lm=128, lmo=128, sel=64, dif=64, mul=64,
           off=64, jwm=64, jws=64, frow=256, fm=256, fs=256)
     b(F32, nb=8, jt=1024, jt2=512, od0=8, od1=8, yo=256)
-    parts("iconst", I32, pi=8, rm=256, dm=256, qi=8, m16i=256, r16i=256, r8i=64, r32i=256, i32i=128, ji=64, c2i=16)
+    parts("iconst", I32, pi=8, hx=8, ai=8, yi=8, ei=8, bi=8, l2i=16)
     parts("iarr", I32, vi=8, fiti=8, nbi=8)
     b(U16, vl=64)
-    parts("lists", U16, jl4=4, lrs=4, lq7=4, grs=4, gr=4, gis=4, l256=16, ofa=2, ofx=2, of=16, ofc=4, ofj=4, l1=2,
-          jw=4, fl=16)
+    parts("lists", U16, jl4=4, in32=4, ou32=4, lrs=4, lq7=4, grs=4, gr=4, gis=4, l256=16, ofa=2, ofx=2, of=16, ofc=4,
+          ofj=4, l1=2, jw=4, fl=16)
     q(uq=128, tq=256, nq=192, wq=128, eh=512, cq=384, oq=128, sp=64, land=256, cd=128, xw=192, xs=32, cw=512,
       sl=256, sb=256, cc=64, cd2=128, fw=448, oq2=256, hq=256)
     SCRATCH["dv"] = ("psum", [128, 2048], F32)
@@ -72,7 +72,7 @@ def ways(core, T, topo, me):
     far = [r for r in range(len(T.cores)) if r != me and topo.chip(T.cores[r]) != topo.chip(core)]
     near = [r for r in range(len(T.cores)) if r != me and topo.chip(T.cores[r]) == topo.chip(core)]
     out = topo.engines(core, T.cores[far[0]])
-    inn = [e for e in topo.engines(core, T.cores[near[0]]) if e not in out]
+    inn = [e for e in topo.engines(core, T.cores[near[0]]) if e not in out][:2]
     return far, near, out, inn
 
 
@@ -81,34 +81,29 @@ def dest(T, topo, r):
     return DstId(rid=rid, pnc=pid)
 
 
-def scatter_call(g, core, T, topo, me, src, dst, sem):
-    far, near, out, inn = ways(core, T, topo, me)
-    tr = [RemoteDMATransfer(dst_ids=[dest(T, topo, r)], dma_engine_mask=1 << out[i], remote_sem=sem,
-                            src=src(r), dst=dst) for i, r in enumerate(far)]
-    tr += [RemoteDMATransfer(dst_ids=[dest(T, topo, r)], dma_engine_mask=bits(inn), remote_sem=sem,
-                             src=src(r), dst=dst) for r in near]
-    g.remote_dma_fused(tr, local_sem=T.sem.lo)
-    return len(far) + len(inn) * len(near)
+def one_each(g, T, topo, to, src, dst, sem):
+    g.remote_dma_fused([RemoteDMATransfer(dst_ids=[dest(T, topo, r)], dma_engine_mask=bits(e), remote_sem=sem,
+                                          src=src(r), dst=dst) for r, e in to], local_sem=T.sem.lo)
+    return sum(len(e) for _, e in to)
 
 
-def gather_call(g, core, T, topo, me, src, dst, sem):
-    far, near, out, inn = ways(core, T, topo, me)
-    g.remote_dma_fused([
-        RemoteDMATransfer(dst_ids=[dest(T, topo, r) for r in far], dma_engine_mask=bits(out), remote_sem=sem,
-                          srcs=[src], dsts=[dst] * len(far)),
-        RemoteDMATransfer(dst_ids=[dest(T, topo, r) for r in near], dma_engine_mask=bits(inn), remote_sem=sem,
-                          srcs=[src], dsts=[dst] * len(near))], local_sem=T.sem.lo)
-    return len(out) + len(inn)
+def same_to_all(g, T, topo, to, src, dst, sem):
+    g.remote_dma_fused([RemoteDMATransfer(dst_ids=[dest(T, topo, r) for r in rs], dma_engine_mask=bits(e),
+                                          remote_sem=sem, srcs=[src], dsts=[dst] * len(rs)) for rs, e in to],
+                       local_sem=T.sem.lo)
+    return sum(len(e) for _, e in to)
 
 
 def hand_on(g, core, T, topo, r):
     S = 32
     c0 = S * (len(T.cores) - 1 - r)
-    g.wait_ge(T.sem.h_c, 16)
-    n = scatter_call(g, core, T, topo, r, lambda s: T.hq[:, S * s:S * s + S].bitcast(dt.uint8),
-                     T.sl[:, c0:c0 + S].bitcast(dt.uint8), T.sem.s_c)
-    g.wait_ge(T.sem.h_s, 16)
-    n += scatter_call(g, core, T, topo, r, lambda s: T.hqs[:, S * s:S * s + S], T.sls[:, c0:c0 + S], T.sem.s_s)
+    far, near, out, inn = ways(core, T, topo, r)
+    to = [(s, out[i:i + 1]) for i, s in enumerate(far)] + [(s, inn[:1]) for s in near]
+    g.wait_ge(T.sem.h_c, len(out))
+    n = one_each(g, T, topo, to, lambda s: T.hq[:, S * s:S * s + S].bitcast(dt.uint8),
+                 T.sl[:, c0:c0 + S].bitcast(dt.uint8), T.sem.s_c)
+    g.wait_ge(T.sem.h_s, len(out))
+    n += one_each(g, T, topo, to, lambda s: T.hqs[:, S * s:S * s + S], T.sls[:, c0:c0 + S], T.sem.s_s)
     g.wait_ge(T.sem.lo, n)
 
 
@@ -203,6 +198,7 @@ def rank_program(g, core, T, topo):
     ap, run, dma, arrive, ready, finish = builder(g, T)
     u8, u32 = dt.uint8, dt.uint32
     slot = 7 - me
+    far, near, out, inn = ways(core, T, topo, me)
     sent = [0]
 
     def sca(x):
@@ -233,13 +229,13 @@ def rank_program(g, core, T, topo):
     def red(out, in_):
         run("v", lambda q: q.tensor_reduce(out["v"], in_["v"], AxisListType.X, A.add), [out], [in_])
 
-    def act(out, in_, func=F.Copy, bias=None, accum=None):
-        if bias is not None:
-            run("s", lambda q: q.activation(out["v"], in_["v"], F.Identity, bias=bias["v"]), [out], [in_, bias])
-        elif accum is not None:
-            run("s", lambda q: q.activation(out["v"], in_["v"], func, accum_out=accum["v"]), [out, accum], [in_])
-        else:
-            run("s", lambda q: q.activation(out["v"], in_["v"], func), [out], [in_])
+    def act(out, in_, func=None, bias=0.0, scale=1.0, accum=None):
+        plain = not dic(bias, scale) and bias == 0.0 and scale == 1.0
+        func = func or (F.Copy if plain else F.Identity)
+        kw = {} if plain else {"bias": sca(bias), "scale": sca(scale)}
+        if accum:
+            kw["accum_out"] = accum["v"]
+        run("s", lambda q: q.activation(out["v"], in_["v"], func, **kw), [out] + dic(accum), [in_] + dic(bias, scale))
 
     def quant(n, a, b, tile, x0=0):
         o, p, x = ap(n, a, b), ap(n + "s", a, b), ap(tile, x0, x0 + 4 * (b - a))
@@ -267,93 +263,115 @@ def rank_program(g, core, T, topo):
 
     def to_all(src, dst, sem):
         ready("g", [src])
-        sent[0] += gather_call(g, core, T, topo, me, src["v"], dst["v"], T.sem[sem])
+        sent[0] += same_to_all(g, T, topo, [(far, out), (near, inn)], src["v"], dst["v"], T.sem[sem])
 
     def c(n, k=0):
         return ap(n, k, k + 1)
 
-    load("s", "u4", 0, 4, T.u[:, 0:4])
-    load("y", "tbx", 0, 1024, T.tb[:, 0:1024])
-    load("y", "nzx", 0, 256, T.nz[:, 0:256])
-    load("y", "wx", 0, 512, T.w[:, 0:512])
-
-    def iota(n, k, pat, base, cm):
-        o = ap(n, 0, k)
-        run("g", lambda q: q.iota(o["v"], pat, base, cm), [o], [])
+    def iota(n, k, pat, base=0, cm=0):
+        o, small = ap(n, 0, k), SCRATCH[PART[n][0]][2] != I32
+        kw = {"allow_small_or_imprecise_dtypes": True} if small else {}
+        run("g", lambda q: q.iota(o["v"], pat, base, cm, **kw), [o], [])
 
     def asel(n, i, op, fl):
         o, x = ap(n, 0, 128), ap(i, 0, 128)
         run("g", lambda q: q.affine_select(o["v"], x["v"], [[-1, 128]], op, fl, 0, 1), [o], [x])
 
-    iota("pi", 1, [[0, 1]], 0, 1)
+    load("s", "u4", 0, 4, T.u[:, 0:4])
+    load("y", "tbx", 0, 1024, T.tb[:, 0:1024])
+    load("y", "nzx", 0, 256, T.nz[:, 0:256])
+    load("y", "wx", 0, 512, T.w[:, 0:512])
+    iota("pi", 4, [[0, 4]], 0, 1)
+    iota("c16r", 4, [[16, 4]])
+    iota("c2", 4, [[2, 4]])
     fill(ap("zf", 0, 128), 0.0)
+    fill(ap("sx", 0, 128), 16.0)
     fill(ap("hb", 0, 128), 0.5)
     asel("f0", "zf", A.is_gt, 1e29)
+    iota("io64", 64, [[1, 64]])
+    iota("md16", 256, [[0, 16], [1, 16]])
     asel("idn", "hb", A.is_equal, 0.0)
-    iota("rm", 256, [[1, 256]], 0, 0)
-    iota("dm", 256, [[1, 256]], 128, -1)
+    iota("ri", 64, [[0, 8], [1, 8]])
+    iota("tsum", 64, [[1, 8], [1, 8]])
+    pi, ai, yi = ap("pi", 0, 4), ap("ai", 0, 4), ap("yi", 0, 4)
+    ts(c("hx"), c("pi"), 4, A.logical_shift_right)
+    ts(ai, pi, 15, A.bitwise_and)
+    ts(yi, pi, 7, A.bitwise_and)
+    ts(c("ei"), c("pi"), 31, A.bitwise_and)
+    cp(c("hif"), c("hx"))
+    tt(ap("wr", 0, 4), ai, ap("c16r", 0, 4), A.add)
+    ts(ap("bi", 0, 4), ai, 3, A.logical_shift_right)
+    hi, lo, zf, sx = c("hif"), c("wr"), ap("zf", 0, 128), ap("sx", 0, 128)
+
+    def digit(k, t, in_, **kw):
+        act(ap("ct", 512 * k + t, 512 * k + 512, 4), in_, **kw)
+    digit(0, 0, sx, scale=hi)
+    digit(0, 1, sx, scale=hi, bias=128.0)
+    for t in (0, 1):
+        digit(1, t, zf, bias=lo)
+        for k in (0, 1):
+            digit(k, t + 2, zf)
     for t in range(4):
-        act(ap("ux", t, 512, 4), ap("zf", 0, 128), bias=c("u4", t))
-    ts(c("qi", 0), c("pi"), 15, A.bitwise_and)
-    ts(c("qi", 1), c("pi"), 4, A.logical_shift_right)
-    ts(c("dg", 0), c("qi", 1), 16.0, A.mult)
-    ts(c("dg", 1), c("qi", 1), 16.0, A.mult, 128.0, A.add)
-    cp(c("dg", 2), c("qi", 0))
-    cp(c("dg", 3), c("qi", 1))
-    ts(c("dg", 4), c("qi", 1), 8.0, A.add)
+        act(ap("ux", t, 512, 4), zf, bias=c("u4", t))
+    digit(2, 0, zf, bias=hi)
+    digit(2, 1, sx, scale=0.5, bias=hi)
+    for t in (2, 3):
+        digit(2, t, zf, bias=lo)
+    act(ap("r16", 0, 256), ap("md16", 0, 256), F.Sign)
     fill(ap("oh", 0, 512), 0.0)
-    fill(ap("ct", 0, 1024), 0.0)
+    ts(ap("m16", 0, 256), ap("md16", 0, 256), lo, A.is_equal)
+    fill(ap("eb", 0, 2048), 0.0)
     quant("uq", 0, 128, "ux")
-    for k, t, col in ((0, 0, 0), (0, 1, 1), (1, 0, 2), (1, 1, 2), (2, 0, 3), (2, 1, 4), (2, 2, 2), (2, 3, 2)):
-        act(ap("ct", 512 * k + t, 512 * k + 512, 4), ap("zf", 0, 128), bias=c("dg", col))
-    cp(ap("io64", 0, 64), ap("rm", 0, 64))
-    ts(ap("m16i", 0, 64), ap("dm", 0, 64), 15, A.bitwise_and)
-    ts(ap("m16", 0, 64), ap("m16i", 0, 64), 0.0, A.is_equal)
-    ts(ap("r16i", 0, 64), ap("rm", 0, 64), 15, A.bitwise_and)
-    ts(ap("r16", 0, 64), ap("r16i", 0, 64), 0.0, A.not_equal)
 
     quant("tq", 0, 256, "tbx")
     P0, P1, P2, P3 = 0, 512, 1024, 1536
     mm(ap("pp", P0, P0 + 256), "uq", 0, "tq", 0, 256)
     mm(ap("pp", P1, P1 + 128), "tq", 0, "uq", 0, 128)
     mm(ap("pp", P2, P2 + 128), "tq", 128, "uq", 0, 128)
-    h = helpers[me]
-    rid, pid, _ = topo.addr(h)
+    rid, pid, _ = topo.addr(helpers[me])
 
     def to_helper(n, o, sem):
         ready("g", [n])
-        g.remote_dma(o["v"], n["v"], T.sem[sem], T.sem.lo, pid, rid, topo.mask(core, h))
-        sent[0] += len(topo.engines(core, h))
+        g.remote_dma(o["v"], n["v"], T.sem[sem], T.sem.lo, pid, rid, bits(out))
+        sent[0] += len(out)
     to_helper(ap("tq", 0, 256, bc=u8), ap("hq", 0, 256, bc=u8), "h_c")
     quant("cq", 0, 384, "ct")
     s0, s1 = c("pp", P1), c("pp", P2)
-    ts(ap("cmp", 0, 256), ap("pp", P0, P0 + 256), s0, A.is_lt)
+    low, high, row = ap("pp", P0, P0 + 128), ap("pp", P0 + 128, P0 + 256), ap("pp", P0, P0 + 256)
     ts(ap("sm", 0, 128), ap("f0", 0, 128), s0, A.add)
-    tt(ap("cmp", 256, 384), ap("pp", P0, P0 + 128), ap("sm", 0, 128), A.is_equal)
-    act(ap("junk", 0, 384), ap("cmp", 0, 384), accum=c("pos", 0))
-    ts(ap("cmp", 384, 512), ap("pp", P0, P0 + 128), s1, A.is_le)
-    ts(ap("cmp", 512, 640), ap("pp", P0 + 128, P0 + 256), s1, A.is_lt)
     ts(ap("sm", 128, 256), ap("f0", 0, 128), s1, A.add)
-    tt(ap("cmp", 640, 768), ap("pp", P0 + 128, P0 + 256), ap("sm", 128, 256), A.is_equal)
-    red(c("pos", 4), ap("cmp", 384, 768))
-    for hh, k in ((0, 0), (1, 4)):
-        ts(ap("oh", hh, 256, 4), ap("io64", 0, 64), c("pos", k), A.is_equal)
-        ts(ap("oh", 258 + hh, 512, 4), ap("io64", 0, 64), c("pos", k), A.is_equal)
+    ts(ap("cmp", 384, 512), low, s1, A.is_le)
+    ts(ap("cmp", 512, 640), high, s1, A.is_lt)
+    act(ap("junk", 384, 640), ap("cmp", 384, 640), accum=c("pos", 1))
+    ts(ap("cmp", 0, 256), row, s0, A.is_lt)
+    tt(ap("cmp", 256, 384), low, ap("sm", 0, 128), A.is_equal)
+    act(ap("junk", 0, 384), ap("cmp", 0, 384), accum=c("pos", 0))
+    tt(ap("cmp", 640, 768), high, ap("sm", 128, 256), A.is_equal)
+    ts(ap("gt", 0, 256), row, 0.0, A.is_gt)
+    act(ap("junk", 640, 896), ap("gt", 0, 256), accum=c("ft"))
+    red(c("pos", 4), ap("cmp", 640, 768))
+    for t, e in ((1, 256), (259, 512)):
+        ts(ap("oh", t, e, 4), ap("io64", 0, 64), c("pos", 1), A.subtract, c("pos", 4), A.is_equal)
+    for t, e in ((0, 256), (258, 512)):
+        ts(ap("oh", t, e, 4), ap("io64", 0, 64), c("pos", 0), A.is_equal)
     quant("oq", 0, 128, "oh")
     mm(ap("pp", P3, P3 + 128), "cq", 0, "oq", 0, 128, True, False)
     mm(ap("pp", P3, P3 + 128), "cq", 128, "oq", 0, 128, False, True)
     mm(ap("pp", P1, P1 + 128), "oq", 0, "cq", 256, 384)
-    ts(ap("gt", 0, 256), ap("pp", P0, P0 + 256), 0.0, A.is_gt)
-    red(c("ft", 0), ap("gt", 0, 256))
-    ts(c("ft", 4), c("ft", 0), 16.0, A.mult)
 
-    def wrapped(lst, mm_, ss_, row, w):
-        tt(ap(mm_, 0, w), row, ap("m16", 0, w), A.mult)
-        scan(ap(ss_, 0, w), ap("r16", 0, w), ap(mm_, 0, w))
-        cp(ap(lst, 0, w // 16), ap(ss_, 15, w, 16))
-    wrapped("jl4", "jm", "js", ap("pp", P3, P3 + 64), 64)
+    def wrap1(m, row, w):
+        tt(ap(m, 0, w), row, ap("m16", 0, w), A.mult)
+
+    def wrap2(s, m, w):
+        scan(ap(s, 0, w), ap("r16", 0, w), ap(m, 0, w))
+
+    def wrap3(lst, s, w):
+        cp(ap(lst, 0, w // 16), ap(s, 15, w, 16))
+    wrap1("jm", ap("pp", P3, P3 + 64), 64)
     v = c("vl", 8 * slot)
-    ts(v, c("pp", P1), c("ft", 4), A.add)
+    ts(v, c("ft"), 64.0, A.mult, c("pp", P1), A.add)
+    wrap2("js", "jm", 64)
+    wrap3("jl4", "js", 64)
     pick("sp", 0, 64, "tq", 0, 256, "jl4", 0, 4)
 
     to_all(v, v, "a_v")
@@ -361,74 +379,74 @@ def rank_program(g, core, T, topo):
     to_all(ap("sps", 0, 32), ap("lands", 32 * slot, 32 * slot + 32), "a_s")
     to_helper(ap("tqs", 0, 256), ap("hqs", 0, 256), "h_s")
     move("land", 32 * slot, "sp", 0, 32)
-    move("xw", 128, "sp", 0, 64)
     move("cd", 0, "tq", 0, 128)
+    move("xw", 128, "sp", 0, 64)
     move("cd2", 0, "tq", 0, 128)
     move("sl", 32 * slot, "tq", 32 * me, 32)
 
-    fill(ap("eb", 0, 2048), 0.0)
     for b in range(4):
         act(ap("eb", 512 * b + b, 512 * b + 512, 4), ap("idn", 0, 128))
-    quant("eh", 0, 512, "eb")
+    act(ap("r8", 0, 64), ap("ri", 0, 64), F.Sign)
+    xx = ap("xx", 0, 4)
+    tt(xx, ap("bi", 0, 4), ap("c2", 0, 4), A.add)
+    ts(ap("tie5", 0, 64), ap("tsum", 0, 64), 7.5, A.is_gt, -1.0, A.mult)
+    cp(ap("lq7", 0, 4), yi)
+    ts(ap("lrs", 0, 4), xx, -1.0, A.mult, 7.0, A.add)
+    ts(ap("tie", 0, 64), ap("tie5", 0, 64), 0.5, A.add, 64.0, A.mult)
     fill(ap("nzx", 256, 768), 0.0)
+    fill(ap("vt", 128, 512), 0.0)
+    quant("eh", 0, 512, "eb")
     quant("nq", 0, 192, "nzx")
 
     def noise(t):
         for b in range(4):
             mm(ap("dv", 512 * b, 512 * b + 128), "eh", 128 * b, "nq", 32 * t, 32 * t + 128, True, False)
     noise(0)
-    fill(ap("vt", 128, 512), 0.0)
-    fill(ap("vt2", 128, 512), 0.0)
-    cp(c("qf", 0), c("qi", 0))
-    ts(c("qi", 2), c("pi"), 7, A.bitwise_and)
-    ts(c("qi", 3), c("qi", 0), 3, A.logical_shift_right)
-    cp(ap("c16", 0, 16), ap("rm", 0, 16))
-    ts(c("qf", 1), c("qi", 3), -1.0, A.mult, 7.0, A.add)
-    ts(c("qf", 2), c("qi", 3), -8.0, A.mult, 63.0, A.add)
-    ts(c("qf", 3), c("qi", 3), 8.0, A.mult, 7.0, A.add)
-    ts(c("qf", 4), c("qi", 2), -8.0, A.mult, 63.0, A.add)
-    cp(c("qf", 5), c("qi", 2))
-    c4 = ap("c16", 0, 4)
-    ts(ap("lrs", 0, 4), c4, -2.0, A.mult, c("qf", 1), A.add)
-    ts(ap("grs", 0, 4), c4, -16.0, A.mult, c("qf", 2), A.add)
-    ts(ap("gr", 0, 4), c4, 16.0, A.mult, c("qf", 3), A.add)
-    ts(ap("gis", 0, 4), c4, 0.0, A.mult, c("qf", 4), A.add)
-    ts(ap("lq7", 0, 4), c4, 0.0, A.mult, c("qf", 5), A.add)
-    ts(ap("wr", 0, 4), c4, 16.0, A.mult, c("qf", 0), A.add)
-    ts(ap("w256", 0, 4), ap("wr", 0, 4), 256.0, A.mult)
-    ts(ap("ji", 0, 64), ap("rm", 0, 64), 7, A.bitwise_and)
-    cp(ap("ri", 0, 64), ap("ji", 0, 64))
-    ts(ap("r8", 0, 64), ap("ji", 0, 64), 0.0, A.not_equal)
-    ts(ap("i7", 0, 64), ap("ri", 0, 64), -1.0, A.mult, 7.0, A.add)
-    ts(ap("r8i", 0, 64), ap("rm", 0, 64), 3, A.logical_shift_right)
-    cp(ap("j8", 0, 64), ap("r8i", 0, 64))
-    tt(ap("tie", 0, 64), ap("ri", 0, 64), ap("j8", 0, 64), A.add)
-    ts(ap("tie", 0, 64), ap("tie", 0, 64), 7.5, A.is_gt, -0.5, A.mult)
     fill(ap("wc", 0, 8), 32.0)
+    ts(ap("tie5", 0, 64), ap("tie5", 0, 64), 0.5, A.add)
+    ts(ap("gis", 0, 4), yi, -8.0, A.mult, 63.0, A.add)
+    ts(ap("grs", 0, 4), xx, -8.0, A.mult, 63.0, A.add)
+    ts(ap("gr", 0, 4), xx, 8.0, A.mult, 7.0, A.add)
+    ts(ap("in32", 0, 4), yi, 32.0, A.mult, 31.0, A.add)
+    ts(ap("ou32", 0, 4), xx, -32.0, A.mult, 255.0, A.add)
+    fill(ap("ones", 0, 64), 1.0)
+    ts(c("colf"), hi, 3.5, A.is_lt, 15.0, A.mult)
+    ts(ap("w256", 0, 4), ap("wr", 0, 4), 256.0, A.mult)
+    ts(c("colf", 1), c("colf"), 1.0, A.add)
+    fill(ap("vt2", 128, 512), 0.0)
+    fill(ap("wh8", 0, 16), 0.0)
+    iota("l2i", 16, [[1, 8], [0, 2]])
+    iota("j8", 64, [[1, 8], [0, 8]])
+    iota("i7", 64, [[0, 8], [-1, 8]], 7)
+    iota("md32", 256, [[0, 8], [1, 32]])
+    iota("x32", 8, [[32, 8]], 256)
+    iota("m64", 64, [[-1, 64]], 64)
+    iota("p256", 64, [[1, 64]], 256)
+    iota("frow", 256, [[1, 256]])
+    act(ap("r32", 0, 256), ap("md32", 0, 256), F.Sign)
 
-    n8 = 56
+    n8 = len(far) * len(out) + len(near) * len(inn)
     arrive("vl", 0, 8 * slot, ("a_v", n8))
     arrive("vl", 8 * slot + 8, 64, ("a_v", n8))
     for k in ((0, 32 * slot), (32 * slot + 32, 256)):
         arrive("land", k[0], k[1], ("a_c", n8))
         arrive("lands", k[0], k[1], ("a_s", n8))
     cp(ap("vi", 0, 8), ap("vl", 0, 64, 8))
-    ts(ap("fiti", 0, 8), ap("vi", 0, 8), 4, A.logical_shift_right)
-
-    def places(fit, k1, cm, sc):
-        tt(ap(k1, 0, 64), ap(fit, 0, 8, off=ap("lrs", 0, 4)), ap("tie", 0, 64), A.add)
-        tt(ap(cm, 0, 64), ap(fit, 0, 8, off=ap("lq7", 0, 4)), ap(k1, 0, 64), A.is_gt)
-        scan(ap(sc, 0, 64), ap("r8", 0, 64), ap(cm, 0, 64))
-    places("fiti", "k1", "cm", "sc")
+    lq7, lrs, r8 = ap("lq7", 0, 4), ap("lrs", 0, 4), ap("r8", 0, 64)
+    tt(ap("k1", 0, 64), ap("vi", 0, 8, off=lrs), ap("tie", 0, 64), A.add)
+    tt(ap("cm", 0, 64), ap("vi", 0, 8, off=lq7), ap("k1", 0, 64), A.is_gt)
+    scan(ap("sc", 0, 64), r8, ap("cm", 0, 64))
     mine = c("sc", 8 * me + 7)
     ts(ap("ms", 0, 8), ap("sc", 7, 64, 8), mine, A.add, 7.0, A.not_equal)
     scan(ap("st", 0, 8), ap("wc", 0, 8), ap("ms", 0, 8), A.add, A.mult)
     ts(ap("ofa", 0, 2), ap("wr", 0, 2), c("st", 7), A.add)
     pick("cd", 0, 32, "land", 0, 256, "ofa", 0, 2)
 
-    def make(cd, vt, out, a):
+    def products(cd):
         for b in range(4):
             mm(ap("dv", 512 * b, 512 * b + 128), "eh", 128 * b, cd, 0, 128, False, True)
+
+    def packed(vt, out, a):
         for b in (0, 2, 1, 3):
             o, i = ap(vt, b, 128, 4), ap("dv", 512 * b, 512 * b + 32)
             if b < 2:
@@ -436,59 +454,53 @@ def rank_program(g, core, T, topo):
             else:
                 cp(o, i)
         quant(out, a, a + 128, vt)
-    ts(c("go", 0), mine, 3.5, A.is_lt, 160.0, A.mult)
-    ts(ap("ofx", 0, 2), ap("wr", 0, 2), c("go", 0), A.add)
-    make("cd", "vt", "xw", 0)
+    products("cd")
+    ts(c("go"), mine, 3.5, A.is_lt, 160.0, A.mult)
+    ts(ap("fiti", 0, 8), ap("vi", 0, 8), 6, A.logical_shift_right)
+    ts(ap("ofx", 0, 2), ap("wr", 0, 2), c("go"), A.add)
+    ts(ap("nbi", 0, 8), ap("vi", 0, 8), 15, A.bitwise_and)
+    packed("vt", "xw", 0)
     pick("xs", 0, 32, "xw", 0, 192, "ofx", 0, 2)
 
     to_all(ap("xs", 0, 32, bc=u8), ap("cw", 32 * slot, 32 * slot + 32, bc=u8), "b_c")
     to_all(ap("xss", 0, 32), ap("cws", 32 * slot, 32 * slot + 32), "b_s")
     move("cw", 32 * slot, "xs", 0, 32)
 
-    ts(ap("nbi", 0, 8), ap("vi", 0, 8), 15, A.bitwise_and)
-    cp(c("colf", 0), c("qi", 1))
-    ts(c("colf", 1), c("colf", 0), 3.5, A.is_lt, 15.0, A.mult)
-    ts(c("colf", 2), c("colf", 1), 1.0, A.add)
-    ts(ap("nb", 0, 8), ap("nbi", 0, 8), c("colf", 2), A.mult)
+    gi, grs = ap("gis", 0, 4), ap("grs", 0, 4)
+    ts(ap("a0", 0, 64), ap("sc", 0, 64, off=grs), -1.0, A.mult, 7.0, A.add)
+    ts(ap("nb", 0, 8), ap("nbi", 0, 8), c("colf", 1), A.mult)
     o, i = ap("jt", 0, 1024, p=(0, 1)), ap("nb", 0, 8)
     dma("y", o["v"], i["v"], [o], [i])
     move("cw", 256, "land", 0, 256)
-    gi, grs = ap("gis", 0, 4), ap("grs", 0, 4)
-    ts(ap("a0", 0, 64), ap("sc", 0, 64, off=grs), -1.0, A.mult, 7.0, A.add)
     tt(ap("b0", 0, 64), ap("sc", 0, 64, off=grs), ap("a0", 0, 64), A.min)
-    tt(ap("hit", 0, 64), ap("sc", 0, 64, off=gi), ap("b0", 0, 64), A.is_equal)
-    tt(ap("hf", 0, 64), ap("fiti", 0, 8, off=ap("lq7", 0, 4)), ap("hit", 0, 64), A.mult)
-    scan(ap("hfs", 0, 64), ap("r8", 0, 64), ap("hf", 0, 64))
-    tt(ap("hh", 0, 64), ap("hit", 0, 64), ap("ri", 0, 64), A.mult)
-    scan(ap("hhs", 0, 64), ap("r8", 0, 64), ap("hh", 0, 64))
     ts(ap("tks", 0, 8), ap("a0", 0, 64, 8), 3.5, A.is_lt)
+    tt(ap("hit", 0, 64), ap("sc", 0, 64, off=gi), ap("b0", 0, 64), A.is_equal)
     ts(ap("thr8", 0, 8), ap("tks", 0, 8), -1e29, A.mult, 1e29, A.add)
-    ts(ap("c2i", 0, 16), ap("rm", 0, 16), 1, A.logical_shift_right)
-    cp(ap("l256", 0, 16), ap("c2i", 0, 16))
-    cp(ap("thr", 0, 256), ap("thr8", 0, 8, off=ap("l256", 0, 16)))
-    ts(ap("r32i", 0, 256), ap("rm", 0, 256), 31, A.bitwise_and)
-    ts(ap("r32", 0, 256), ap("r32i", 0, 256), 0.0, A.not_equal)
+    tt(ap("hf", 0, 64), ap("fiti", 0, 8, off=lq7), ap("hit", 0, 64), A.mult)
+    tt(ap("hh", 0, 64), ap("hit", 0, 64), ap("ri", 0, 64), A.mult)
+    scan(ap("hfs", 0, 64), r8, ap("hf", 0, 64))
+    scan(ap("hhs", 0, 64), r8, ap("hh", 0, 64))
     fh = ap("hfs", 7, 64, 8)
-    ts(ap("tmp", 0, 8), fh, 224.0, A.min)
-    tt(ap("tmp", 0, 8), ap("tmp", 0, 8), fh, A.subtract)
-    tt(ap("tmp", 0, 8), ap("tmp", 0, 8), ap("tks", 0, 8), A.mult)
-    tt(ap("base1", 0, 8), ap("tmp", 0, 8), fh, A.add)
-    fill(c("wh8", 0), 0.0)
+    ts(ap("tmp", 0, 8), fh, -224.0, A.add, 0.0, A.max)
     tt(ap("wh8", 1, 8), ap("hhs", 7, 56, 8), ap("hhs", 15, 64, 8), A.subtract)
-    ts(ap("wh", 0, 64), ap("wh8", 0, 8, off=ap("lq7", 0, 4)), 32.0, A.mult)
+    tt(ap("tmp2", 0, 8), ap("tmp", 0, 8), ap("tks", 0, 8), A.mult)
+    ts(ap("wh", 0, 64), ap("wh8", 0, 8, off=lq7), 32.0, A.mult)
+    tt(ap("base1", 0, 8), fh, ap("tmp2", 0, 8), A.subtract)
+    ts(c("cola", 0), c("hhs", 63), 32.0, A.mult, c("wr", 0), A.add)
+    ts(c("cola", 1), c("hhs", 63), 32.0, A.mult, c("wr", 1), A.add)
+    tt(ap("dd", 0, 64), ap("base1", 0, 8, off=lrs), ap("tie5", 0, 64), A.add)
+    cp(ap("l256", 0, 16), ap("l2i", 0, 16))
     ts(c("cola", 2), c("hhs", 63), 32.0, A.mult)
-    tt(c("cola", 0), c("cola", 2), c("qf", 0), A.add)
-    ts(c("cola", 1), c("cola", 0), 16.0, A.add)
-    fill(ap("ones", 0, 64), 1.0)
-    ts(ap("m64", 0, 64), ap("rm", 0, 64), -1.0, A.mult, 64.0, A.add)
-    ts(ap("p256", 0, 64), ap("rm", 0, 64), 256.0, A.add)
-    ts(ap("x32", 0, 8), ap("c16", 0, 8), 32.0, A.mult, 256.0, A.add)
-    ts(ap("o0", 0, 8), ap("tks", 0, 8), -256.0, A.mult)
-    tt(ap("o0", 0, 8), ap("o0", 0, 8), ap("x32", 0, 8), A.add)
-    fill(c("w0", 0), 0.0)
-    tt(ap("w0", 1, 8), ap("o0", 0, 7), ap("o0", 1, 8), A.subtract)
+    tt(ap("nd", 0, 64), ap("base1", 0, 8, off=lq7), ap("dd", 0, 64), A.subtract)
+    cp(ap("thr", 0, 256), ap("thr8", 0, 8, off=ap("l256", 0, 16)))
     mm(ap("pp", P1, P1 + 256), "uq", 0, "land", 0, 256)
     act(ap("sw", 256, 512), ap("pp", P1, P1 + 256))
+    ts(ap("o0a", 0, 8), ap("tks", 0, 8), -256.0, A.mult)
+    cp(c("ef"), c("ei"))
+    tt(ap("o0", 0, 8), ap("o0a", 0, 8), ap("x32", 0, 8), A.add)
+    quant("wq", 0, 128, "wx")
+    tt(ap("w0", 1, 8), ap("o0", 0, 7), ap("o0", 1, 8), A.subtract)
+    ts(ap("i32r", 0, 128), ap("md32", 0, 128), c("ef"), A.is_equal)
     j1, j2, j3 = ap("jt", 0, 512, p=(0, 1)), ap("jt", 512, 1024, p=(0, 1)), ap("jt2", 0, 512, p=(0, 1))
     tt(j3, j1, j2, A.add)
     jr = ap("jr", 0, 512)
@@ -497,31 +509,24 @@ def rank_program(g, core, T, topo):
     def order_out(sc, row, t):
         tt(ap("oda", 0, 64), ap(sc, 0, 64, off=gi), ap("j8", 0, 64), A.is_equal)
         tt(ap("odb", 0, 64), ap("oda", 0, 64), ap("i7", 0, 64), A.mult)
-        scan(ap("odc", 0, 64), ap("r8", 0, 64), ap("odb", 0, 64))
+        scan(ap("odc", 0, 64), r8, ap("odb", 0, 64))
         cp(ap(row, 0, 8), ap("odc", 7, 64, 8))
         x = ap(row, 0, 8, p=(0, 1))
         dma("y", T.od[t:t + 1, 0:8], x["v"], [], [x])
     order_out("sc", "od0", 0)
-    ts(ap("m16i", 64, 256), ap("dm", 64, 256), 15, A.bitwise_and)
-    ts(ap("m16", 64, 256), ap("m16i", 64, 256), 0.0, A.is_equal)
-    ts(ap("r16i", 64, 256), ap("rm", 64, 256), 15, A.bitwise_and)
-    ts(ap("r16", 64, 256), ap("r16i", 64, 256), 0.0, A.not_equal)
-    ts(ap("i32i", 0, 128), ap("dm", 0, 128), 31, A.bitwise_and)
-    ts(ap("i32r", 0, 128), ap("i32i", 0, 128), 0.0, A.is_equal)
-    cp(ap("frow", 0, 256), ap("rm", 0, 256))
-    quant("wq", 0, 128, "wx")
 
     for k in ((0, 32 * slot), (32 * slot + 32, 256)):
         arrive("cw", k[0], k[1], ("b_c", n8))
         arrive("cws", k[0], k[1], ("b_s", n8))
-        arrive("sl", k[0], k[1], ("s_c", 14))
-        arrive("sls", k[0], k[1], ("s_s", 14))
+        arrive("sl", k[0], k[1], ("s_c", 7))
+        arrive("sls", k[0], k[1], ("s_s", 7))
     mm(ap("pp", P0, P0 + 256), "uq", 0, "cw", 0, 256)
     noise(1)
     tt(ap("c1", 0, 256), ap("pp", P0, P0 + 256), ap("thr", 0, 256), A.is_gt)
     scan(ap("s1", 0, 256), ap("r32", 0, 256), ap("c1", 0, 256))
-    tt(ap("fit1", 0, 8), ap("s1", 31, 256, 32), ap("base1", 0, 8), A.add)
-    places("fit1", "k1b", "cmb", "scb")
+    tt(ap("k1b", 0, 64), ap("s1", 0, 256, off=ap("in32", 0, 4)), ap("nd", 0, 64), A.add)
+    tt(ap("cmb", 0, 64), ap("s1", 0, 256, off=ap("ou32", 0, 4)), ap("k1b", 0, 64), A.is_lt)
+    scan(ap("scb", 0, 64), r8, ap("cmb", 0, 64))
     gr = ap("gr", 0, 4)
     ts(ap("ab", 0, 64), ap("scb", 0, 64, off=gr), -1.0, A.mult, 7.0, A.add)
     tt(ap("bb", 0, 64), ap("scb", 0, 64, off=gr), ap("ab", 0, 64), A.min)
@@ -529,67 +534,84 @@ def rank_program(g, core, T, topo):
     scan(ap("bs", 0, 64), ap("wh", 0, 64), ap("miss", 0, 64), A.add, A.mult)
     ts(ap("of", 0, 16, 2), ap("bs", 7, 64, 8), c("cola", 0), A.add)
     ts(ap("of", 1, 16, 2), ap("bs", 7, 64, 8), c("cola", 1), A.add)
-    pick("sb", 0, 256, "sl", 0, 256, "of", 0, 16)
+    mh = 4 * (me // 4)
+    halves = (4 - mh, mh)
+    for r0 in halves:
+        pick("sb", 32 * r0, 32 * r0 + 128, "sl", 0, 256, "of", 2 * r0, 2 * r0 + 8)
 
     for n, b, sem in (("sb", u8, "c_c"), ("sbs", None, "c_s")):
-        ready("g", [ap(n, 0, 256)])
-        sent[0] += scatter_call(g, core, T, topo, me,
-                                lambda r: ap(n, 32 * r, 32 * r + 32, bc=b)["v"],
+        for r0 in halves:
+            to = [r for r in range(r0, r0 + 4) if r in far]
+            w = len(out) // len(to)
+            to = [(r, out[w * i:w * i + w]) for i, r in enumerate(to)] + [(r, inn) for r in near if r0 == mh]
+            ready("g", [ap(n, 32 * r0, 32 * r0 + 128)])
+            sent[0] += one_each(g, T, topo, to, lambda r: ap(n, 32 * r, 32 * r + 32, bc=b)["v"],
                                 ap("fw" + n[2:], 32 * me, 32 * me + 32, bc=b)["v"], T.sem[sem])
+    n3 = 4 * len(out) // 4 + 2 * len(out) // 2 + len(inn)
     move("fw", 32 * me, "sb", 32 * me, 32)
 
     act(ap("sw", 0, 256), ap("pp", P0, P0 + 256))
-    tt(c("o1", 0), c("bs", 8 * me + 7), c("cola", 2), A.add)
+    tt(c("o1"), c("bs", 8 * me + 7), c("cola", 2), A.add)
     scan(ap("st0", 0, 8), ap("w0", 0, 8), ap("miss", 8 * me, 8 * me + 8), A.add, A.mult)
+    ts(ap("ofj", 0, 4), ap("w256", 0, 4), c("o1"), A.add, 1.0 / 32, A.mult)
+    ts(ap("ofc", 2, 4), ap("wr", 0, 2), c("o1"), A.add)
     ts(ap("ofc", 0, 2), ap("wr", 0, 2), c("st0", 7), A.add, c("o0", 7), A.add)
-    ts(ap("ofc", 2, 4), ap("wr", 0, 2), c("o1", 0), A.add)
-    ts(ap("ofj", 0, 4), ap("w256", 0, 4), c("o1", 0), A.add, 1.0 / 32, A.mult)
-    cp(ap("csj", 0, 64), ap("sw", 0, 512, off=ap("ofc", 0, 4)))
-    cp(ap("csj", 64, 128), ap("jr", 0, 512, off=ap("ofj", 0, 4)))
-    tt(ap("dgo", 0, 128), ap("csj", 0, 128), ap("i32r", 0, 128), A.mult)
-    scan(ap("ds", 0, 128), ap("r32", 0, 128), ap("dgo", 0, 128))
-    pick("cc", 0, 64, "cw", 0, 512, "ofc", 0, 4)
     cs, cj, cr, tp = ap("csj", 0, 64), ap("csj", 64, 128), ap("cr", 0, 64), ap("tp", 0, 64)
-    for e in (0, 1):
-        w = (64 * e, 64 * e + 64)
-        ts(ap("lt", *w), cs, c("ds", 32 * e + 31), A.is_lt)
+    cp(cj, ap("jr", 0, 512, off=ap("ofj", 0, 4)))
+    cp(cs, ap("sw", 0, 512, off=ap("ofc", 0, 4)))
+    ts(c("t32"), c("scb", 8 * me + 7), 3.5, A.is_gt, 32.0, A.mult)
+    tt(ap("dgo", 0, 128), ap("csj", 0, 128), ap("i32r", 0, 128), A.mult)
+    pick("cc", 0, 64, "cw", 0, 512, "ofc", 0, 4)
+    scan(ap("ds", 0, 128), ap("r32", 0, 128), ap("dgo", 0, 128))
+    pick("fw", 256, 320, "cw", 0, 512, "ofc", 0, 4)
+    two = [(e, (64 * e, 64 * e + 64)) for e in (0, 1)]
+    for e, w in two:
         ts(ap("eq", *w), cs, c("ds", 32 * e + 31), A.is_equal)
         ts(ap("jl", *w), cj, c("ds", 64 + 32 * e + 31), A.is_lt)
+    for e, w in two:
+        ts(ap("lt", *w), cs, c("ds", 32 * e + 31), A.is_lt)
         tt(ap("eqj", *w), ap("eq", *w), ap("jl", *w), A.mult)
+    wrap1("jwm", cj, 64)
+    for e, w in two:
         scan(ap("cnt", *w), ap("lt", *w), ap("eqj", *w), A.add, A.add)
+    for e, w in two:
         ts(ap("tp", 32 * e, 32 * e + 32), ap("zf", 0, 32), c("cnt", 64 * e + 63), A.add)
+    wrap2("jws", "jwm", 64)
     run("v", lambda q: q.transpose(cr["v"], tp["v"]), [cr], [tp])
-    for e in (0, 1):
-        w = (64 * e, 64 * e + 64)
+    wrap3("jw", "jws", 64)
+    for e, w in two:
         ts(ap("lm", *w), cr, c("wr", e), A.not_equal)
+    ts(ap("sel", 0, 64), cr, c("t32"), A.is_lt)
+    for e, w in two:
         scan(ap("lmo", *w), ap("ones", 0, 64), ap("lm", *w), A.add, A.mult)
-        ts(c("l1", e), c("lmo", 64 * e + 63), -1.0, A.mult, 63.0, A.add)
-    pick("cd2", 0, 32, "cc", 0, 64, "l1", 0, 2)
-    make("cd2", "vt2", "fw", 320)
-
-    ts(c("t32", 0), c("scb", 8 * me + 7), 3.5, A.is_gt, 32.0, A.mult)
-    ts(ap("sel", 0, 64), cr, c("t32", 0), A.is_lt)
     tt(ap("dif", 0, 64), cr, ap("m64", 0, 64), A.add)
+    for e, w in two:
+        ts(c("l1", e), c("lmo", 64 * e + 63), -1.0, A.mult, 63.0, A.add)
     tt(ap("mul", 0, 64), ap("dif", 0, 64), ap("sel", 0, 64), A.mult)
+    pick("cd2", 0, 32, "cc", 0, 64, "l1", 0, 2)
+    products("cd2")
     tt(ap("off", 0, 64), ap("mul", 0, 64), ap("p256", 0, 64), A.add)
-    wrapped("jw", "jwm", "jws", cj, 64)
     cp(ap("frow", 0, 256, off=ap("jw", 0, 4)), ap("off", 0, 64))
-    wrapped("fl", "fm", "fs", ap("frow", 0, 256), 256)
-    pick("fw", 256, 320, "cw", 0, 512, "ofc", 0, 4)
+    wrap1("fm", ap("frow", 0, 256), 256)
+    packed("vt2", "fw", 320)
+    wrap2("fs", "fm", 256)
+    wrap3("fl", "fs", 256)
 
     for k in ((0, 32 * me), (32 * me + 32, 256)):
-        arrive("fw", k[0], k[1], ("c_c", 14))
-        arrive("fws", k[0], k[1], ("c_s", 14))
-    pick("oq2", 0, 256, "fw", 0, 448, "fl", 0, 16)
+        arrive("fw", k[0], k[1], ("c_c", n3))
+        arrive("fws", k[0], k[1], ("c_s", n3))
+    for k, pk in ((0, P2), (1, P3)):
+        pick("oq2", 128 * k, 128 * k + 128, "fw", 0, 448, "fl", 8 * k, 8 * k + 8)
+        mm(ap("pp", pk, pk + 128), "wq", 0, "oq2", 128 * k, 128 * k + 128)
     x = ap("oq2", 0, 256, bc=u8)
     dma("y", T.oc[:, 0:1024], x["v"], [], [x])
+    order_out("scb", "od1", 1)
     for k in range(4):
         x = ap("oq2s", 0, 256, p=(32 * k, 32 * k + 4))
         dma("s" if k % 2 else "y", T.osc[4 * k:4 * k + 4, 0:256], x["v"], [], [x])
-    mm(ap("pp", P2, P2 + 256), "wq", 0, "oq2", 0, 256)
-    cp(ap("yo", 0, 256), ap("pp", P2, P2 + 256))
+    act(ap("yo", 0, 128), ap("pp", P2, P2 + 128))
+    cp(ap("yo", 128, 256), ap("pp", P3, P3 + 128))
     x = ap("yo", 0, 256)
     dma("y", T.y[:, 0:256], x["v"], [], [x])
-    order_out("scb", "od1", 1)
     finish()
     g.wait_ge(T.sem.lo, sent[0])

@@ -23,33 +23,33 @@ def _bufs():
         for k in kw:
             SCRATCH[k] = ("sbuf", [128, kw[k]], CODE)
             SCRATCH[k + "s"] = ("sbuf", [128, kw[k]], PLANE)
-    b(BF, tbx=1024, nzx=768, wx=512, ux=512, u4=8, eb=2048, ct=1536, oh=512, vt=512, vt2=512, hb=128, idn=128,
-      cmp=768, gt=256, c1=256)
-    parts("bconst", BF, m16=256, r16=256, r8=64, r32=256, io64=64, i32r=128)
-    parts("fconst", F32, zf=128, sx=128, f0=128, hif=8, wr=8, c16r=8, c2=8, md16=256)
-    parts("fown", F32, ft=8, sm=256, pos=8, jm=64, js=64, junk=896)
-    parts("flist", F32, xx=8, w256=8, tsum=64, tie5=64, tie=64, ri=64, i7=64, j8=64, md32=256, ef=8, wc=8, x32=8,
-          colf=8, ones=64, m64=64, p256=64, tmp2=8, o0a=8, dd=64, nd=64,
-          k1=64, cm=64, sc=64, ms=8, st=8, go=8, a0=64, b0=64, hit=64, hf=64, hfs=64, hh=64, hhs=64, tks=8, thr8=8,
-          thr=256, tmp=8, base1=8, wh8=8, w0=8, wh=64, cola=8, o0=8, sw=512, jr=512, oda=64, odb=64, odc=64,
-          s1=256, k1b=64, cmb=64, scb=64, ab=64, bb=64, miss=64, bs=64, o1=8, st0=8, t32=8, csj=128, dgo=128,
-          ds=128, lt=128, eq=128, jl=128, eqj=128, cnt=128, tp=64, cr=64, lm=128, lmo=128, sel=64, dif=64, mul=64,
-          off=64, jwm=64, jws=64, frow=256, fm=256, fs=256)
-    b(F32, nb=8, jt=1024, jt2=512, od0=8, od1=8, yo=256)
+    b(BF, tbx=1024, nzx=512, wx=512, ux=512, u4=8, eb=528, ct=1024, oh=512, vt=512, vt2=512, zb=128, cmp=512,
+      c1=256, s1=256)
+    parts("bconst", BF, m16=256, md16=256, r8=64, r32=256, md32=256, io=128, io64=128, mask=128, i32r=128)
+    parts("fconst", F32, hif=8, hi8=8, h16=8, h16b=8, wr=8, pf=8, c16r=8, c2=8, corr=8, corr32=8, wt=256)
+    parts("fown", F32, ft=8, f64=8, sm=256, pos=8, ss=8, ds01=8, js=64, junk=512)
+    parts("flist", F32, xx=8, w256=8, tsum=64, tie5=64, tie=64, ri=64, ef=8, wc=8, x32=8,
+          colf=8, ones=64, p256=64, tmp2=8, o0a=8, dd=64, nd=64, nl=8, nj=8,
+          k1=64, cm=64, sc=64, ms=8, st=8, go=8, q0=64, g0=64, hit=64, hf=64, hfs=64, hh=64, hhs=64, tks=8, thr8=8,
+          thr=256, tmp=8, base1=8, wh8=8, w0=8, wh=64, cola=8, o0=8, sw=512, jr=512, ode=8, odc=8, odr=8,
+          k1b=64, cmb=64, scb=64, q1=64, g1=64, miss=64, bs=64, o1=8, st0=8, t32=8, csj=128, dgo=128,
+          ds=128, lt=128, eq=128, jl=128, eqj=128, cnt=128, tp=64, cr=64, crw=64, sel=64, zf=32,
+          off=64, jws=64, frow=256, fs=256)
+    b(F32, nb=8, jt=512, yo=256)
     parts("iconst", I32, pi=8, hx=8, ai=8, yi=8, ei=8, bi=8, l2i=16)
     parts("iarr", I32, vi=8, fiti=8, nbi=8)
     b(U16, vl=64)
     parts("lists", U16, jl4=4, in32=4, ou32=4, lrs=4, lq7=4, grs=4, gr=4, gis=4, l256=16, ofa=2, ofx=2, of=16, ofc=4,
-          ofj=4, l1=2, jw=4, fl=16)
-    q(uq=128, tq=256, nq=192, wq=128, eh=512, cq=384, oq=128, sp=64, land=256, cd=128, xw=192, xs=32, cw=512,
-      sl=256, sb=256, cc=64, cd2=128, fw=448, oq2=256, hq=256)
+          ofj=4, pl=4, jw=4, fl=16)
+    q(uq=128, tq=256, nq=128, wq=128, eh=512, cq=256, oq=128, sp=64, land=256, cd=128, xw=192, xs=32, cw=512,
+      sl=256, sb=256, cc=128, np=128, fw=448, oq2=256, hq=256)
     SCRATCH["dv"] = ("psum", [128, 2048], F32)
     SCRATCH["pp"] = ("psum", [128, 2048], F32)
 
 
 _bufs()
 SEMAPHORES = ["cv", "cs", "ct_", "cg", "lo", "a_v", "a_c", "a_s", "b_c", "b_s", "c_c", "c_s", "s_c", "s_s", "h_c",
-              "h_s"] + ["d%d" % i for i in range(40)]
+              "h_s"] + ["d%d" % i for i in range(48)]
 
 
 def find_helpers(T, topo):
@@ -265,69 +265,74 @@ def rank_program(g, core, T, topo):
         ready("g", [src])
         sent[0] += same_to_all(g, T, topo, [(far, out), (near, inn)], src["v"], dst["v"], T.sem[sem])
 
-    def c(n, k=0):
-        return ap(n, k, k + 1)
+    def c(n, k=0, p=None):
+        return ap(n, k, k + 1, p=p)
 
     def iota(n, k, pat, base=0, cm=0):
         o, small = ap(n, 0, k), SCRATCH[PART[n][0]][2] != I32
         kw = {"allow_small_or_imprecise_dtypes": True} if small else {}
         run("g", lambda q: q.iota(o["v"], pat, base, cm, **kw), [o], [])
 
-    def asel(n, i, op, fl):
-        o, x = ap(n, 0, 128), ap(i, 0, 128)
-        run("g", lambda q: q.affine_select(o["v"], x["v"], [[-1, 128]], op, fl, 0, 1), [o], [x])
+    def wrap(s, row, w):
+        scan(ap(s, 0, w), ap("wt", 0, w), row, A.add, A.max)
+
+    def listed(lst, s, w, corr="corr", a=0):
+        ts(ap(lst, a // 16, w // 16), ap(s, a + 15, w, 16), c(corr), A.add)
 
     load("s", "u4", 0, 4, T.u[:, 0:4])
-    load("y", "tbx", 0, 1024, T.tb[:, 0:1024])
+    load("y", "tbx", 0, 512, T.tb[:, 0:512])
+    load("s", "tbx", 512, 1024, T.tb[:, 512:1024])
     load("y", "nzx", 0, 256, T.nz[:, 0:256])
     load("y", "wx", 0, 512, T.w[:, 0:512])
     iota("pi", 4, [[0, 4]], 0, 1)
     iota("c16r", 4, [[16, 4]])
-    iota("c2", 4, [[2, 4]])
-    fill(ap("zf", 0, 128), 0.0)
-    fill(ap("sx", 0, 128), 16.0)
-    fill(ap("hb", 0, 128), 0.5)
-    asel("f0", "zf", A.is_gt, 1e29)
-    iota("io64", 64, [[1, 64]])
+    iota("io", 128, [[1, 128]])
+    iota("io64", 128, [[0, 2], [1, 64]])
     iota("md16", 256, [[0, 16], [1, 16]])
-    asel("idn", "hb", A.is_equal, 0.0)
-    iota("ri", 64, [[0, 8], [1, 8]])
-    iota("tsum", 64, [[1, 8], [1, 8]])
+    zb = ap("zb", 0, 128)
+    fill(zb, 0.0)
+    fill(ap("ct", 512, 1024), 0.0)
     pi, ai, yi = ap("pi", 0, 4), ap("ai", 0, 4), ap("yi", 0, 4)
-    ts(c("hx"), c("pi"), 4, A.logical_shift_right)
     ts(ai, pi, 15, A.bitwise_and)
+    ts(c("hx"), c("pi"), 4, A.logical_shift_right)
     ts(yi, pi, 7, A.bitwise_and)
-    ts(c("ei"), c("pi"), 31, A.bitwise_and)
+    tt(c("h16"), c("pi"), c("ai"), A.subtract)
     cp(c("hif"), c("hx"))
     tt(ap("wr", 0, 4), ai, ap("c16r", 0, 4), A.add)
-    ts(ap("bi", 0, 4), ai, 3, A.logical_shift_right)
-    hi, lo, zf, sx = c("hif"), c("wr"), ap("zf", 0, 128), ap("sx", 0, 128)
-
-    def digit(k, t, in_, **kw):
-        act(ap("ct", 512 * k + t, 512 * k + 512, 4), in_, **kw)
-    digit(0, 0, sx, scale=hi)
-    digit(0, 1, sx, scale=hi, bias=128.0)
-    for t in (0, 1):
-        digit(1, t, zf, bias=lo)
-        for k in (0, 1):
-            digit(k, t + 2, zf)
-    for t in range(4):
-        act(ap("ux", t, 512, 4), zf, bias=c("u4", t))
-    digit(2, 0, zf, bias=hi)
-    digit(2, 1, sx, scale=0.5, bias=hi)
-    for t in (2, 3):
-        digit(2, t, zf, bias=lo)
-    act(ap("r16", 0, 256), ap("md16", 0, 256), F.Sign)
-    fill(ap("oh", 0, 512), 0.0)
+    cp(c("pf"), c("pi"))
+    ts(c("h16b"), c("h16"), 128.0, A.add)
+    ts(c("hi8"), c("hif"), 8.0, A.add)
+    hi, lo = c("hif"), c("wr")
+    for t, col in ((0, c("h16")), (1, c("h16b")), (2, lo), (3, lo)):
+        act(ap("ct", t, 512, 4), zb, bias=col)
+    act(c("ct", 512), c("zb"), bias=hi)
+    act(c("ct", 513), c("zb"), bias=c("hi8"))
+    act(ap("ct", 518, 520), ap("zb", 0, 2), bias=lo)
+    fill(ap("eb", 0, 528), 0.0)
+    o = ap("eb", 0, 516)
+    run("g", lambda q: q.affine_select(o["v"], o["v"], [[-1, 516]], A.not_equal, 0.5, 3, 4), [o], [o])
+    ts(ap("mask", 0, 128), ap("io", 0, 128), c("pf"), A.is_lt)
+    ts(c("corr"), lo, 512.0, A.mult, -7680.0, A.add)
     ts(ap("m16", 0, 256), ap("md16", 0, 256), lo, A.is_equal)
-    fill(ap("eb", 0, 2048), 0.0)
+    for t in (0, 1, 2, 3):
+        if t < 2:
+            act(ap("ux", t, 512, 4), zb, bias=c("u4", t))
+        else:
+            ts(ap("ux", t, 512, 4), zb, c("u4", t), A.add)
+    fill(ap("vt", 128, 512), 0.0)
+    fill(ap("nzx", 256, 512), 0.0)
+    fill(ap("zf", 0, 32), 0.0)
+    act(ap("wt", 0, 256), ap("m16", 0, 256), scale=-1000512.0, bias=512.0)
     quant("uq", 0, 128, "ux")
 
-    quant("tq", 0, 256, "tbx")
     P0, P1, P2, P3 = 0, 512, 1024, 1536
-    mm(ap("pp", P0, P0 + 256), "uq", 0, "tq", 0, 256)
+    quant("tq", 0, 128, "tbx")
     mm(ap("pp", P1, P1 + 128), "tq", 0, "uq", 0, 128)
+    mm(ap("pp", P0, P0 + 128), "uq", 0, "tq", 0, 128)
+    quant("tq", 128, 256, "tbx", 512)
     mm(ap("pp", P2, P2 + 128), "tq", 128, "uq", 0, 128)
+    mm(ap("pp", P3, P3 + 128), "uq", 0, "tq", 128, 256)
+    mm(ap("dv", 0, 256), "uq", 0, "tq", 0, 256)
     rid, pid, _ = topo.addr(helpers[me])
 
     def to_helper(n, o, sem):
@@ -335,92 +340,69 @@ def rank_program(g, core, T, topo):
         g.remote_dma(o["v"], n["v"], T.sem[sem], T.sem.lo, pid, rid, bits(out))
         sent[0] += len(out)
     to_helper(ap("tq", 0, 256, bc=u8), ap("hq", 0, 256, bc=u8), "h_c")
-    quant("cq", 0, 384, "ct")
-    s0, s1 = c("pp", P1), c("pp", P2)
-    low, high, row = ap("pp", P0, P0 + 128), ap("pp", P0 + 128, P0 + 256), ap("pp", P0, P0 + 256)
-    ts(ap("sm", 0, 128), ap("f0", 0, 128), s0, A.add)
-    ts(ap("sm", 128, 256), ap("f0", 0, 128), s1, A.add)
-    ts(ap("cmp", 384, 512), low, s1, A.is_le)
-    ts(ap("cmp", 512, 640), high, s1, A.is_lt)
-    act(ap("junk", 384, 640), ap("cmp", 384, 640), accum=c("pos", 1))
-    ts(ap("cmp", 0, 256), row, s0, A.is_lt)
-    tt(ap("cmp", 256, 384), low, ap("sm", 0, 128), A.is_equal)
-    act(ap("junk", 0, 384), ap("cmp", 0, 384), accum=c("pos", 0))
-    tt(ap("cmp", 640, 768), high, ap("sm", 128, 256), A.is_equal)
-    ts(ap("gt", 0, 256), row, 0.0, A.is_gt)
-    act(ap("junk", 640, 896), ap("gt", 0, 256), accum=c("ft"))
-    red(c("pos", 4), ap("cmp", 640, 768))
-    for t, e in ((1, 256), (259, 512)):
-        ts(ap("oh", t, e, 4), ap("io64", 0, 64), c("pos", 1), A.subtract, c("pos", 4), A.is_equal)
-    for t, e in ((0, 256), (258, 512)):
-        ts(ap("oh", t, e, 4), ap("io64", 0, 64), c("pos", 0), A.is_equal)
+    low, high = ap("pp", P0, P0 + 128), ap("pp", P3, P3 + 128)
+    s0, s1 = c("ss", 0), c("ss", 1)
+    for h, pk in ((0, P1), (1, P2)):
+        act(c("ss", h), c("pp", pk))
+        act(c("ds01", h), c("pp", pk), F.Abs, bias=2.0 ** -120, scale=0.7 * 2.0 ** -23)
+        act(ap("sm", 128 * h, 128 * h + 128), ap("mask", 0, 128), bias=c("ss", h), scale=c("ds01", h))
+    quant("cq", 0, 256, "ct")
+    tt(ap("cmp", 0, 128), low, ap("sm", 0, 128), A.is_lt)
+    ts(ap("cmp", 128, 256), high, s0, A.is_lt)
+    act(ap("junk", 0, 256), ap("cmp", 0, 256), accum=c("pos", 0))
+    ts(ap("cmp", 256, 384), low, s1, A.is_le)
+    tt(ap("cmp", 384, 512), high, ap("sm", 128, 256), A.is_lt)
+    act(ap("junk", 256, 512), ap("dv", 0, 256), F.Sign, bias=-2.0 ** -100, accum=c("ft"))
+    act(c("f64"), c("ft"), scale=32.0, bias=8192.0)
+    red(c("pos", 1), ap("cmp", 256, 512))
+    for t in (0, 2, 1, 3):
+        ts(ap("oh", t, 512, 4), ap("io64", 0, 128), c("pos", t % 2), A.is_equal)
     quant("oq", 0, 128, "oh")
-    mm(ap("pp", P3, P3 + 128), "cq", 0, "oq", 0, 128, True, False)
-    mm(ap("pp", P3, P3 + 128), "cq", 128, "oq", 0, 128, False, True)
-    mm(ap("pp", P1, P1 + 128), "oq", 0, "cq", 256, 384)
+    mm(ap("pp", P0, P0 + 128), "cq", 0, "oq", 0, 128)
+    mm(ap("dv", 512, 640), "oq", 0, "cq", 128, 256)
+    iota("tsum", 64, [[1, 8], [1, 8]])
+    iota("ri", 64, [[0, 8], [1, 8]])
+    iota("c2", 4, [[2, 4]])
+    ts(ap("bi", 0, 4), ai, 3, A.logical_shift_right)
+    cp(ap("lq7", 0, 4), yi)
+    ts(ap("gis", 0, 4), yi, -8.0, A.mult, 63.0, A.add)
+    ts(ap("in32", 0, 4), yi, 32.0, A.mult, 31.0, A.add)
+    act(ap("r8", 0, 64), ap("ri", 0, 64), F.Sign)
+    wrap("js", ap("pp", P0, P0 + 64), 64)
+    for k, p in ((0, (0, 64)), (1, (64, 128))):
+        ts(ap("vl", 8 * slot, 8 * slot + 1, p=p), c("dv", 512 + k, p), c("f64", 0, p), A.add)
+    listed("jl4", "js", 32)
+    xx = ap("xx", 0, 4)
+    tt(xx, ap("bi", 0, 4), ap("c2", 0, 4), A.add)
+    pick("sp", 0, 32, "tq", 0, 256, "jl4", 0, 2)
+    listed("jl4", "js", 64, a=32)
 
-    def wrap1(m, row, w):
-        tt(ap(m, 0, w), row, ap("m16", 0, w), A.mult)
-
-    def wrap2(s, m, w):
-        scan(ap(s, 0, w), ap("r16", 0, w), ap(m, 0, w))
-
-    def wrap3(lst, s, w):
-        cp(ap(lst, 0, w // 16), ap(s, 15, w, 16))
-    wrap1("jm", ap("pp", P3, P3 + 64), 64)
     v = c("vl", 8 * slot)
-    ts(v, c("ft"), 64.0, A.mult, c("pp", P1), A.add)
-    wrap2("js", "jm", 64)
-    wrap3("jl4", "js", 64)
-    pick("sp", 0, 64, "tq", 0, 256, "jl4", 0, 4)
-
     to_all(v, v, "a_v")
     to_all(ap("sp", 0, 32, bc=u8), ap("land", 32 * slot, 32 * slot + 32, bc=u8), "a_c")
     to_all(ap("sps", 0, 32), ap("lands", 32 * slot, 32 * slot + 32), "a_s")
     to_helper(ap("tqs", 0, 256), ap("hqs", 0, 256), "h_s")
     move("land", 32 * slot, "sp", 0, 32)
     move("cd", 0, "tq", 0, 128)
-    move("xw", 128, "sp", 0, 64)
-    move("cd2", 0, "tq", 0, 128)
-    move("sl", 32 * slot, "tq", 32 * me, 32)
 
-    for b in range(4):
-        act(ap("eb", 512 * b + b, 512 * b + 512, 4), ap("idn", 0, 128))
-    act(ap("r8", 0, 64), ap("ri", 0, 64), F.Sign)
-    xx = ap("xx", 0, 4)
-    tt(xx, ap("bi", 0, 4), ap("c2", 0, 4), A.add)
     ts(ap("tie5", 0, 64), ap("tsum", 0, 64), 7.5, A.is_gt, -1.0, A.mult)
-    cp(ap("lq7", 0, 4), yi)
     ts(ap("lrs", 0, 4), xx, -1.0, A.mult, 7.0, A.add)
+    pick("sp", 32, 64, "tq", 0, 256, "jl4", 2, 4)
+    move("xw", 128, "sp", 0, 64)
+    move("sl", 32 * slot, "tq", 32 * me, 32)
     ts(ap("tie", 0, 64), ap("tie5", 0, 64), 0.5, A.add, 64.0, A.mult)
-    fill(ap("nzx", 256, 768), 0.0)
-    fill(ap("vt", 128, 512), 0.0)
-    quant("eh", 0, 512, "eb")
-    quant("nq", 0, 192, "nzx")
-
-    def noise(t):
-        for b in range(4):
-            mm(ap("dv", 512 * b, 512 * b + 128), "eh", 128 * b, "nq", 32 * t, 32 * t + 128, True, False)
-    noise(0)
-    fill(ap("wc", 0, 8), 32.0)
-    ts(ap("tie5", 0, 64), ap("tie5", 0, 64), 0.5, A.add)
-    ts(ap("gis", 0, 4), yi, -8.0, A.mult, 63.0, A.add)
-    ts(ap("grs", 0, 4), xx, -8.0, A.mult, 63.0, A.add)
-    ts(ap("gr", 0, 4), xx, 8.0, A.mult, 7.0, A.add)
-    ts(ap("in32", 0, 4), yi, 32.0, A.mult, 31.0, A.add)
-    ts(ap("ou32", 0, 4), xx, -32.0, A.mult, 255.0, A.add)
-    fill(ap("ones", 0, 64), 1.0)
+    for b in range(4):
+        quant("eh", 128 * b, 128 * b + 128, "eb", 3 - b)
+    quant("nq", 0, 128, "nzx")
+    for b in range(4):
+        mm(ap("dv", 512 * b, 512 * b + 128), "eh", 128 * b, "nq", 0, 128, True, False)
     ts(c("colf"), hi, 3.5, A.is_lt, 15.0, A.mult)
-    ts(ap("w256", 0, 4), ap("wr", 0, 4), 256.0, A.mult)
+    fill(ap("wc", 0, 8), 32.0)
+    ts(ap("grs", 0, 4), xx, -8.0, A.mult, 63.0, A.add)
     ts(c("colf", 1), c("colf"), 1.0, A.add)
-    fill(ap("vt2", 128, 512), 0.0)
-    fill(ap("wh8", 0, 16), 0.0)
     iota("l2i", 16, [[1, 8], [0, 2]])
-    iota("j8", 64, [[1, 8], [0, 8]])
-    iota("i7", 64, [[0, 8], [-1, 8]], 7)
     iota("md32", 256, [[0, 8], [1, 32]])
     iota("x32", 8, [[32, 8]], 256)
-    iota("m64", 64, [[-1, 64]], 64)
     iota("p256", 64, [[1, 64]], 256)
     iota("frow", 256, [[1, 256]])
     act(ap("r32", 0, 256), ap("md32", 0, 256), F.Sign)
@@ -432,88 +414,99 @@ def rank_program(g, core, T, topo):
         arrive("land", k[0], k[1], ("a_c", n8))
         arrive("lands", k[0], k[1], ("a_s", n8))
     cp(ap("vi", 0, 8), ap("vl", 0, 64, 8))
+    ts(ap("ou32", 0, 4), xx, -32.0, A.mult, 255.0, A.add)
     lq7, lrs, r8 = ap("lq7", 0, 4), ap("lrs", 0, 4), ap("r8", 0, 64)
     tt(ap("k1", 0, 64), ap("vi", 0, 8, off=lrs), ap("tie", 0, 64), A.add)
+    ts(ap("nbi", 0, 8), ap("vi", 0, 8), 15, A.bitwise_and)
     tt(ap("cm", 0, 64), ap("vi", 0, 8, off=lq7), ap("k1", 0, 64), A.is_gt)
+    ts(ap("nb", 0, 8), ap("nbi", 0, 8), c("colf", 1), A.mult)
     scan(ap("sc", 0, 64), r8, ap("cm", 0, 64))
+    i = ap("nb", 0, 8, p=(64, 128))
+    o = ap("nl", 0, 8, p=(0, 64))
+    dma("y", o["v"], i["v"], [o], [i])
+    ts(ap("fiti", 0, 8), ap("vi", 0, 8), 6, A.logical_shift_right)
     mine = c("sc", 8 * me + 7)
     ts(ap("ms", 0, 8), ap("sc", 7, 64, 8), mine, A.add, 7.0, A.not_equal)
-    scan(ap("st", 0, 8), ap("wc", 0, 8), ap("ms", 0, 8), A.add, A.mult)
-    ts(ap("ofa", 0, 2), ap("wr", 0, 2), c("st", 7), A.add)
-    pick("cd", 0, 32, "land", 0, 256, "ofa", 0, 2)
-
-    def products(cd):
-        for b in range(4):
-            mm(ap("dv", 512 * b, 512 * b + 128), "eh", 128 * b, cd, 0, 128, False, True)
-
-    def packed(vt, out, a):
-        for b in (0, 2, 1, 3):
-            o, i = ap(vt, b, 128, 4), ap("dv", 512 * b, 512 * b + 32)
-            if b < 2:
-                act(o, i)
-            else:
-                cp(o, i)
-        quant(out, a, a + 128, vt)
-    products("cd")
     ts(c("go"), mine, 3.5, A.is_lt, 160.0, A.mult)
-    ts(ap("fiti", 0, 8), ap("vi", 0, 8), 6, A.logical_shift_right)
+    scan(ap("st", 0, 8), ap("wc", 0, 8), ap("ms", 0, 8), A.add, A.mult)
     ts(ap("ofx", 0, 2), ap("wr", 0, 2), c("go"), A.add)
-    ts(ap("nbi", 0, 8), ap("vi", 0, 8), 15, A.bitwise_and)
-    packed("vt", "xw", 0)
+    ts(ap("ofa", 0, 2), ap("wr", 0, 2), c("st", 7), A.add)
+    gi, grs = ap("gis", 0, 4), ap("grs", 0, 4)
+    act(ap("q0", 0, 64), ap("sc", 0, 64, off=grs), F.Abs, bias=-3.5)
+    pick("cd", 0, 32, "land", 0, 256, "ofa", 0, 2)
+    for b in range(4):
+        mm(ap("dv", 512 * b, 512 * b + 128), "eh", 128 * b, "cd", 0, 128, False, True)
+
+    def packed(vt, w, out, a):
+        for b in (0, 1, 2, 3):
+            o, i = ap(vt, b, 4 * w, 4), ap("dv", 512 * b, 512 * b + w)
+            if b % 2:
+                cp(o, i)
+            else:
+                act(o, i)
+        quant(out, a, a + 128, vt)
+    ts(ap("g0", 0, 64), ap("sc", 0, 64, off=gi), -1.0, A.mult, 3.5, A.add)
+    ts(ap("tie5", 0, 64), ap("tie5", 0, 64), 0.5, A.add)
+    ts(ap("gr", 0, 4), xx, 8.0, A.mult, 7.0, A.add)
+    tt(ap("hit", 0, 64), ap("g0", 0, 64), ap("q0", 0, 64), A.is_equal)
+    ts(ap("tks", 0, 8), ap("g0", 0, 8), 0.0, A.is_lt)
+    tt(ap("hf", 0, 64), ap("fiti", 0, 8, off=lq7), ap("hit", 0, 64), A.mult)
+    tt(ap("hh", 0, 64), ap("hit", 0, 64), ap("ri", 0, 64), A.mult)
+    packed("vt", 32, "xw", 0)
+    ts(ap("thr8", 0, 8), ap("tks", 0, 8), -1e29, A.mult, 1e29, A.add)
     pick("xs", 0, 32, "xw", 0, 192, "ofx", 0, 2)
 
     to_all(ap("xs", 0, 32, bc=u8), ap("cw", 32 * slot, 32 * slot + 32, bc=u8), "b_c")
     to_all(ap("xss", 0, 32), ap("cws", 32 * slot, 32 * slot + 32), "b_s")
     move("cw", 32 * slot, "xs", 0, 32)
 
-    gi, grs = ap("gis", 0, 4), ap("grs", 0, 4)
-    ts(ap("a0", 0, 64), ap("sc", 0, 64, off=grs), -1.0, A.mult, 7.0, A.add)
-    ts(ap("nb", 0, 8), ap("nbi", 0, 8), c("colf", 1), A.mult)
-    o, i = ap("jt", 0, 1024, p=(0, 1)), ap("nb", 0, 8)
-    dma("y", o["v"], i["v"], [o], [i])
+    nj = ap("nj", 0, 8, p=(0, 64))
+    tt(nj, ap("nb", 0, 8, p=(0, 64)), ap("nl", 0, 8, p=(0, 64)), A.add)
+    o = ap("jt", 0, 512, p=(0, 1))
+    dma("y", o["v"], nj["v"], [o], [nj])
+    jr = ap("jr", 0, 512)
+    run("g", lambda q: q.partition_broadcast(jr["v"], o["v"], 128), [jr], [o])
     move("cw", 256, "land", 0, 256)
-    tt(ap("b0", 0, 64), ap("sc", 0, 64, off=grs), ap("a0", 0, 64), A.min)
-    ts(ap("tks", 0, 8), ap("a0", 0, 64, 8), 3.5, A.is_lt)
-    tt(ap("hit", 0, 64), ap("sc", 0, 64, off=gi), ap("b0", 0, 64), A.is_equal)
-    ts(ap("thr8", 0, 8), ap("tks", 0, 8), -1e29, A.mult, 1e29, A.add)
-    tt(ap("hf", 0, 64), ap("fiti", 0, 8, off=lq7), ap("hit", 0, 64), A.mult)
-    tt(ap("hh", 0, 64), ap("hit", 0, 64), ap("ri", 0, 64), A.mult)
+    move("cc", 64, "tq", 0, 64)
+    move("np", 64, "nq", 64, 64)
     scan(ap("hfs", 0, 64), r8, ap("hf", 0, 64))
     scan(ap("hhs", 0, 64), r8, ap("hh", 0, 64))
+    cp(ap("l256", 0, 16), ap("l2i", 0, 16))
+    act(ap("thr", 0, 256), ap("thr8", 0, 8, off=ap("l256", 0, 16)))
     fh = ap("hfs", 7, 64, 8)
     ts(ap("tmp", 0, 8), fh, -224.0, A.add, 0.0, A.max)
+    fill(ap("wh8", 0, 1), 0.0)
+    fill(ap("w0", 0, 1), 0.0)
     tt(ap("wh8", 1, 8), ap("hhs", 7, 56, 8), ap("hhs", 15, 64, 8), A.subtract)
     tt(ap("tmp2", 0, 8), ap("tmp", 0, 8), ap("tks", 0, 8), A.mult)
+    ts(ap("o0a", 0, 8), ap("tks", 0, 8), -256.0, A.mult)
     ts(ap("wh", 0, 64), ap("wh8", 0, 8, off=lq7), 32.0, A.mult)
     tt(ap("base1", 0, 8), fh, ap("tmp2", 0, 8), A.subtract)
     ts(c("cola", 0), c("hhs", 63), 32.0, A.mult, c("wr", 0), A.add)
     ts(c("cola", 1), c("hhs", 63), 32.0, A.mult, c("wr", 1), A.add)
     tt(ap("dd", 0, 64), ap("base1", 0, 8, off=lrs), ap("tie5", 0, 64), A.add)
-    cp(ap("l256", 0, 16), ap("l2i", 0, 16))
     ts(c("cola", 2), c("hhs", 63), 32.0, A.mult)
+    tt(ap("o0", 0, 8), ap("o0a", 0, 8), ap("x32", 0, 8), A.add)
     tt(ap("nd", 0, 64), ap("base1", 0, 8, off=lq7), ap("dd", 0, 64), A.subtract)
-    cp(ap("thr", 0, 256), ap("thr8", 0, 8, off=ap("l256", 0, 16)))
     mm(ap("pp", P1, P1 + 256), "uq", 0, "land", 0, 256)
     act(ap("sw", 256, 512), ap("pp", P1, P1 + 256))
-    ts(ap("o0a", 0, 8), ap("tks", 0, 8), -256.0, A.mult)
-    cp(c("ef"), c("ei"))
-    tt(ap("o0", 0, 8), ap("o0a", 0, 8), ap("x32", 0, 8), A.add)
-    quant("wq", 0, 128, "wx")
+    ts(c("ei"), c("pi"), 31, A.bitwise_and)
     tt(ap("w0", 1, 8), ap("o0", 0, 7), ap("o0", 1, 8), A.subtract)
+    fill(ap("ones", 0, 64), 1.0)
+    cp(c("ef"), c("ei"))
+    ts(ap("w256", 0, 4), ap("wr", 0, 4), 256.0, A.mult)
+    ts(c("corr32"), c("corr"), 32.0, A.add)
     ts(ap("i32r", 0, 128), ap("md32", 0, 128), c("ef"), A.is_equal)
-    j1, j2, j3 = ap("jt", 0, 512, p=(0, 1)), ap("jt", 512, 1024, p=(0, 1)), ap("jt2", 0, 512, p=(0, 1))
-    tt(j3, j1, j2, A.add)
-    jr = ap("jr", 0, 512)
-    run("g", lambda q: q.partition_broadcast(jr["v"], j3["v"], 128), [jr], [j3])
+    quant("wq", 0, 128, "wx")
+    fill(ap("vt2", 256, 512), 0.0)
 
-    def order_out(sc, row, t):
-        tt(ap("oda", 0, 64), ap(sc, 0, 64, off=gi), ap("j8", 0, 64), A.is_equal)
-        tt(ap("odb", 0, 64), ap("oda", 0, 64), ap("i7", 0, 64), A.mult)
-        scan(ap("odc", 0, 64), r8, ap("odb", 0, 64))
-        cp(ap(row, 0, 8), ap("odc", 7, 64, 8))
-        x = ap(row, 0, 8, p=(0, 1))
+    def order_out(sc, t):
+        ts(ap("ode", 0, 8), ap(sc, 7, 64, 8), c("pf"), A.not_equal)
+        scan(ap("odc", 0, 8), ap("ones", 0, 8), ap("ode", 0, 8), A.add, A.mult)
+        act(c("odr", t), c("odc", 7), scale=-1.0, bias=7.0)
+        x = ap("odr", t, t + 1, p=(0, 8))
         dma("y", T.od[t:t + 1, 0:8], x["v"], [], [x])
-    order_out("sc", "od0", 0)
+    order_out("sc", 0)
 
     for k in ((0, 32 * slot), (32 * slot + 32, 256)):
         arrive("cw", k[0], k[1], ("b_c", n8))
@@ -521,21 +514,21 @@ def rank_program(g, core, T, topo):
         arrive("sl", k[0], k[1], ("s_c", 7))
         arrive("sls", k[0], k[1], ("s_s", 7))
     mm(ap("pp", P0, P0 + 256), "uq", 0, "cw", 0, 256)
-    noise(1)
     tt(ap("c1", 0, 256), ap("pp", P0, P0 + 256), ap("thr", 0, 256), A.is_gt)
     scan(ap("s1", 0, 256), ap("r32", 0, 256), ap("c1", 0, 256))
     tt(ap("k1b", 0, 64), ap("s1", 0, 256, off=ap("in32", 0, 4)), ap("nd", 0, 64), A.add)
     tt(ap("cmb", 0, 64), ap("s1", 0, 256, off=ap("ou32", 0, 4)), ap("k1b", 0, 64), A.is_lt)
     scan(ap("scb", 0, 64), r8, ap("cmb", 0, 64))
-    gr = ap("gr", 0, 4)
-    ts(ap("ab", 0, 64), ap("scb", 0, 64, off=gr), -1.0, A.mult, 7.0, A.add)
-    tt(ap("bb", 0, 64), ap("scb", 0, 64, off=gr), ap("ab", 0, 64), A.min)
-    tt(ap("miss", 0, 64), ap("scb", 0, 64, off=gi), ap("bb", 0, 64), A.not_equal)
+    act(ap("q1", 0, 64), ap("scb", 0, 64, off=ap("gr", 0, 4)), F.Abs, bias=-3.5)
+    ts(ap("g1", 0, 64), ap("scb", 0, 64, off=gi), -1.0, A.mult, 3.5, A.add)
+    tt(ap("miss", 0, 64), ap("g1", 0, 64), ap("q1", 0, 64), A.not_equal)
+    ts(c("t32"), c("scb", 8 * me + 7), 3.5, A.is_gt, 32.0, A.mult)
     scan(ap("bs", 0, 64), ap("wh", 0, 64), ap("miss", 0, 64), A.add, A.mult)
-    ts(ap("of", 0, 16, 2), ap("bs", 7, 64, 8), c("cola", 0), A.add)
-    ts(ap("of", 1, 16, 2), ap("bs", 7, 64, 8), c("cola", 1), A.add)
+    scan(ap("st0", 0, 8), ap("w0", 0, 8), ap("miss", 8 * me, 8 * me + 8), A.add, A.mult)
     mh = 4 * (me // 4)
     halves = (4 - mh, mh)
+    ts(ap("of", 0, 16, 2), ap("bs", 7, 64, 8), c("cola", 0), A.add)
+    ts(ap("of", 1, 16, 2), ap("bs", 7, 64, 8), c("cola", 1), A.add)
     for r0 in halves:
         pick("sb", 32 * r0, 32 * r0 + 128, "sl", 0, 256, "of", 2 * r0, 2 * r0 + 8)
 
@@ -552,18 +545,20 @@ def rank_program(g, core, T, topo):
 
     act(ap("sw", 0, 256), ap("pp", P0, P0 + 256))
     tt(c("o1"), c("bs", 8 * me + 7), c("cola", 2), A.add)
-    scan(ap("st0", 0, 8), ap("w0", 0, 8), ap("miss", 8 * me, 8 * me + 8), A.add, A.mult)
+    ts(ap("ofc", 0, 2), ap("wr", 0, 2), c("st0", 7), A.add, c("o0", 7), A.add)
     ts(ap("ofj", 0, 4), ap("w256", 0, 4), c("o1"), A.add, 1.0 / 32, A.mult)
     ts(ap("ofc", 2, 4), ap("wr", 0, 2), c("o1"), A.add)
-    ts(ap("ofc", 0, 2), ap("wr", 0, 2), c("st0", 7), A.add, c("o0", 7), A.add)
     cs, cj, cr, tp = ap("csj", 0, 64), ap("csj", 64, 128), ap("cr", 0, 64), ap("tp", 0, 64)
     cp(cj, ap("jr", 0, 512, off=ap("ofj", 0, 4)))
     cp(cs, ap("sw", 0, 512, off=ap("ofc", 0, 4)))
-    ts(c("t32"), c("scb", 8 * me + 7), 3.5, A.is_gt, 32.0, A.mult)
-    tt(ap("dgo", 0, 128), ap("csj", 0, 128), ap("i32r", 0, 128), A.mult)
-    pick("cc", 0, 64, "cw", 0, 512, "ofc", 0, 4)
+    tt(ap("dgo", 64, 128), cj, ap("i32r", 64, 128), A.mult)
+    tt(ap("dgo", 0, 64), cs, ap("i32r", 0, 64), A.mult)
+    wrap("jws", cj, 64)
     scan(ap("ds", 0, 128), ap("r32", 0, 128), ap("dgo", 0, 128))
-    pick("fw", 256, 320, "cw", 0, 512, "ofc", 0, 4)
+    pick("cc", 0, 64, "cw", 0, 512, "ofc", 0, 4)
+    move("fw", 256, "cc", 0, 64)
+    for b in range(4):
+        mm(ap("dv", 512 * b, 512 * b + 128), "eh", 128 * b, "cc", 0, 128, True, False)
     two = [(e, (64 * e, 64 * e + 64)) for e in (0, 1)]
     for e, w in two:
         ts(ap("eq", *w), cs, c("ds", 32 * e + 31), A.is_equal)
@@ -571,31 +566,24 @@ def rank_program(g, core, T, topo):
     for e, w in two:
         ts(ap("lt", *w), cs, c("ds", 32 * e + 31), A.is_lt)
         tt(ap("eqj", *w), ap("eq", *w), ap("jl", *w), A.mult)
-    wrap1("jwm", cj, 64)
+    listed("jw", "jws", 64)
     for e, w in two:
         scan(ap("cnt", *w), ap("lt", *w), ap("eqj", *w), A.add, A.add)
     for e, w in two:
         ts(ap("tp", 32 * e, 32 * e + 32), ap("zf", 0, 32), c("cnt", 64 * e + 63), A.add)
-    wrap2("jws", "jwm", 64)
     run("v", lambda q: q.transpose(cr["v"], tp["v"]), [cr], [tp])
-    wrap3("jw", "jws", 64)
-    for e, w in two:
-        ts(ap("lm", *w), cr, c("wr", e), A.not_equal)
-    ts(ap("sel", 0, 64), cr, c("t32"), A.is_lt)
-    for e, w in two:
-        scan(ap("lmo", *w), ap("ones", 0, 64), ap("lm", *w), A.add, A.mult)
-    tt(ap("dif", 0, 64), cr, ap("m64", 0, 64), A.add)
-    for e, w in two:
-        ts(c("l1", e), c("lmo", 64 * e + 63), -1.0, A.mult, 63.0, A.add)
-    tt(ap("mul", 0, 64), ap("dif", 0, 64), ap("sel", 0, 64), A.mult)
-    pick("cd2", 0, 32, "cc", 0, 64, "l1", 0, 2)
-    products("cd2")
-    tt(ap("off", 0, 64), ap("mul", 0, 64), ap("p256", 0, 64), A.add)
+    wrap("crw", cr, 64)
+    ts(ap("sel", 0, 64), cr, c("t32"), A.is_lt, 64.0, A.mult)
+    listed("pl", "crw", 64, "corr32")
+    tt(ap("off", 0, 64), ap("sel", 0, 64), ap("p256", 0, 64), A.add)
+    pick("np", 0, 64, "nq", 0, 128, "pl", 0, 4)
+    for b in range(4):
+        mm(ap("dv", 512 * b, 512 * b + 128), "eh", 128 * b, "np", 0, 128, False, True)
     cp(ap("frow", 0, 256, off=ap("jw", 0, 4)), ap("off", 0, 64))
-    wrap1("fm", ap("frow", 0, 256), 256)
-    packed("vt2", "fw", 320)
-    wrap2("fs", "fm", 256)
-    wrap3("fl", "fs", 256)
+    packed("vt2", 64, "fw", 320)
+    wrap("fs", ap("frow", 0, 256), 256)
+    order_out("scb", 1)
+    listed("fl", "fs", 256)
 
     for k in ((0, 32 * me), (32 * me + 32, 256)):
         arrive("fw", k[0], k[1], ("c_c", n3))
@@ -605,13 +593,13 @@ def rank_program(g, core, T, topo):
         mm(ap("pp", pk, pk + 128), "wq", 0, "oq2", 128 * k, 128 * k + 128)
     x = ap("oq2", 0, 256, bc=u8)
     dma("y", T.oc[:, 0:1024], x["v"], [], [x])
-    order_out("scb", "od1", 1)
     for k in range(4):
         x = ap("oq2s", 0, 256, p=(32 * k, 32 * k + 4))
-        dma("s" if k % 2 else "y", T.osc[4 * k:4 * k + 4, 0:256], x["v"], [], [x])
+        dma("y", T.osc[4 * k:4 * k + 4, 0:256], x["v"], [], [x])
     act(ap("yo", 0, 128), ap("pp", P2, P2 + 128))
     cp(ap("yo", 128, 256), ap("pp", P3, P3 + 128))
-    x = ap("yo", 0, 256)
-    dma("y", T.y[:, 0:256], x["v"], [], [x])
+    for k, q in ((0, "s"), (1, "y")):
+        x = ap("yo", 128 * k, 128 * k + 128)
+        dma(q, T.y[:, 128 * k:128 * k + 128], x["v"], [], [x])
     finish()
     g.wait_ge(T.sem.lo, sent[0])

@@ -23,33 +23,32 @@ def _bufs():
         for k in kw:
             SCRATCH[k] = ("sbuf", [128, kw[k]], CODE)
             SCRATCH[k + "s"] = ("sbuf", [128, kw[k]], PLANE)
-    b(BF, tbx=1024, nzx=512, wx=512, ux=512, u4=8, eb=528, ct=1024, oh=512, vt=512, vt2=512, zb=128, cmp=512,
-      c1=256, s1=256)
+    b(BF, tbx=1024, nzx=512, wx=512, ux=512, u4=8, eb=528, ct=1024, oh=512, vt=512, vt2=512, zb=128, hb=128, idn=128,
+      lt4=512, cmp=512, c1=256, s1=256)
     parts("bconst", BF, m16=256, md16=256, r8=64, r32=256, md32=256, io=128, io64=128, mask=128, i32r=128)
     parts("fconst", F32, hif=8, hi8=8, h16=8, h16b=8, wr=8, pf=8, c16r=8, c2=8, corr=8, corr32=8, wt=256)
-    parts("fown", F32, ft=8, f64=8, sm=256, pos=8, ss=8, ds01=8, js=64, junk=512)
+    parts("fown", F32, ft=8, sm=256, pos=8, ss=8, ds01=8, js=64, junk=512)
     parts("flist", F32, xx=8, w256=8, tsum=64, tie5=64, tie=64, ri=64, ef=8, wc=8, x32=8,
-          colf=8, ones=64, p256=64, tmp2=8, o0a=8, dd=64, nd=64, nl=8, nj=8,
+          ones=64, p256=64, tmp2=8, o0a=8, dd=64, nd=64, nl=8, nh=8, nj=8,
           k1=64, cm=64, sc=64, ms=8, st=8, go=8, q0=64, g0=64, hit=64, hf=64, hfs=64, hh=64, hhs=64, tks=8, thr8=8,
           thr=256, tmp=8, base1=8, wh8=8, w0=8, wh=64, cola=8, o0=8, sw=512, jr=512, ode=8, odc=8, odr=8,
-          k1b=64, cmb=64, scb=64, q1=64, g1=64, miss=64, bs=64, o1=8, st0=8, t32=8, csj=128, dgo=128,
+          k1b=64, x1b=64, cmb=64, scb=64, q1=64, g1=64, miss=64, bs=64, o1=8, st0=8, t32=8, csj=128, dgo=128,
           ds=128, lt=128, eq=128, jl=128, eqj=128, cnt=128, tp=64, cr=64, crw=64, sel=64, zf=32,
           off=64, jws=64, frow=256, fs=256)
-    b(F32, nb=8, jt=512, yo=256)
+    b(F32, vi=8, fiti=8, jt=512, yo=256)
     parts("iconst", I32, pi=8, hx=8, ai=8, yi=8, ei=8, bi=8, l2i=16)
-    parts("iarr", I32, vi=8, fiti=8, nbi=8)
     b(U16, vl=64)
     parts("lists", U16, jl4=4, in32=4, ou32=4, lrs=4, lq7=4, grs=4, gr=4, gis=4, l256=16, ofa=2, ofx=2, of=16, ofc=4,
           ofj=4, pl=4, jw=4, fl=16)
-    q(uq=128, tq=256, nq=128, wq=128, eh=512, cq=256, oq=128, sp=64, land=256, cd=128, xw=192, xs=32, cw=512,
-      sl=256, sb=256, cc=128, np=128, fw=448, oq2=256, hq=256)
+    q(uq=128, tq=384, nq=128, wq=128, eh=512, cq=256, oq=128, sp=64, land=256, cd=128, xw=192, xs=32, cw=512,
+      sl=256, sb=256, cc=128, np=128, fw=448, oq2=256, hq=264, ll=128)
     SCRATCH["dv"] = ("psum", [128, 2048], F32)
     SCRATCH["pp"] = ("psum", [128, 2048], F32)
 
 
 _bufs()
 SEMAPHORES = ["cv", "cs", "ct_", "cg", "lo", "a_v", "a_c", "a_s", "b_c", "b_s", "c_c", "c_s", "s_c", "s_s", "h_c",
-              "h_s"] + ["d%d" % i for i in range(48)]
+              "h_s", "h_l", "l_c", "l_s"] + ["d%d" % i for i in range(48)]
 
 
 def find_helpers(T, topo):
@@ -96,13 +95,18 @@ def same_to_all(g, T, topo, to, src, dst, sem):
 
 def hand_on(g, core, T, topo, r):
     S = 32
-    c0 = S * (len(T.cores) - 1 - r)
+    c0, l0 = S * (len(T.cores) - 1 - r), 2 * (len(T.cores) - 1 - r)
     far, near, out, inn = ways(core, T, topo, r)
     to = [(s, out[i:i + 1]) for i, s in enumerate(far)] + [(s, inn[:1]) for s in near]
+    lists = [(far, out), (near, inn)]
     g.wait_ge(T.sem.h_c, len(out))
     n = one_each(g, T, topo, to, lambda s: T.hq[:, S * s:S * s + S].bitcast(dt.uint8),
                  T.sl[:, c0:c0 + S].bitcast(dt.uint8), T.sem.s_c)
+    g.wait_ge(T.sem.h_l, len(out))
+    n += same_to_all(g, T, topo, lists, T.hq[:, 256:258].bitcast(dt.uint8), T.ll[:, l0:l0 + 2].bitcast(dt.uint8),
+                     T.sem.l_c)
     g.wait_ge(T.sem.h_s, len(out))
+    n += same_to_all(g, T, topo, lists, T.hqs[:, 256:258], T.lls[:, l0:l0 + 2], T.sem.l_s)
     n += one_each(g, T, topo, to, lambda s: T.hqs[:, S * s:S * s + S], T.sls[:, c0:c0 + S], T.sem.s_s)
     g.wait_ge(T.sem.lo, n)
 
@@ -265,8 +269,8 @@ def rank_program(g, core, T, topo):
         ready("g", [src])
         sent[0] += same_to_all(g, T, topo, [(far, out), (near, inn)], src["v"], dst["v"], T.sem[sem])
 
-    def c(n, k=0, p=None):
-        return ap(n, k, k + 1, p=p)
+    def c(n, k=0):
+        return ap(n, k, k + 1)
 
     def iota(n, k, pat, base=0, cm=0):
         o, small = ap(n, 0, k), SCRATCH[PART[n][0]][2] != I32
@@ -308,21 +312,24 @@ def rank_program(g, core, T, topo):
     act(c("ct", 512), c("zb"), bias=hi)
     act(c("ct", 513), c("zb"), bias=c("hi8"))
     act(ap("ct", 518, 520), ap("zb", 0, 2), bias=lo)
+    fill(ap("hb", 0, 128), 0.5)
+    o, i = ap("idn", 0, 128), ap("hb", 0, 128)
+    run("g", lambda q: q.affine_select(o["v"], i["v"], [[-1, 128]], A.is_equal, 0.0, 0, 1), [o], [i])
     fill(ap("eb", 0, 528), 0.0)
-    o = ap("eb", 0, 516)
-    run("g", lambda q: q.affine_select(o["v"], o["v"], [[-1, 516]], A.not_equal, 0.5, 3, 4), [o], [o])
+    iota("tsum", 64, [[1, 8], [1, 8]])
+    iota("ri", 64, [[0, 8], [1, 8]])
+    iota("c2", 4, [[2, 4]])
     ts(ap("mask", 0, 128), ap("io", 0, 128), c("pf"), A.is_lt)
     ts(c("corr"), lo, 512.0, A.mult, -7680.0, A.add)
-    ts(ap("m16", 0, 256), ap("md16", 0, 256), lo, A.is_equal)
+    fill(ap("vt", 128, 512), 0.0)
+    fill(ap("nzx", 256, 512), 0.0)
+    fill(ap("zf", 0, 32), 0.5)
+    fill(ap("lt4", 0, 512), 0.0)
     for t in (0, 1, 2, 3):
         if t < 2:
             act(ap("ux", t, 512, 4), zb, bias=c("u4", t))
         else:
             ts(ap("ux", t, 512, 4), zb, c("u4", t), A.add)
-    fill(ap("vt", 128, 512), 0.0)
-    fill(ap("nzx", 256, 512), 0.0)
-    fill(ap("zf", 0, 32), 0.0)
-    act(ap("wt", 0, 256), ap("m16", 0, 256), scale=-1000512.0, bias=512.0)
     quant("uq", 0, 128, "ux")
 
     P0, P1, P2, P3 = 0, 512, 1024, 1536
@@ -345,43 +352,48 @@ def rank_program(g, core, T, topo):
     for h, pk in ((0, P1), (1, P2)):
         act(c("ss", h), c("pp", pk))
         act(c("ds01", h), c("pp", pk), F.Abs, bias=2.0 ** -120, scale=0.7 * 2.0 ** -23)
-        act(ap("sm", 128 * h, 128 * h + 128), ap("mask", 0, 128), bias=c("ss", h), scale=c("ds01", h))
     quant("cq", 0, 256, "ct")
-    tt(ap("cmp", 0, 128), low, ap("sm", 0, 128), A.is_lt)
-    ts(ap("cmp", 128, 256), high, s0, A.is_lt)
-    act(ap("junk", 0, 256), ap("cmp", 0, 256), accum=c("pos", 0))
+    ts(ap("sm", 0, 128), ap("mask", 0, 128), c("ds01", 0), A.mult, s0, A.add)
+    act(ap("sm", 128, 256), ap("mask", 0, 128), bias=s1, scale=c("ds01", 1))
+    ts(ap("cmp", 0, 128), high, s0, A.is_lt)
     ts(ap("cmp", 256, 384), low, s1, A.is_le)
+    tt(ap("cmp", 128, 256), low, ap("sm", 0, 128), A.is_lt)
     tt(ap("cmp", 384, 512), high, ap("sm", 128, 256), A.is_lt)
+    act(ap("junk", 256, 384), ap("cmp", 256, 384), accum=c("pos", 1))
+    act(ap("junk", 0, 256), ap("cmp", 0, 256), accum=c("pos", 0))
     act(ap("junk", 256, 512), ap("dv", 0, 256), F.Sign, bias=-2.0 ** -100, accum=c("ft"))
-    act(c("f64"), c("ft"), scale=32.0, bias=8192.0)
-    red(c("pos", 1), ap("cmp", 256, 512))
-    for t in (0, 2, 1, 3):
-        ts(ap("oh", t, 512, 4), ap("io64", 0, 128), c("pos", t % 2), A.is_equal)
+    ts(ap("m16", 0, 256), ap("md16", 0, 256), lo, A.is_equal)
+    act(ap("wt", 0, 256), ap("m16", 0, 256), scale=-1000512.0, bias=512.0)
+    red(c("pos", 4), ap("cmp", 384, 512))
+    for t in (1, 3):
+        ts(ap("oh", t, 512, 4), ap("io64", 0, 128), c("pos", 1), A.subtract, c("pos", 4), A.is_equal)
+    for t in (0, 2):
+        ts(ap("oh", t, 512, 4), ap("io64", 0, 128), c("pos", 0), A.is_equal)
+    v = c("vl", 8 * slot)
+    ts(v, c("ft"), 256.0, A.add)
+    to_all(v, v, "a_v")
     quant("oq", 0, 128, "oh")
-    mm(ap("pp", P0, P0 + 128), "cq", 0, "oq", 0, 128)
     mm(ap("dv", 512, 640), "oq", 0, "cq", 128, 256)
-    iota("tsum", 64, [[1, 8], [1, 8]])
-    iota("ri", 64, [[0, 8], [1, 8]])
-    iota("c2", 4, [[2, 4]])
+    mm(ap("pp", P0, P0 + 128), "cq", 0, "oq", 0, 128)
     ts(ap("bi", 0, 4), ai, 3, A.logical_shift_right)
     cp(ap("lq7", 0, 4), yi)
     ts(ap("gis", 0, 4), yi, -8.0, A.mult, 63.0, A.add)
     ts(ap("in32", 0, 4), yi, 32.0, A.mult, 31.0, A.add)
     act(ap("r8", 0, 64), ap("ri", 0, 64), F.Sign)
+    act(ap("eb", 3, 515, 4), ap("idn", 0, 128))
     wrap("js", ap("pp", P0, P0 + 64), 64)
-    for k, p in ((0, (0, 64)), (1, (64, 128))):
-        ts(ap("vl", 8 * slot, 8 * slot + 1, p=p), c("dv", 512 + k, p), c("f64", 0, p), A.add)
-    listed("jl4", "js", 32)
     xx = ap("xx", 0, 4)
     tt(xx, ap("bi", 0, 4), ap("c2", 0, 4), A.add)
+    listed("jl4", "js", 32)
     pick("sp", 0, 32, "tq", 0, 256, "jl4", 0, 2)
     listed("jl4", "js", 64, a=32)
 
-    v = c("vl", 8 * slot)
-    to_all(v, v, "a_v")
     to_all(ap("sp", 0, 32, bc=u8), ap("land", 32 * slot, 32 * slot + 32, bc=u8), "a_c")
     to_all(ap("sps", 0, 32), ap("lands", 32 * slot, 32 * slot + 32), "a_s")
-    to_helper(ap("tqs", 0, 256), ap("hqs", 0, 256), "h_s")
+    cp(ap("lt4", 0, 2), ap("dv", 512, 514))
+    quant("tq", 256, 384, "lt4")
+    to_helper(ap("tq", 256, 258, bc=u8), ap("hq", 256, 258, bc=u8), "h_l")
+    to_helper(ap("tqs", 0, 258), ap("hqs", 0, 258), "h_s")
     move("land", 32 * slot, "sp", 0, 32)
     move("cd", 0, "tq", 0, 128)
 
@@ -390,16 +402,16 @@ def rank_program(g, core, T, topo):
     pick("sp", 32, 64, "tq", 0, 256, "jl4", 2, 4)
     move("xw", 128, "sp", 0, 64)
     move("sl", 32 * slot, "tq", 32 * me, 32)
-    ts(ap("tie", 0, 64), ap("tie5", 0, 64), 0.5, A.add, 64.0, A.mult)
+    move("ll", 2 * slot, "tq", 256, 2)
+    move("ll", 16, "tq", 0, 112)
+    ts(ap("tie", 0, 64), ap("tie5", 0, 64), 0.5, A.add, 2.0, A.mult)
     for b in range(4):
         quant("eh", 128 * b, 128 * b + 128, "eb", 3 - b)
     quant("nq", 0, 128, "nzx")
     for b in range(4):
         mm(ap("dv", 512 * b, 512 * b + 128), "eh", 128 * b, "nq", 0, 128, True, False)
-    ts(c("colf"), hi, 3.5, A.is_lt, 15.0, A.mult)
     fill(ap("wc", 0, 8), 32.0)
     ts(ap("grs", 0, 4), xx, -8.0, A.mult, 63.0, A.add)
-    ts(c("colf", 1), c("colf"), 1.0, A.add)
     iota("l2i", 16, [[1, 8], [0, 2]])
     iota("md32", 256, [[0, 8], [1, 32]])
     iota("x32", 8, [[32, 8]], 256)
@@ -417,14 +429,9 @@ def rank_program(g, core, T, topo):
     ts(ap("ou32", 0, 4), xx, -32.0, A.mult, 255.0, A.add)
     lq7, lrs, r8 = ap("lq7", 0, 4), ap("lrs", 0, 4), ap("r8", 0, 64)
     tt(ap("k1", 0, 64), ap("vi", 0, 8, off=lrs), ap("tie", 0, 64), A.add)
-    ts(ap("nbi", 0, 8), ap("vi", 0, 8), 15, A.bitwise_and)
     tt(ap("cm", 0, 64), ap("vi", 0, 8, off=lq7), ap("k1", 0, 64), A.is_gt)
-    ts(ap("nb", 0, 8), ap("nbi", 0, 8), c("colf", 1), A.mult)
     scan(ap("sc", 0, 64), r8, ap("cm", 0, 64))
-    i = ap("nb", 0, 8, p=(64, 128))
-    o = ap("nl", 0, 8, p=(0, 64))
-    dma("y", o["v"], i["v"], [o], [i])
-    ts(ap("fiti", 0, 8), ap("vi", 0, 8), 6, A.logical_shift_right)
+    ts(ap("fiti", 0, 8), ap("vi", 0, 8), 0.5, A.mult)
     mine = c("sc", 8 * me + 7)
     ts(ap("ms", 0, 8), ap("sc", 7, 64, 8), mine, A.add, 7.0, A.not_equal)
     ts(c("go"), mine, 3.5, A.is_lt, 160.0, A.mult)
@@ -460,12 +467,6 @@ def rank_program(g, core, T, topo):
     to_all(ap("xss", 0, 32), ap("cws", 32 * slot, 32 * slot + 32), "b_s")
     move("cw", 32 * slot, "xs", 0, 32)
 
-    nj = ap("nj", 0, 8, p=(0, 64))
-    tt(nj, ap("nb", 0, 8, p=(0, 64)), ap("nl", 0, 8, p=(0, 64)), A.add)
-    o = ap("jt", 0, 512, p=(0, 1))
-    dma("y", o["v"], nj["v"], [o], [nj])
-    jr = ap("jr", 0, 512)
-    run("g", lambda q: q.partition_broadcast(jr["v"], o["v"], 128), [jr], [o])
     move("cw", 256, "land", 0, 256)
     move("cc", 64, "tq", 0, 64)
     move("np", 64, "nq", 64, 64)
@@ -490,6 +491,18 @@ def rank_program(g, core, T, topo):
     tt(ap("nd", 0, 64), ap("base1", 0, 8, off=lq7), ap("dd", 0, 64), A.subtract)
     mm(ap("pp", P1, P1 + 256), "uq", 0, "land", 0, 256)
     act(ap("sw", 256, 512), ap("pp", P1, P1 + 256))
+    for k in ((0, 2 * slot), (2 * slot + 2, 16)):
+        arrive("ll", k[0], k[1], ("l_c", n8))
+        arrive("lls", k[0], k[1], ("l_s", n8))
+    mm(ap("pp", P2, P2 + 128), "eh", 0, "ll", 0, 128)
+    mm(ap("pp", P3, P3 + 128), "eh", 128, "ll", 0, 128)
+    ts(ap("nh", 0, 8), ap("pp", P2, P2 + 16, 2), 32.0, A.mult)
+    ts(ap("nl", 0, 8), ap("pp", P3, P3 + 16, 2), 2.0, A.mult)
+    tt(ap("nj", 0, 8), ap("nh", 0, 8), ap("nl", 0, 8), A.add)
+    o, i = ap("jt", 0, 512, p=(0, 1)), ap("nj", 0, 8, p=(0, 64))
+    dma("y", o["v"], i["v"], [o], [i])
+    jr = ap("jr", 0, 512)
+    run("g", lambda q: q.partition_broadcast(jr["v"], o["v"], 128), [jr], [o])
     ts(c("ei"), c("pi"), 31, A.bitwise_and)
     tt(ap("w0", 1, 8), ap("o0", 0, 7), ap("o0", 1, 8), A.subtract)
     fill(ap("ones", 0, 64), 1.0)
@@ -500,24 +513,29 @@ def rank_program(g, core, T, topo):
     quant("wq", 0, 128, "wx")
     fill(ap("vt2", 256, 512), 0.0)
 
-    def order_out(sc, t):
-        ts(ap("ode", 0, 8), ap(sc, 7, 64, 8), c("pf"), A.not_equal)
+    def order_out(t):
         scan(ap("odc", 0, 8), ap("ones", 0, 8), ap("ode", 0, 8), A.add, A.mult)
         act(c("odr", t), c("odc", 7), scale=-1.0, bias=7.0)
         x = ap("odr", t, t + 1, p=(0, 8))
         dma("y", T.od[t:t + 1, 0:8], x["v"], [], [x])
-    order_out("sc", 0)
+    ts(ap("ode", 0, 8), ap("sc", 7, 64, 8), c("pf"), A.not_equal)
+    order_out(0)
 
     for k in ((0, 32 * slot), (32 * slot + 32, 256)):
         arrive("cw", k[0], k[1], ("b_c", n8))
         arrive("cws", k[0], k[1], ("b_s", n8))
         arrive("sl", k[0], k[1], ("s_c", 7))
         arrive("sls", k[0], k[1], ("s_s", 7))
-    mm(ap("pp", P0, P0 + 256), "uq", 0, "cw", 0, 256)
-    tt(ap("c1", 0, 256), ap("pp", P0, P0 + 256), ap("thr", 0, 256), A.is_gt)
+    mm(ap("pp", P0, P0 + 128), "uq", 0, "cw", 0, 128)
+    mm(ap("pp", P3, P3 + 128), "uq", 0, "cw", 128, 256)
+    for k, pk in ((0, P0), (128, P3)):
+        tt(ap("c1", k, k + 128), ap("pp", pk, pk + 128), ap("thr", k, k + 128), A.is_gt)
     scan(ap("s1", 0, 256), ap("r32", 0, 256), ap("c1", 0, 256))
+    act(ap("x1b", 0, 64), ap("s1", 0, 256, off=ap("ou32", 0, 4)))
     tt(ap("k1b", 0, 64), ap("s1", 0, 256, off=ap("in32", 0, 4)), ap("nd", 0, 64), A.add)
-    tt(ap("cmb", 0, 64), ap("s1", 0, 256, off=ap("ou32", 0, 4)), ap("k1b", 0, 64), A.is_lt)
+    for k, pk in ((0, P0), (128, P3)):
+        act(ap("sw", k, k + 128), ap("pp", pk, pk + 128))
+    tt(ap("cmb", 0, 64), ap("x1b", 0, 64), ap("k1b", 0, 64), A.is_lt)
     scan(ap("scb", 0, 64), r8, ap("cmb", 0, 64))
     act(ap("q1", 0, 64), ap("scb", 0, 64, off=ap("gr", 0, 4)), F.Abs, bias=-3.5)
     ts(ap("g1", 0, 64), ap("scb", 0, 64, off=gi), -1.0, A.mult, 3.5, A.add)
@@ -543,7 +561,6 @@ def rank_program(g, core, T, topo):
     n3 = 4 * len(out) // 4 + 2 * len(out) // 2 + len(inn)
     move("fw", 32 * me, "sb", 32 * me, 32)
 
-    act(ap("sw", 0, 256), ap("pp", P0, P0 + 256))
     tt(c("o1"), c("bs", 8 * me + 7), c("cola", 2), A.add)
     ts(ap("ofc", 0, 2), ap("wr", 0, 2), c("st0", 7), A.add, c("o0", 7), A.add)
     ts(ap("ofj", 0, 4), ap("w256", 0, 4), c("o1"), A.add, 1.0 / 32, A.mult)
@@ -561,17 +578,19 @@ def rank_program(g, core, T, topo):
         mm(ap("dv", 512 * b, 512 * b + 128), "eh", 128 * b, "cc", 0, 128, True, False)
     two = [(e, (64 * e, 64 * e + 64)) for e in (0, 1)]
     for e, w in two:
+        act(ap("jl", *w), cj, F.Sign, bias=c("ds", 64 + 32 * e + 31), scale=-1.0)
         ts(ap("eq", *w), cs, c("ds", 32 * e + 31), A.is_equal)
-        ts(ap("jl", *w), cj, c("ds", 64 + 32 * e + 31), A.is_lt)
     for e, w in two:
-        ts(ap("lt", *w), cs, c("ds", 32 * e + 31), A.is_lt)
+        act(ap("lt", *w), cs, F.Sign, bias=c("ds", 32 * e + 31), scale=-1.0)
         tt(ap("eqj", *w), ap("eq", *w), ap("jl", *w), A.mult)
     listed("jw", "jws", 64)
     for e, w in two:
         scan(ap("cnt", *w), ap("lt", *w), ap("eqj", *w), A.add, A.add)
     for e, w in two:
-        ts(ap("tp", 32 * e, 32 * e + 32), ap("zf", 0, 32), c("cnt", 64 * e + 63), A.add)
+        ts(ap("tp", 32 * e, 32 * e + 32), ap("zf", 0, 32), c("cnt", 64 * e + 63), A.mult, 31.5, A.add)
+    ts(ap("ode", 0, 8), ap("scb", 7, 64, 8), c("pf"), A.not_equal)
     run("v", lambda q: q.transpose(cr["v"], tp["v"]), [cr], [tp])
+    order_out(1)
     wrap("crw", cr, 64)
     ts(ap("sel", 0, 64), cr, c("t32"), A.is_lt, 64.0, A.mult)
     listed("pl", "crw", 64, "corr32")
@@ -580,9 +599,8 @@ def rank_program(g, core, T, topo):
     for b in range(4):
         mm(ap("dv", 512 * b, 512 * b + 128), "eh", 128 * b, "np", 0, 128, False, True)
     cp(ap("frow", 0, 256, off=ap("jw", 0, 4)), ap("off", 0, 64))
-    packed("vt2", 64, "fw", 320)
     wrap("fs", ap("frow", 0, 256), 256)
-    order_out("scb", 1)
+    packed("vt2", 64, "fw", 320)
     listed("fl", "fs", 256)
 
     for k in ((0, 32 * me), (32 * me + 32, 256)):

from concourse.bass import DstId, RemoteDMATransfer
from concourse.mybir import dt, AluOpType, AxisListType, ActivationFunctionType

A = AluOpType
F = ActivationFunctionType
CODE, PLANE, F32, BF, I32, U16 = "float8_e4m3fn_x4", "uint8", "float32", "bfloat16", "int32", "uint16"
SCRATCH, PART = {}, {}


def _bufs():
    def b(dtype, **kw):
        for k in kw:
            SCRATCH[k] = ("sbuf", [128, kw[k]], dtype)

    def parts(name, dtype, **kw):
        n = 0
        for k in kw:
            PART[k] = (name, n)
            n += kw[k]
        SCRATCH[name] = ("sbuf", [128, n], dtype)

    def q(**kw):
        for k in kw:
            SCRATCH[k] = ("sbuf", [128, kw[k]], CODE)
            SCRATCH[k + "s"] = ("sbuf", [128, kw[k]], PLANE)
    b(BF, tbx=1024, nzx=512, wx=512, ux=512, u4=8, eb=528, ct=1024, oh=512, vt=512, vt2=512, zb=128, hb=128, idn=128,
      lt4=512, cmp=512, c1=256, s1=256)
    parts("bconst", BF, m16=256, md16=256, r8=64, r32=256, md32=256, io=128, io64=128, mask=128, i32r=128)
    parts("fconst", F32, hif=8, hi8=8, h16=8, h16b=8, wr=8, pf=8, c16r=8, c2=8, corr=8, corr32=8, wt=256)
    parts("fown", F32, ft=8, sm=256, pos=8, ss=8, ds01=8, js=64, junk=512)
    parts("flist", F32, xx=8, w256=8, tsum=64, tie5=64, tie=64, ri=64, ef=8, wc=8, x32=8,
          ones=64, p256=64, tmp2=8, o0a=8, dd=64, nd=64, nl=8, nh=8, nj=8,
          k1=64, cm=64, sc=64, ms=8, st=8, go=8, q0=64, g0=64, hit=64, hf=64, hfs=64, hh=64, hhs=64, tks=8, thr8=8,
          thr=256, tmp=8, base1=8, wh8=8, w0=8, wh=64, cola=8, o0=8, sw=512, jr=512, ode=8, odc=8, odr=8,
          k1b=64, x1b=64, cmb=64, scb=64, q1=64, g1=64, miss=64, bs=64, o1=8, st0=8, t32=8, csj=128, dgo=128,
          ds=128, lt=128, eq=128, jl=128, eqj=128, cnt=128, tp=64, cr=64, crw=64, sel=64, zf=32,
          off=64, jws=64, frow=256, fs=256)
    b(F32, vi=8, fiti=8, jt=512, yo=256)
    parts("iconst", I32, pi=8, hx=8, ai=8, yi=8, ei=8, bi=8, l2i=16)
    b(U16, vl=64)
    parts("lists", U16, jl4=4, in32=4, ou32=4, lrs=4, lq7=4, grs=4, gr=4, gis=4, l256=16, ofa=2, ofx=2, of=16, ofc=4,
          ofj=4, pl=4, jw=4, fl=16)
    q(uq=128, tq=384, nq=128, wq=128, eh=512, cq=256, oq=128, sp=64, land=256, cd=128, xw=192, xs=32, cw=512,
      sl=256, sb=256, cc=128, np=128, fw=448, oq2=256, hq=264, ll=128)
    SCRATCH["dv"] = ("psum", [128, 2048], F32)
    SCRATCH["pp"] = ("psum", [128, 2048], F32)


_bufs()
SEMAPHORES = ["cv", "cs", "ct_", "cg", "lo", "a_v", "a_c", "a_s", "b_c", "b_s", "c_c", "c_s", "s_c", "s_s", "h_c",
              "h_s", "h_l", "l_c", "l_s"] + ["d%d" % i for i in range(48)]


def find_helpers(T, topo):
    out = []
    for c in T.cores:
        for k in topo.cores_of(c):
            if k in T.cores or k in out or topo.die(k) == topo.die(c):
                continue
            if all(topo.may_write(k, x) for x in T.cores):
                out.append(k)
                break
    return out


def bits(engines):
    return sum(1 << e for e in engines)


def ways(core, T, topo, me):
    far = [r for r in range(len(T.cores)) if r != me and topo.chip(T.cores[r]) != topo.chip(core)]
    near = [r for r in range(len(T.cores)) if r != me and topo.chip(T.cores[r]) == topo.chip(core)]
    out = topo.engines(core, T.cores[far[0]])
    inn = [e for e in topo.engines(core, T.cores[near[0]]) if e not in out][:2]
    return far, near, out, inn


def dest(T, topo, r):
    rid, pid, _ = topo.addr(T.cores[r])
    return DstId(rid=rid, pnc=pid)


def one_each(g, T, topo, to, src, dst, sem):
    g.remote_dma_fused([RemoteDMATransfer(dst_ids=[dest(T, topo, r)], dma_engine_mask=bits(e), remote_sem=sem,
                                          src=src(r), dst=dst) for r, e in to], local_sem=T.sem.lo)
    return sum(len(e) for _, e in to)


def same_to_all(g, T, topo, to, src, dst, sem):
    g.remote_dma_fused([RemoteDMATransfer(dst_ids=[dest(T, topo, r) for r in rs], dma_engine_mask=bits(e),
                                          remote_sem=sem, srcs=[src], dsts=[dst] * len(rs)) for rs, e in to],
                       local_sem=T.sem.lo)
    return sum(len(e) for _, e in to)


def hand_on(g, core, T, topo, r):
    S = 32
    c0, l0 = S * (len(T.cores) - 1 - r), 2 * (len(T.cores) - 1 - r)
    far, near, out, inn = ways(core, T, topo, r)
    to = [(s, out[i:i + 1]) for i, s in enumerate(far)] + [(s, inn[:1]) for s in near]
    lists = [(far, out), (near, inn)]
    g.wait_ge(T.sem.h_c, len(out))
    n = one_each(g, T, topo, to, lambda s: T.hq[:, S * s:S * s + S].bitcast(dt.uint8),
                 T.sl[:, c0:c0 + S].bitcast(dt.uint8), T.sem.s_c)
    g.wait_ge(T.sem.h_l, len(out))
    n += same_to_all(g, T, topo, lists, T.hq[:, 256:258].bitcast(dt.uint8), T.ll[:, l0:l0 + 2].bitcast(dt.uint8),
                     T.sem.l_c)
    g.wait_ge(T.sem.h_s, len(out))
    n += same_to_all(g, T, topo, lists, T.hqs[:, 256:258], T.lls[:, l0:l0 + 2], T.sem.l_s)
    n += one_each(g, T, topo, to, lambda s: T.hqs[:, S * s:S * s + S], T.sls[:, c0:c0 + S], T.sem.s_s)
    g.wait_ge(T.sem.lo, n)


def builder(g, T):
    queue = {"v": g.vector, "s": g.scalar, "t": g.tensor, "g": g, "y": g.sync}
    sem = {"v": "cv", "s": "cs", "t": "ct_", "g": "cg"}
    count = {"v": 0, "s": 0, "t": 0, "g": 0}
    seen, log, dmas = {}, {}, [0]

    def ap(n, a, b, st=1, p=None, bc=None, off=None):
        n, k = PART.get(n, (n, 0))
        a, b, t = a + k, b + k, T[n]
        rows = slice(None) if p is None else slice(p[0], p[1])
        v = t[rows, a:b] if st == 1 else t[rows, a:b:st]
        if bc is not None:
            v = v.bitcast(bc)
        if off is not None:
            v = v.indirect(off["v"])
        return {"v": v, "n": n, "a": a, "b": b, "st": st, "off": off}

    def apart(x, y):
        if x["n"] in ("dv", "pp"):
            return x["a"] // 512 != y["a"] // 512
        if x["a"] >= y["b"] or y["a"] >= x["b"]:
            return True
        return x["st"] == y["st"] and x["st"] > 1 and (x["a"] - y["a"]) % x["st"] != 0

    def wait(q, tok):
        if seen.get((q, tok[0]), 0) < tok[1]:
            queue[q].wait_ge(T.sem[tok[0]], tok[1])
            seen[(q, tok[0])] = tok[1]

    def need(q, outs, ins):
        toks = {}
        for w, xs in ((True, outs), (False, ins)):
            for x in xs:
                for (y, yw, yq, tok) in log.get(x["n"], []):
                    if apart(x, y):
                        continue
                    psum = x["n"] in ("dv", "pp")
                    if yw or (w and yq != q) or (psum and yq != q):
                        if yq == q == "t" and yw and w:
                            continue
                        toks[tok[0]] = max(toks.get(tok[0], 0), tok[1])
        for k in toks:
            wait(q, (k, toks[k]))

    def note(q, outs, ins, tok):
        for w, xs in ((True, outs), (False, ins)):
            for x in xs:
                log.setdefault(x["n"], []).append((x, w, q, tok))

    def full(xs):
        return [x for x in xs if x] + [x["off"] for x in xs if x and x["off"]]

    def run(q, fn, outs, ins):
        ins = full(ins) + [x["off"] for x in outs if x["off"]]
        need(q, outs, ins)
        count[q] += 1
        fn(queue[q]).then_inc(T.sem[sem[q]], 1)
        note(q, outs, ins, (sem[q], count[q]))

    def dma(q, out, in_, outs, ins):
        need(q, outs, ins)
        s = "d%d" % dmas[0]
        dmas[0] += 1
        queue[q].dma_start(out, in_).then_inc(T.sem[s], 16)
        note("dma", outs, ins, (s, 16))

    def arrive(n, a, b, tok):
        x = {"n": n, "a": a, "b": b, "st": 1, "off": None}
        log.setdefault(n, []).append((x, True, "far", tok))

    def ready(q, ins):
        need(q, [], full(ins))

    def finish():
        for q in count:
            wait("y", (sem[q], count[q]))
        for k in range(dmas[0]):
            wait("y", ("d%d" % k, 16))
    return ap, run, dma, arrive, ready, finish


def rank_program(g, core, T, topo):
    me = T.rank_of(core)
    helpers = find_helpers(T, topo)
    if me is None:
        if core in helpers:
            hand_on(g, core, T, topo, helpers.index(core))
        return
    ap, run, dma, arrive, ready, finish = builder(g, T)
    u8, u32 = dt.uint8, dt.uint32
    slot = 7 - me
    far, near, out, inn = ways(core, T, topo, me)
    sent = [0]

    def sca(x):
        return x["v"] if isinstance(x, dict) else x

    def dic(*xs):
        return [x for x in xs if isinstance(x, dict)]

    def ts(out, in0, s1, op0, s2=None, op1=None):
        if op1 is None:
            run("v", lambda q: q.tensor_scalar(out["v"], in0["v"], sca(s1), None, op0), [out], dic(in0, s1))
        else:
            run("v", lambda q: q.tensor_scalar(out["v"], in0["v"], sca(s1), sca(s2), op0, op1), [out],
                dic(in0, s1, s2))

    def tt(out, in0, in1, op):
        run("v", lambda q: q.tensor_tensor(out["v"], in0["v"], in1["v"], op), [out], [in0, in1])

    def scan(out, d0, d1, op0=A.mult, op1=A.add):
        run("v", lambda q: q.tensor_tensor_scan(out["v"], d0["v"], d1["v"], 0.0, op0, op1), [out], [d0, d1])

    def cp(out, in_):
        run("v", lambda q: q.tensor_copy(out["v"], in_["v"]), [out], [in_])

    def fill(out, c):
        run("v", lambda q: q.memset(out["v"], c), [out], [])

    def red(out, in_):
        run("v", lambda q: q.tensor_reduce(out["v"], in_["v"], AxisListType.X, A.add), [out], [in_])

    def act(out, in_, func=None, bias=0.0, scale=1.0, accum=None):
        plain = not dic(bias, scale) and bias == 0.0 and scale == 1.0
        func = func or (F.Copy if plain else F.Identity)
        kw = {} if plain else {"bias": sca(bias), "scale": sca(scale)}
        if accum:
            kw["accum_out"] = accum["v"]
        run("s", lambda q: q.activation(out["v"], in_["v"], func, **kw), [out] + dic(accum), [in_] + dic(bias, scale))

    def quant(n, a, b, tile, x0=0):
        o, p, x = ap(n, a, b), ap(n + "s", a, b), ap(tile, x0, x0 + 4 * (b - a))
        run("v", lambda q: q.quantize_mx(o["v"], p["v"], x["v"]), [o, p], [x])

    def mm(out, l, la, r, ra, rb, start=True, stop=True):
        xs = [ap(l, la, la + 128), ap(l + "s", la, la + 128), ap(r, ra, rb), ap(r + "s", ra, rb)]
        run("t", lambda q: q.matmul_mx(out["v"], xs[0]["v"], xs[1]["v"], xs[2]["v"], xs[3]["v"], start, stop),
            [out], xs)

    def pick(dn, c, d, sn, a, b, on, e, f):
        off = ap(on, e, f)
        cp(ap(dn, c, d, bc=u32), ap(sn, a, b, bc=u32, off=off))
        act(ap(dn + "s", c, d), ap(sn + "s", a, b, off=off))

    def move(dn, c, sn, a, n):
        o, i = ap(dn, c, c + n, bc=u8), ap(sn, a, a + n, bc=u8)
        dma("y", o["v"], i["v"], [o], [i])
        o, i = ap(dn + "s", c, c + n), ap(sn + "s", a, a + n)
        dma("y", o["v"], i["v"], [o], [i])

    def load(q, n, a, b, src):
        o = ap(n, a, b)
        dma(q, o["v"], src, [o], [])

    def to_all(src, dst, sem):
        ready("g", [src])
        sent[0] += same_to_all(g, T, topo, [(far, out), (near, inn)], src["v"], dst["v"], T.sem[sem])

    def c(n, k=0):
        return ap(n, k, k + 1)

    def iota(n, k, pat, base=0, cm=0):
        o, small = ap(n, 0, k), SCRATCH[PART[n][0]][2] != I32
        kw = {"allow_small_or_imprecise_dtypes": True} if small else {}
        run("g", lambda q: q.iota(o["v"], pat, base, cm, **kw), [o], [])

    def wrap(s, row, w):
        scan(ap(s, 0, w), ap("wt", 0, w), row, A.add, A.max)

    def listed(lst, s, w, corr="corr", a=0):
        ts(ap(lst, a // 16, w // 16), ap(s, a + 15, w, 16), c(corr), A.add)

    load("s", "u4", 0, 4, T.u[:, 0:4])
    load("y", "tbx", 0, 512, T.tb[:, 0:512])
    load("s", "tbx", 512, 1024, T.tb[:, 512:1024])
    load("y", "nzx", 0, 256, T.nz[:, 0:256])
    load("y", "wx", 0, 512, T.w[:, 0:512])
    iota("pi", 4, [[0, 4]], 0, 1)
    iota("c16r", 4, [[16, 4]])
    iota("io", 128, [[1, 128]])
    iota("io64", 128, [[0, 2], [1, 64]])
    iota("md16", 256, [[0, 16], [1, 16]])
    zb = ap("zb", 0, 128)
    fill(zb, 0.0)
    fill(ap("ct", 512, 1024), 0.0)
    pi, ai, yi = ap("pi", 0, 4), ap("ai", 0, 4), ap("yi", 0, 4)
    ts(ai, pi, 15, A.bitwise_and)
    ts(c("hx"), c("pi"), 4, A.logical_shift_right)
    ts(yi, pi, 7, A.bitwise_and)
    tt(c("h16"), c("pi"), c("ai"), A.subtract)
    cp(c("hif"), c("hx"))
    tt(ap("wr", 0, 4), ai, ap("c16r", 0, 4), A.add)
    cp(c("pf"), c("pi"))
    ts(c("h16b"), c("h16"), 128.0, A.add)
    ts(c("hi8"), c("hif"), 8.0, A.add)
    hi, lo = c("hif"), c("wr")
    for t, col in ((0, c("h16")), (1, c("h16b")), (2, lo), (3, lo)):
        act(ap("ct", t, 512, 4), zb, bias=col)
    act(c("ct", 512), c("zb"), bias=hi)
    act(c("ct", 513), c("zb"), bias=c("hi8"))
    act(ap("ct", 518, 520), ap("zb", 0, 2), bias=lo)
    fill(ap("hb", 0, 128), 0.5)
    o, i = ap("idn", 0, 128), ap("hb", 0, 128)
    run("g", lambda q: q.affine_select(o["v"], i["v"], [[-1, 128]], A.is_equal, 0.0, 0, 1), [o], [i])
    fill(ap("eb", 0, 528), 0.0)
    iota("tsum", 64, [[1, 8], [1, 8]])
    iota("ri", 64, [[0, 8], [1, 8]])
    iota("c2", 4, [[2, 4]])
    ts(ap("mask", 0, 128), ap("io", 0, 128), c("pf"), A.is_lt)
    ts(c("corr"), lo, 512.0, A.mult, -7680.0, A.add)
    fill(ap("vt", 128, 512), 0.0)
    fill(ap("nzx", 256, 512), 0.0)
    fill(ap("zf", 0, 32), 0.5)
    fill(ap("lt4", 0, 512), 0.0)
    for t in (0, 1, 2, 3):
        if t < 2:
            act(ap("ux", t, 512, 4), zb, bias=c("u4", t))
        else:
            ts(ap("ux", t, 512, 4), zb, c("u4", t), A.add)
    quant("uq", 0, 128, "ux")

    P0, P1, P2, P3 = 0, 512, 1024, 1536
    quant("tq", 0, 128, "tbx")
    mm(ap("pp", P1, P1 + 128), "tq", 0, "uq", 0, 128)
    mm(ap("pp", P0, P0 + 128), "uq", 0, "tq", 0, 128)
    quant("tq", 128, 256, "tbx", 512)
    mm(ap("pp", P2, P2 + 128), "tq", 128, "uq", 0, 128)
    mm(ap("pp", P3, P3 + 128), "uq", 0, "tq", 128, 256)
    mm(ap("dv", 0, 256), "uq", 0, "tq", 0, 256)
    rid, pid, _ = topo.addr(helpers[me])

    def to_helper(n, o, sem):
        ready("g", [n])
        g.remote_dma(o["v"], n["v"], T.sem[sem], T.sem.lo, pid, rid, bits(out))
        sent[0] += len(out)
    to_helper(ap("tq", 0, 256, bc=u8), ap("hq", 0, 256, bc=u8), "h_c")
    low, high = ap("pp", P0, P0 + 128), ap("pp", P3, P3 + 128)
    s0, s1 = c("ss", 0), c("ss", 1)
    for h, pk in ((0, P1), (1, P2)):
        act(c("ss", h), c("pp", pk))
        act(c("ds01", h), c("pp", pk), F.Abs, bias=2.0 ** -120, scale=0.7 * 2.0 ** -23)
    quant("cq", 0, 256, "ct")
    ts(ap("sm", 0, 128), ap("mask", 0, 128), c("ds01", 0), A.mult, s0, A.add)
    act(ap("sm", 128, 256), ap("mask", 0, 128), bias=s1, scale=c("ds01", 1))
    ts(ap("cmp", 0, 128), high, s0, A.is_lt)
    ts(ap("cmp", 256, 384), low, s1, A.is_le)
    tt(ap("cmp", 128, 256), low, ap("sm", 0, 128), A.is_lt)
    tt(ap("cmp", 384, 512), high, ap("sm", 128, 256), A.is_lt)
    act(ap("junk", 256, 384), ap("cmp", 256, 384), accum=c("pos", 1))
    act(ap("junk", 0, 256), ap("cmp", 0, 256), accum=c("pos", 0))
    act(ap("junk", 256, 512), ap("dv", 0, 256), F.Sign, bias=-2.0 ** -100, accum=c("ft"))
    ts(ap("m16", 0, 256), ap("md16", 0, 256), lo, A.is_equal)
    act(ap("wt", 0, 256), ap("m16", 0, 256), scale=-1000512.0, bias=512.0)
    red(c("pos", 4), ap("cmp", 384, 512))
    for t in (1, 3):
        ts(ap("oh", t, 512, 4), ap("io64", 0, 128), c("pos", 1), A.subtract, c("pos", 4), A.is_equal)
    for t in (0, 2):
        ts(ap("oh", t, 512, 4), ap("io64", 0, 128), c("pos", 0), A.is_equal)
    v = c("vl", 8 * slot)
    ts(v, c("ft"), 256.0, A.add)
    to_all(v, v, "a_v")
    quant("oq", 0, 128, "oh")
    mm(ap("dv", 512, 640), "oq", 0, "cq", 128, 256)
    mm(ap("pp", P0, P0 + 128), "cq", 0, "oq", 0, 128)
    ts(ap("bi", 0, 4), ai, 3, A.logical_shift_right)
    cp(ap("lq7", 0, 4), yi)
    ts(ap("gis", 0, 4), yi, -8.0, A.mult, 63.0, A.add)
    ts(ap("in32", 0, 4), yi, 32.0, A.mult, 31.0, A.add)
    act(ap("r8", 0, 64), ap("ri", 0, 64), F.Sign)
    act(ap("eb", 3, 515, 4), ap("idn", 0, 128))
    wrap("js", ap("pp", P0, P0 + 64), 64)
    xx = ap("xx", 0, 4)
    tt(xx, ap("bi", 0, 4), ap("c2", 0, 4), A.add)
    listed("jl4", "js", 32)
    pick("sp", 0, 32, "tq", 0, 256, "jl4", 0, 2)
    listed("jl4", "js", 64, a=32)

    to_all(ap("sp", 0, 32, bc=u8), ap("land", 32 * slot, 32 * slot + 32, bc=u8), "a_c")
    to_all(ap("sps", 0, 32), ap("lands", 32 * slot, 32 * slot + 32), "a_s")
    cp(ap("lt4", 0, 2), ap("dv", 512, 514))
    quant("tq", 256, 384, "lt4")
    to_helper(ap("tq", 256, 258, bc=u8), ap("hq", 256, 258, bc=u8), "h_l")
    to_helper(ap("tqs", 0, 258), ap("hqs", 0, 258), "h_s")
    move("land", 32 * slot, "sp", 0, 32)
    move("cd", 0, "tq", 0, 128)

    ts(ap("tie5", 0, 64), ap("tsum", 0, 64), 7.5, A.is_gt, -1.0, A.mult)
    ts(ap("lrs", 0, 4), xx, -1.0, A.mult, 7.0, A.add)
    pick("sp", 32, 64, "tq", 0, 256, "jl4", 2, 4)
    move("xw", 128, "sp", 0, 64)
    move("sl", 32 * slot, "tq", 32 * me, 32)
    move("ll", 2 * slot, "tq", 256, 2)
    move("ll", 16, "tq", 0, 112)
    ts(ap("tie", 0, 64), ap("tie5", 0, 64), 0.5, A.add, 2.0, A.mult)
    for b in range(4):
        quant("eh", 128 * b, 128 * b + 128, "eb", 3 - b)
    quant("nq", 0, 128, "nzx")
    for b in range(4):
        mm(ap("dv", 512 * b, 512 * b + 128), "eh", 128 * b, "nq", 0, 128, True, False)
    fill(ap("wc", 0, 8), 32.0)
    ts(ap("grs", 0, 4), xx, -8.0, A.mult, 63.0, A.add)
    iota("l2i", 16, [[1, 8], [0, 2]])
    iota("md32", 256, [[0, 8], [1, 32]])
    iota("x32", 8, [[32, 8]], 256)
    iota("p256", 64, [[1, 64]], 256)
    iota("frow", 256, [[1, 256]])
    act(ap("r32", 0, 256), ap("md32", 0, 256), F.Sign)

    n8 = len(far) * len(out) + len(near) * len(inn)
    arrive("vl", 0, 8 * slot, ("a_v", n8))
    arrive("vl", 8 * slot + 8, 64, ("a_v", n8))
    for k in ((0, 32 * slot), (32 * slot + 32, 256)):
        arrive("land", k[0], k[1], ("a_c", n8))
        arrive("lands", k[0], k[1], ("a_s", n8))
    cp(ap("vi", 0, 8), ap("vl", 0, 64, 8))
    ts(ap("ou32", 0, 4), xx, -32.0, A.mult, 255.0, A.add)
    lq7, lrs, r8 = ap("lq7", 0, 4), ap("lrs", 0, 4), ap("r8", 0, 64)
    tt(ap("k1", 0, 64), ap("vi", 0, 8, off=lrs), ap("tie", 0, 64), A.add)
    tt(ap("cm", 0, 64), ap("vi", 0, 8, off=lq7), ap("k1", 0, 64), A.is_gt)
    scan(ap("sc", 0, 64), r8, ap("cm", 0, 64))
    ts(ap("fiti", 0, 8), ap("vi", 0, 8), 0.5, A.mult)
    mine = c("sc", 8 * me + 7)
    ts(ap("ms", 0, 8), ap("sc", 7, 64, 8), mine, A.add, 7.0, A.not_equal)
    ts(c("go"), mine, 3.5, A.is_lt, 160.0, A.mult)
    scan(ap("st", 0, 8), ap("wc", 0, 8), ap("ms", 0, 8), A.add, A.mult)
    ts(ap("ofx", 0, 2), ap("wr", 0, 2), c("go"), A.add)
    ts(ap("ofa", 0, 2), ap("wr", 0, 2), c("st", 7), A.add)
    gi, grs = ap("gis", 0, 4), ap("grs", 0, 4)
    act(ap("q0", 0, 64), ap("sc", 0, 64, off=grs), F.Abs, bias=-3.5)
    pick("cd", 0, 32, "land", 0, 256, "ofa", 0, 2)
    for b in range(4):
        mm(ap("dv", 512 * b, 512 * b + 128), "eh", 128 * b, "cd", 0, 128, False, True)

    def packed(vt, w, out, a):
        for b in (0, 1, 2, 3):
            o, i = ap(vt, b, 4 * w, 4), ap("dv", 512 * b, 512 * b + w)
            if b % 2:
                cp(o, i)
            else:
                act(o, i)
        quant(out, a, a + 128, vt)
    ts(ap("g0", 0, 64), ap("sc", 0, 64, off=gi), -1.0, A.mult, 3.5, A.add)
    ts(ap("tie5", 0, 64), ap("tie5", 0, 64), 0.5, A.add)
    ts(ap("gr", 0, 4), xx, 8.0, A.mult, 7.0, A.add)
    tt(ap("hit", 0, 64), ap("g0", 0, 64), ap("q0", 0, 64), A.is_equal)
    ts(ap("tks", 0, 8), ap("g0", 0, 8), 0.0, A.is_lt)
    tt(ap("hf", 0, 64), ap("fiti", 0, 8, off=lq7), ap("hit", 0, 64), A.mult)
    tt(ap("hh", 0, 64), ap("hit", 0, 64), ap("ri", 0, 64), A.mult)
    packed("vt", 32, "xw", 0)
    ts(ap("thr8", 0, 8), ap("tks", 0, 8), -1e29, A.mult, 1e29, A.add)
    pick("xs", 0, 32, "xw", 0, 192, "ofx", 0, 2)

    to_all(ap("xs", 0, 32, bc=u8), ap("cw", 32 * slot, 32 * slot + 32, bc=u8), "b_c")
    to_all(ap("xss", 0, 32), ap("cws", 32 * slot, 32 * slot + 32), "b_s")
    move("cw", 32 * slot, "xs", 0, 32)

    move("cw", 256, "land", 0, 256)
    move("cc", 64, "tq", 0, 64)
    move("np", 64, "nq", 64, 64)
    scan(ap("hfs", 0, 64), r8, ap("hf", 0, 64))
    scan(ap("hhs", 0, 64), r8, ap("hh", 0, 64))
    cp(ap("l256", 0, 16), ap("l2i", 0, 16))
    act(ap("thr", 0, 256), ap("thr8", 0, 8, off=ap("l256", 0, 16)))
    fh = ap("hfs", 7, 64, 8)
    ts(ap("tmp", 0, 8), fh, -224.0, A.add, 0.0, A.max)
    fill(ap("wh8", 0, 1), 0.0)
    fill(ap("w0", 0, 1), 0.0)
    tt(ap("wh8", 1, 8), ap("hhs", 7, 56, 8), ap("hhs", 15, 64, 8), A.subtract)
    tt(ap("tmp2", 0, 8), ap("tmp", 0, 8), ap("tks", 0, 8), A.mult)
    ts(ap("o0a", 0, 8), ap("tks", 0, 8), -256.0, A.mult)
    ts(ap("wh", 0, 64), ap("wh8", 0, 8, off=lq7), 32.0, A.mult)
    tt(ap("base1", 0, 8), fh, ap("tmp2", 0, 8), A.subtract)
    ts(c("cola", 0), c("hhs", 63), 32.0, A.mult, c("wr", 0), A.add)
    ts(c("cola", 1), c("hhs", 63), 32.0, A.mult, c("wr", 1), A.add)
    tt(ap("dd", 0, 64), ap("base1", 0, 8, off=lrs), ap("tie5", 0, 64), A.add)
    ts(c("cola", 2), c("hhs", 63), 32.0, A.mult)
    tt(ap("o0", 0, 8), ap("o0a", 0, 8), ap("x32", 0, 8), A.add)
    tt(ap("nd", 0, 64), ap("base1", 0, 8, off=lq7), ap("dd", 0, 64), A.subtract)
    mm(ap("pp", P1, P1 + 256), "uq", 0, "land", 0, 256)
    act(ap("sw", 256, 512), ap("pp", P1, P1 + 256))
    for k in ((0, 2 * slot), (2 * slot + 2, 16)):
        arrive("ll", k[0], k[1], ("l_c", n8))
        arrive("lls", k[0], k[1], ("l_s", n8))
    mm(ap("pp", P2, P2 + 128), "eh", 0, "ll", 0, 128)
    mm(ap("pp", P3, P3 + 128), "eh", 128, "ll", 0, 128)
    ts(ap("nh", 0, 8), ap("pp", P2, P2 + 16, 2), 32.0, A.mult)
    ts(ap("nl", 0, 8), ap("pp", P3, P3 + 16, 2), 2.0, A.mult)
    tt(ap("nj", 0, 8), ap("nh", 0, 8), ap("nl", 0, 8), A.add)
    o, i = ap("jt", 0, 512, p=(0, 1)), ap("nj", 0, 8, p=(0, 64))
    dma("y", o["v"], i["v"], [o], [i])
    jr = ap("jr", 0, 512)
    run("g", lambda q: q.partition_broadcast(jr["v"], o["v"], 128), [jr], [o])
    ts(c("ei"), c("pi"), 31, A.bitwise_and)
    tt(ap("w0", 1, 8), ap("o0", 0, 7), ap("o0", 1, 8), A.subtract)
    fill(ap("ones", 0, 64), 1.0)
    cp(c("ef"), c("ei"))
    ts(ap("w256", 0, 4), ap("wr", 0, 4), 256.0, A.mult)
    ts(c("corr32"), c("corr"), 32.0, A.add)
    ts(ap("i32r", 0, 128), ap("md32", 0, 128), c("ef"), A.is_equal)
    quant("wq", 0, 128, "wx")
    fill(ap("vt2", 256, 512), 0.0)

    def order_out(t):
        scan(ap("odc", 0, 8), ap("ones", 0, 8), ap("ode", 0, 8), A.add, A.mult)
        act(c("odr", t), c("odc", 7), scale=-1.0, bias=7.0)
        x = ap("odr", t, t + 1, p=(0, 8))
        dma("y", T.od[t:t + 1, 0:8], x["v"], [], [x])
    ts(ap("ode", 0, 8), ap("sc", 7, 64, 8), c("pf"), A.not_equal)
    order_out(0)

    for k in ((0, 32 * slot), (32 * slot + 32, 256)):
        arrive("cw", k[0], k[1], ("b_c", n8))
        arrive("cws", k[0], k[1], ("b_s", n8))
        arrive("sl", k[0], k[1], ("s_c", 7))
        arrive("sls", k[0], k[1], ("s_s", 7))
    mm(ap("pp", P0, P0 + 128), "uq", 0, "cw", 0, 128)
    mm(ap("pp", P3, P3 + 128), "uq", 0, "cw", 128, 256)
    for k, pk in ((0, P0), (128, P3)):
        tt(ap("c1", k, k + 128), ap("pp", pk, pk + 128), ap("thr", k, k + 128), A.is_gt)
    scan(ap("s1", 0, 256), ap("r32", 0, 256), ap("c1", 0, 256))
    act(ap("x1b", 0, 64), ap("s1", 0, 256, off=ap("ou32", 0, 4)))
    tt(ap("k1b", 0, 64), ap("s1", 0, 256, off=ap("in32", 0, 4)), ap("nd", 0, 64), A.add)
    for k, pk in ((0, P0), (128, P3)):
        act(ap("sw", k, k + 128), ap("pp", pk, pk + 128))
    tt(ap("cmb", 0, 64), ap("x1b", 0, 64), ap("k1b", 0, 64), A.is_lt)
    scan(ap("scb", 0, 64), r8, ap("cmb", 0, 64))
    act(ap("q1", 0, 64), ap("scb", 0, 64, off=ap("gr", 0, 4)), F.Abs, bias=-3.5)
    ts(ap("g1", 0, 64), ap("scb", 0, 64, off=gi), -1.0, A.mult, 3.5, A.add)
    tt(ap("miss", 0, 64), ap("g1", 0, 64), ap("q1", 0, 64), A.not_equal)
    ts(c("t32"), c("scb", 8 * me + 7), 3.5, A.is_gt, 32.0, A.mult)
    scan(ap("bs", 0, 64), ap("wh", 0, 64), ap("miss", 0, 64), A.add, A.mult)
    scan(ap("st0", 0, 8), ap("w0", 0, 8), ap("miss", 8 * me, 8 * me + 8), A.add, A.mult)
    mh = 4 * (me // 4)
    halves = (4 - mh, mh)
    ts(ap("of", 0, 16, 2), ap("bs", 7, 64, 8), c("cola", 0), A.add)
    ts(ap("of", 1, 16, 2), ap("bs", 7, 64, 8), c("cola", 1), A.add)
    for r0 in halves:
        pick("sb", 32 * r0, 32 * r0 + 128, "sl", 0, 256, "of", 2 * r0, 2 * r0 + 8)

    for n, b, sem in (("sb", u8, "c_c"), ("sbs", None, "c_s")):
        for r0 in halves:
            to = [r for r in range(r0, r0 + 4) if r in far]
            w = len(out) // len(to)
            to = [(r, out[w * i:w * i + w]) for i, r in enumerate(to)] + [(r, inn) for r in near if r0 == mh]
            ready("g", [ap(n, 32 * r0, 32 * r0 + 128)])
            sent[0] += one_each(g, T, topo, to, lambda r: ap(n, 32 * r, 32 * r + 32, bc=b)["v"],
                                ap("fw" + n[2:], 32 * me, 32 * me + 32, bc=b)["v"], T.sem[sem])
    n3 = 4 * len(out) // 4 + 2 * len(out) // 2 + len(inn)
    move("fw", 32 * me, "sb", 32 * me, 32)

    tt(c("o1"), c("bs", 8 * me + 7), c("cola", 2), A.add)
    ts(ap("ofc", 0, 2), ap("wr", 0, 2), c("st0", 7), A.add, c("o0", 7), A.add)
    ts(ap("ofj", 0, 4), ap("w256", 0, 4), c("o1"), A.add, 1.0 / 32, A.mult)
    ts(ap("ofc", 2, 4), ap("wr", 0, 2), c("o1"), A.add)
    cs, cj, cr, tp = ap("csj", 0, 64), ap("csj", 64, 128), ap("cr", 0, 64), ap("tp", 0, 64)
    cp(cj, ap("jr", 0, 512, off=ap("ofj", 0, 4)))
    cp(cs, ap("sw", 0, 512, off=ap("ofc", 0, 4)))
    tt(ap("dgo", 64, 128), cj, ap("i32r", 64, 128), A.mult)
    tt(ap("dgo", 0, 64), cs, ap("i32r", 0, 64), A.mult)
    wrap("jws", cj, 64)
    scan(ap("ds", 0, 128), ap("r32", 0, 128), ap("dgo", 0, 128))
    pick("cc", 0, 64, "cw", 0, 512, "ofc", 0, 4)
    move("fw", 256, "cc", 0, 64)
    for b in range(4):
        mm(ap("dv", 512 * b, 512 * b + 128), "eh", 128 * b, "cc", 0, 128, True, False)
    two = [(e, (64 * e, 64 * e + 64)) for e in (0, 1)]
    for e, w in two:
        act(ap("jl", *w), cj, F.Sign, bias=c("ds", 64 + 32 * e + 31), scale=-1.0)
        ts(ap("eq", *w), cs, c("ds", 32 * e + 31), A.is_equal)
    for e, w in two:
        act(ap("lt", *w), cs, F.Sign, bias=c("ds", 32 * e + 31), scale=-1.0)
        tt(ap("eqj", *w), ap("eq", *w), ap("jl", *w), A.mult)
    listed("jw", "jws", 64)
    for e, w in two:
        scan(ap("cnt", *w), ap("lt", *w), ap("eqj", *w), A.add, A.add)
    for e, w in two:
        ts(ap("tp", 32 * e, 32 * e + 32), ap("zf", 0, 32), c("cnt", 64 * e + 63), A.mult, 31.5, A.add)
    ts(ap("ode", 0, 8), ap("scb", 7, 64, 8), c("pf"), A.not_equal)
    run("v", lambda q: q.transpose(cr["v"], tp["v"]), [cr], [tp])
    order_out(1)
    wrap("crw", cr, 64)
    ts(ap("sel", 0, 64), cr, c("t32"), A.is_lt, 64.0, A.mult)
    listed("pl", "crw", 64, "corr32")
    tt(ap("off", 0, 64), ap("sel", 0, 64), ap("p256", 0, 64), A.add)
    pick("np", 0, 64, "nq", 0, 128, "pl", 0, 4)
    for b in range(4):
        mm(ap("dv", 512 * b, 512 * b + 128), "eh", 128 * b, "np", 0, 128, False, True)
    cp(ap("frow", 0, 256, off=ap("jw", 0, 4)), ap("off", 0, 64))
    wrap("fs", ap("frow", 0, 256), 256)
    packed("vt2", 64, "fw", 320)
    listed("fl", "fs", 256)

    for k in ((0, 32 * me), (32 * me + 32, 256)):
        arrive("fw", k[0], k[1], ("c_c", n3))
        arrive("fws", k[0], k[1], ("c_s", n3))
    for k, pk in ((0, P2), (1, P3)):
        pick("oq2", 128 * k, 128 * k + 128, "fw", 0, 448, "fl", 8 * k, 8 * k + 8)
        mm(ap("pp", pk, pk + 128), "wq", 0, "oq2", 128 * k, 128 * k + 128)
    x = ap("oq2", 0, 256, bc=u8)
    dma("y", T.oc[:, 0:1024], x["v"], [], [x])
    for k in range(4):
        x = ap("oq2s", 0, 256, p=(32 * k, 32 * k + 4))
        dma("y", T.osc[4 * k:4 * k + 4, 0:256], x["v"], [], [x])
    act(ap("yo", 0, 128), ap("pp", P2, P2 + 128))
    cp(ap("yo", 128, 256), ap("pp", P3, P3 + 128))
    for k, q in ((0, "s"), (1, "y")):
        x = ap("yo", 128 * k, 128 * k + 128)
        dma(q, T.y[:, 128 * k:128 * k + 128], x["v"], [], [x])
    finish()
    g.wait_ge(T.sem.lo, sent[0])
